import numpy as np
import ml_dtypes


def mxq(x, axis, fmt="e4m3"):
    dtype, down = {"e4m3": (ml_dtypes.float8_e4m3fn, 7), "e5m2": (ml_dtypes.float8_e5m2, 14)}[fmt]
    v = np.moveaxis(np.asarray(x, np.float32).astype(ml_dtypes.bfloat16).astype(np.float64), axis, -1)
    blocks = v.reshape(v.shape[:-1] + (-1, 32))
    amax = np.abs(blocks).max(-1, keepdims=True)
    byte = np.maximum(np.where(amax > 0, np.frexp(amax)[1] - 1 + 127, 0) - down, 1)
    scale = np.exp2(byte - 127.0)
    codes = (blocks / scale).astype(np.float32).astype(dtype).astype(np.float64)
    return np.moveaxis((codes * scale).reshape(v.shape), -1, axis)


WIDE = False


def mx_kscale(k):
    if not WIDE:
        return np.ones(k)
    levels = np.array([24, -24, 12, -12, 0])
    if k % 512:
        return np.exp2(np.random.permutation(np.resize(levels, k // 32))).repeat(32)
    a = np.empty((k // 512, 16))
    for p in range(k // 512):
        a[p, :8] = np.random.permutation(np.resize(levels, 8))
        for g in range(8):
            far = levels[np.abs(levels - a[p, g]) >= 10]
            a[p, g + 8] = far[np.random.randint(len(far))]
    return np.exp2(a.ravel()).repeat(32)


def f64(x):
    return np.asarray(x).astype(np.float64)


def striped(idx):
    return np.tile(idx.reshape(-1, 16).T, (8, 1)).astype(np.uint16)


def unstriped(offs):
    return offs[:16].T.reshape(-1).astype(np.int64)


E2M1 = np.array([0.0, 0.5, 1.0, 1.5, 2.0, 3.0, 4.0, 6.0, -0.0, -0.5, -1.0, -1.5, -2.0, -3.0, -4.0, -6.0])


def pack_weight(w, fmt):
    k, n = w.shape
    w = f64(np.asarray(w, np.float32).astype(ml_dtypes.bfloat16)).reshape(k // 32, 32, n)
    amax = np.abs(w).max(1)
    if fmt == "e4m3":
        byte = np.frexp(amax)[1] - 1 + 127 - 7
    else:
        mant, ex = np.frexp(amax / 6.0)
        byte = np.where(mant > 0.5, ex, ex - 1) + 127
    byte = np.clip(np.where(amax > 0, byte, 1), 1, 254)
    scaled = (w * np.exp2(127.0 - byte)[:, None, :]).reshape(k, n).astype(np.float32)
    by_word = np.ascontiguousarray(scaled.reshape(k // 512, 128, 4, n).transpose(0, 1, 3, 2))
    if fmt == "e4m3":
        words = by_word.astype(ml_dtypes.float8_e4m3fn).view(np.uint8)
    else:
        c = by_word.astype(ml_dtypes.float4_e2m1fn).view(np.uint8) & 0xF
        words = (c[..., 0::2] | (c[..., 1::2] << 4)).reshape(k // 512, 128, 2 * n)
    return np.ascontiguousarray(words), np.ascontiguousarray(byte.astype(np.uint8).reshape(k // 512, 16, n))


def unpack_weight(words, scales, fmt):
    g, _, n = scales.shape
    words = np.ascontiguousarray(words).reshape(g, 128, n, -1)
    if fmt == "e4m3":
        vals = words.view(ml_dtypes.float8_e4m3fn).astype(np.float64)
    else:
        nib = np.empty((g, 128, n, 4), np.uint8)
        nib[..., 0::2] = words & 0xF
        nib[..., 1::2] = words >> 4
        vals = E2M1[nib]
    vals = vals * np.repeat(np.exp2(scales.astype(np.float64) - 127.0), 8, axis=1)[..., None]
    return vals.transpose(0, 1, 3, 2).reshape(g * 512, n)


def pack_table4(v):
    words, scales = pack_weight(v, "e2m1")
    g, t = words.shape[0] // 2, v.shape[1]
    return np.ascontiguousarray(words.reshape(g, 2, 128, t, 2).transpose(0, 2, 3, 1, 4).reshape(g, 128, t, 4)), scales


def unpack_table4(words, scales):
    g, _, t, _ = words.shape
    return unpack_weight(words.reshape(g, 128, t, 2, 2).transpose(0, 3, 1, 2, 4).reshape(2 * g, 128, 2 * t), scales, "e2m1")


def planes(y):
    n, m = y.shape
    v = y.astype(np.float32).astype(ml_dtypes.bfloat16).astype(np.float64).reshape(n // 32, 32, m)
    top = np.abs(v).max(1)
    byte = np.clip(np.where(top > 0, np.frexp(top)[1] - 1 + 127 - 7, 1), 1, 254)
    codes = (v * np.exp2(127.0 - byte)[:, None, :]).reshape(n, m).astype(np.float32).astype(ml_dtypes.float8_e4m3fn).view(np.uint8)
    words = codes.reshape(n // 512, 128, 4, m).transpose(0, 1, 3, 2)
    return np.ascontiguousarray(words), np.ascontiguousarray(byte.astype(np.uint8).reshape(n // 512, 16, m))


def sigm(f):
    return 1.0 / (1.0 + np.exp(-np.maximum(f, -700.0)))


K, N, T, J = 1024, 512, 2048, 1024


def setup_inputs():
    n = np.random.standard_normal
    s = mx_kscale(K)[:, None]
    p_tab = pack_table4(n((K, T)) * s)
    p_wg = pack_weight(n((K, N)) / np.sqrt(K) / s, "e2m1")
    return {
        "tab_words": p_tab[0],
        "tab_scales": p_tab[1],
        "wg_words": p_wg[0],
        "wg_scales": p_wg[1],
        "wh": (n((K, N)) / np.sqrt(K) / s).astype(np.float32),
        "bg": (0.3 * n(N) - 1.0).astype(np.float32),
        "rT": (n((N, T))).astype(np.float32),
        "offs": striped(np.random.permutation(T)[:J]),
    }


def reference(tab_words, tab_scales, wg_words, wg_scales, wh, bg, rT, offs):
    idx = unstriped(offs)
    tab_ = unpack_table4(tab_words, tab_scales)[:, idx]
    wg_ = unpack_weight(wg_words, wg_scales, "e2m1")
    wh_ = mxq(f64(wh), 0, "e4m3")
    ga = wg_.T @ tab_
    gate = sigm(ga + f64(bg)[:, None])
    ha = wh_.T @ tab_
    out_0 = f64(rT)[:, idx] + gate * (np.tanh(ha) - f64(rT)[:, idx])
    return (out_0,) + planes(out_0)

@@ -1,0 +1,204 @@
+from contextlib import ExitStack
+
+import concourse.mybir as mybir
+
+K, N, T, J = 1024, 512, 2048, 1024
+FLOPS = 2 * 2 * K * N * J
+
+F32 = mybir.dt.float32
+BF16 = mybir.dt.bfloat16
+I32 = mybir.dt.int32
+U32 = mybir.dt.uint32
+U16 = mybir.dt.uint16
+U8 = mybir.dt.uint8
+FP8X4 = mybir.dt.float8_e4m3fn_x4
+FP4X4 = mybir.dt.float4_e2m1fn_x4
+ALU = mybir.AluOpType
+ACT = mybir.ActivationFunctionType
+
+P = 128
+PACK = 4
+PASSES = K // (P * PACK)
+HALF = 512
+HALVES = J // HALF
+CHUNKS = ((0, 256), (256, 256), (512, 256), (768, 128), (896, 128))
+
+
+def tile_list_hwayt_tanhP_kernel(
+    tc, tab_words, tab_scales, wg_words, wg_scales, wh, bg, rT, offs, out_0, out_1, out_2
+):
+    nc = tc.nc
+    with ExitStack() as ctx:
+        keep = ctx.enter_context(tc.tile_pool(name="keep", bufs=1))
+        psum = ctx.enter_context(tc.psum_pool(name="psum", bufs=8))
+
+        tsc = keep.tile([P, T], U8, name="tsc", align_bytes=64)
+        nc.vector.memset(tsc[:].bitcast(I32), 0)
+        gsc_raw = keep.tile([P, PASSES * N], U8, name="gsc_raw", align_bytes=64)
+        nc.vector.memset(gsc_raw[:].bitcast(I32), 0)
+        vs1 = keep.tile([P, J], U8, name="vs1", align_bytes=64)
+        nc.vector.memset(vs1[:].bitcast(I32), 0)
+
+        offsets = keep.tile([P, J // 16], U16, name="offsets")
+        nc.sync.dma_start(offsets[:], offs)
+        bias = keep.tile([P, PACK], F32, name="bias")
+        nc.sync.dma_start(bias[:], bg.rearrange("(p t) -> p t", t=PACK))
+        gw_raw = keep.tile([P, PASSES, N // 2], I32, name="gw_raw", align_bytes=64)
+        nc.sync.dma_start(gw_raw[:], wg_words.bitcast(I32).rearrange("a p n -> p a n"))
+        for q in range(4):
+            nc.sync.dma_start(
+                tsc[32 * q : 32 * q + 8, :].bitcast(I32),
+                tab_scales[:, 4 * q : 4 * q + 4, :].bitcast(I32),
+            )
+        tw = keep.tile([P, T], I32, name="tw", align_bytes=64)
+        nc.sync.dma_start(tw[:], tab_words[0].rearrange("p t b -> p (t b)").bitcast(I32))
+        for q in range(4):
+            nc.sync.dma_start(
+                gsc_raw[32 * q : 32 * q + 4, :].bitcast(I32).rearrange("r (a n) -> r a n", a=PASSES),
+                wg_scales[:, 4 * q : 4 * q + 4, :].bitcast(I32).rearrange("a r n -> r a n"),
+            )
+        r_rows = rT.rearrange("(p t) c -> t p c", t=PACK)
+        r_sb = [keep.tile([P, T], F32, name="r%d" % t, align_bytes=64) for t in range(PACK)]
+        wh_raw = [keep.tile([P, PACK, N], F32, name="wh%d" % a, align_bytes=64) for a in range(PASSES)]
+        for a in range(PASSES):
+            nc.sync.dma_start(wh_raw[a][:], wh[512 * a : 512 * (a + 1), :].rearrange("(p j) n -> p j n", j=PACK))
+            nc.sync.dma_start(r_sb[a][:], r_rows[a])
+        for t in range(PASSES, PACK):
+            nc.sync.dma_start(r_sb[t][:], r_rows[t])
+
+        nbias = keep.tile([P, PACK], F32, name="nbias")
+        nc.scalar.mul(nbias[:], bias[:], -1.0)
+        gw = keep.tile([P, PASSES * N * 2], U8, name="gw", align_bytes=64)
+        nc.vector.tensor_copy(
+            gw[:].bitcast(U16).rearrange("p (a t m) -> p a t m", a=PASSES, t=PACK),
+            gw_raw[:].rearrange("p a n -> p (a n)").bitcast(U16).rearrange("p (a m t) -> p a t m", a=PASSES, t=PACK),
+        )
+
+        vs0 = keep.tile([P, J], U8, name="vs0", align_bytes=64)
+        nc.vector.tensor_copy(vs0[:], tsc[:].indirect(offsets[:]))
+        nc.scalar.dma_start(vs1[0:112, :].bitcast(I32), vs0[4:116, :].bitcast(I32))
+        vs = (vs0, vs1)
+
+        gsc = keep.tile([P, PASSES * N], U8, name="gsc", align_bytes=64)
+        vw = []
+        for h in range(HALVES):
+            pair = keep.tile([P, HALF], U32, name="pair%d" % h, align_bytes=64)
+            nc.vector.tensor_copy(pair[:], tw[:].bitcast(U32).indirect(offsets[:, 32 * h : 32 * (h + 1)]))
+            if h == 0:
+                nc.vector.tensor_copy(
+                    gsc[:].rearrange("p (a t m) -> p a t m", a=PASSES, t=PACK),
+                    gsc_raw[:].rearrange("p (a m t) -> p a t m", a=PASSES, t=PACK),
+                )
+            parted = keep.tile([P, PASSES * HALF * 2], U8, name="parted%d" % h, align_bytes=64)
+            nc.vector.tensor_copy(
+                parted[:].bitcast(U16).rearrange("p (d j) -> p d j", d=PASSES),
+                pair[:].bitcast(U16).rearrange("p (j d) -> p d j", d=PASSES),
+            )
+            vw.append(parted)
+
+        carry = [keep.tile([P, PACK, HALF], F32, name="carry%d" % h) for h in range(HALVES)]
+        cand = [keep.tile([P, PACK, HALF], F32, name="cand%d" % h) for h in range(HALVES)]
+        kept = [keep.tile([P, PACK, HALF], F32, name="kept%d" % h) for h in range(HALVES)]
+        grouped = [keep.tile([P, PACK * N], BF16, name="whb%d" % a, align_bytes=64) for a in range(PASSES)]
+        hw = [keep.tile([P, N], U32, name="hw%d" % a, align_bytes=64) for a in range(PASSES)]
+        hs = [keep.tile([P, N], U8, name="hs%d" % a, align_bytes=64) for a in range(PASSES)]
+
+        def round_wh(a, u):
+            dst = grouped[a][:].rearrange("p (t m j) -> p m j t", t=PACK, j=PACK)
+            src = wh_raw[a][:].rearrange("p j (m t) -> p m j t", t=PACK)
+            nc.scalar.copy(dst[:, 64 * u : 64 * (u + 1)], src[:, 64 * u : 64 * (u + 1)])
+
+        def quantise_wh(a):
+            nc.vector.quantize_mx(out=hw[a][:].bitcast(FP8X4), scales=hs[a][:], in_=grouped[a][:])
+
+        def gate(t, h):
+            acc = psum.tile([P, HALF], F32, name="acc")
+            for a in range(PASSES):
+                col = a * N + t * P
+                nc.tensor.matmul_mx(
+                    out=acc[:],
+                    lhsT=gw[:, 2 * col : 2 * (col + P)].bitcast(FP4X4),
+                    lhsT_scale=gsc[:, col : col + P],
+                    rhs=vw[h][:, 2 * a * HALF : 2 * (a + 1) * HALF].bitcast(FP4X4),
+                    rhs_scale=vs[a][:, h * HALF : (h + 1) * HALF],
+                    start=(a == 0),
+                    stop=(a == PASSES - 1),
+                )
+            nc.scalar.activation(carry[h][:, t, :], acc[:], ACT.Sigmoid, bias=nbias[:, t : t + 1], scale=-1.0)
+
+        def candidate(t, h):
+            acc = psum.tile([P, HALF], F32, name="acc")
+            for a in range(PASSES):
+                nc.tensor.matmul_mx(
+                    out=acc[:],
+                    lhsT=hw[a][:, t * P : (t + 1) * P].bitcast(FP8X4),
+                    lhsT_scale=hs[a][:, t * P : (t + 1) * P],
+                    rhs=vw[h][:, 2 * a * HALF : 2 * (a + 1) * HALF].bitcast(FP4X4),
+                    rhs_scale=vs[a][:, h * HALF : (h + 1) * HALF],
+                    start=(a == 0),
+                    stop=(a == PASSES - 1),
+                )
+            nc.scalar.activation(cand[h][:, t, :], acc[:], ACT.Tanh)
+
+        def gather_carry(t, h):
+            nc.vector.tensor_tensor(
+                kept[h][:, t, :], r_sb[t][:].indirect(offsets[:, 32 * h : 32 * (h + 1)]), carry[h][:, t, :], ALU.mult
+            )
+
+        round_wh(0, 0)
+        gate(0, 0)
+        round_wh(0, 1)
+        gate(0, 1)
+        for h in range(HALVES):
+            gather_carry(0, h)
+        quantise_wh(0)
+        for h in range(HALVES):
+            gate(1, h)
+        round_wh(1, 0)
+        round_wh(1, 1)
+        for t in range(2, PACK):
+            for h in range(HALVES):
+                gate(t, h)
+        for h in range(HALVES):
+            gather_carry(1, h)
+        quantise_wh(1)
+        for h in range(HALVES):
+            for t in range(PACK):
+                candidate(t, h)
+        for h in range(HALVES):
+            gather_carry(2, h)
+
+        y_rows = out_0.rearrange("(p t) j -> p t j", t=PACK)
+        y_words = out_1[0].rearrange("p j i -> p (j i)").bitcast(I32)
+        y_scales = keep.tile([P, J], U8, name="y_scales", align_bytes=64)
+
+        def quantise(c0, width, rounded):
+            y_codes = keep.tile([P, width], I32, name="y_codes%d" % c0, align_bytes=64)
+            nc.vector.quantize_mx(out=y_codes[:].bitcast(FP8X4), scales=y_scales[:, c0 : c0 + width], in_=rounded[:])
+            nc.sync.dma_start(y_words[:, c0 : c0 + width], y_codes[:])
+
+        pending = None
+        for c0, width in CHUNKS:
+            h = c0 // HALF
+            cols = slice(c0 - h * HALF, c0 - h * HALF + width)
+            if c0 % HALF == 0:
+                gather_carry(PACK - 1, h)
+            gated = keep.tile([P, PACK, width], F32, name="gated%d" % c0)
+            nc.vector.scalar_tensor_tensor(gated[:], carry[h][:, :, cols], 1.0, cand[h][:, :, cols], ALU.subtract, ALU.mult)
+            y = keep.tile([P, PACK, width], F32, name="y%d" % c0)
+            nc.vector.tensor_tensor(y[:], kept[h][:, :, cols], gated[:], ALU.subtract)
+            nc.sync.dma_start(y_rows[:, :, c0 : c0 + width], y[:])
+            rounded = keep.tile([P, PACK * width], BF16, name="rounded%d" % c0, align_bytes=64)
+            dst = rounded[:].rearrange("p (c i t) -> p c t i", t=PACK, i=4)
+            src = y[:].rearrange("p t (c i) -> p c t i", i=4)
+            if pending is not None:
+                quantise(*pending)
+            if c0 + width == J:
+                nc.vector.tensor_copy(dst, src)
+            else:
+                nc.scalar.copy(dst, src)
+            pending = (c0, width, rounded)
+        quantise(*pending)
+        for q in range(4):
+            eng = nc.sync if q % 2 == 0 else nc.scalar
+            eng.dma_start(out_2[0, 4 * q : 4 * q + 4, :].bitcast(I32), y_scales[32 * q : 32 * q + 4, :].bitcast(I32))

@@ -33,23 +33,22 @@ def tile_list_hwayt_tanhP_kernel(
         psum = ctx.enter_context(tc.psum_pool(name="psum", bufs=8))
 
         tsc = keep.tile([P, T], U8, name="tsc", align_bytes=64)
-        nc.vector.memset(tsc[:].bitcast(I32), 0)
-        gsc_raw = keep.tile([P, PASSES * N], U8, name="gsc_raw", align_bytes=64)
+        nc.vector.memset(tsc[:, : T // 2].bitcast(I32), 0)
+        nc.gpsimd.memset(tsc[:, T // 2 :].bitcast(I32), 0)
+        gsc_raw = keep.tile([P, PASSES * N], U8, name="gsc_raw", tag="slot1", align_bytes=64)
         nc.vector.memset(gsc_raw[:].bitcast(I32), 0)
         vs1 = keep.tile([P, J], U8, name="vs1", align_bytes=64)
         nc.vector.memset(vs1[:].bitcast(I32), 0)
 
         offsets = keep.tile([P, J // 16], U16, name="offsets")
         nc.sync.dma_start(offsets[:], offs)
-        bias = keep.tile([P, PACK], F32, name="bias")
-        nc.sync.dma_start(bias[:], bg.rearrange("(p t) -> p t", t=PACK))
-        gw_raw = keep.tile([P, PASSES, N // 2], I32, name="gw_raw", align_bytes=64)
-        nc.sync.dma_start(gw_raw[:], wg_words.bitcast(I32).rearrange("a p n -> p a n"))
         for q in range(4):
             nc.sync.dma_start(
                 tsc[32 * q : 32 * q + 8, :].bitcast(I32),
                 tab_scales[:, 4 * q : 4 * q + 4, :].bitcast(I32),
             )
+        gw_raw = keep.tile([P, PASSES, N // 2], I32, name="gw_raw", align_bytes=64)
+        nc.sync.dma_start(gw_raw[:], wg_words.bitcast(I32).rearrange("a p n -> p a n"))
         tw = keep.tile([P, T], I32, name="tw", align_bytes=64)
         nc.sync.dma_start(tw[:], tab_words[0].rearrange("p t b -> p (t b)").bitcast(I32))
         for q in range(4):
@@ -57,17 +56,33 @@ def tile_list_hwayt_tanhP_kernel(
                 gsc_raw[32 * q : 32 * q + 4, :].bitcast(I32).rearrange("r (a n) -> r a n", a=PASSES),
                 wg_scales[:, 4 * q : 4 * q + 4, :].bitcast(I32).rearrange("a r n -> r a n"),
             )
+        bias = keep.tile([P, PACK], F32, name="bias")
+        nc.sync.dma_start(bias[:], bg.rearrange("(p t) -> p t", t=PACK))
         r_rows = rT.rearrange("(p t) c -> t p c", t=PACK)
-        r_sb = [keep.tile([P, T], F32, name="r%d" % t, align_bytes=64) for t in range(PACK)]
-        wh_raw = [keep.tile([P, PACK, N], F32, name="wh%d" % a, align_bytes=64) for a in range(PASSES)]
-        for a in range(PASSES):
-            nc.sync.dma_start(wh_raw[a][:], wh[512 * a : 512 * (a + 1), :].rearrange("(p j) n -> p j n", j=PACK))
-            nc.sync.dma_start(r_sb[a][:], r_rows[a])
-        for t in range(PASSES, PACK):
-            nc.sync.dma_start(r_sb[t][:], r_rows[t])
+        carry = keep.tile([P, PACK * J], F32, name="carry", align_bytes=64)
 
-        nbias = keep.tile([P, PACK], F32, name="nbias")
-        nc.scalar.mul(nbias[:], bias[:], -1.0)
+        def load_r(t, tag):
+            rows = keep.tile([P, T], F32, name="r%d" % t, tag=tag, align_bytes=64)
+            nc.sync.dma_start(rows[:], r_rows[t])
+            return rows
+
+        def load_wh(a, rows):
+            nc.sync.dma_start(rows, wh[512 * a : 512 * (a + 1), :].rearrange("(p j) n -> p (j n)", j=PACK))
+
+        wh0 = keep.tile([P, PACK * N], F32, name="wh0", tag="slot3", align_bytes=64)
+        load_wh(0, wh0[:])
+
+        nbias = {}
+
+        def negate_bias(t0, tag):
+            pair = keep.tile([P, 2], F32, name="nbias%d" % t0, tag=tag, align_bytes=64)
+            nc.vector.tensor_scalar(pair[:], bias[:, t0 : t0 + 2], -1.0, None, ALU.mult)
+            nbias[t0] = pair[:, 0:1]
+            nbias[t0 + 1] = pair[:, 1:2]
+
+        warm = keep.tile([P, 1], F32, name="warm")
+        nc.vector.memset(warm[:], 0.0)
+        nc.scalar.activation(warm[:], warm[:], ACT.Sigmoid)
         gw = keep.tile([P, PASSES * N * 2], U8, name="gw", align_bytes=64)
         nc.vector.tensor_copy(
             gw[:].bitcast(U16).rearrange("p (a t m) -> p a t m", a=PASSES, t=PACK),
@@ -76,44 +91,54 @@ def tile_list_hwayt_tanhP_kernel(
 
         vs0 = keep.tile([P, J], U8, name="vs0", align_bytes=64)
         nc.vector.tensor_copy(vs0[:], tsc[:].indirect(offsets[:]))
-        nc.scalar.dma_start(vs1[0:112, :].bitcast(I32), vs0[4:116, :].bitcast(I32))
+        nc.sync.dma_start(vs1[0:112, :].bitcast(I32), vs0[4:116, :].bitcast(I32))
         vs = (vs0, vs1)
+        r0 = load_r(0, "r0")
 
-        gsc = keep.tile([P, PASSES * N], U8, name="gsc", align_bytes=64)
-        vw = []
-        for h in range(HALVES):
-            pair = keep.tile([P, HALF], U32, name="pair%d" % h, align_bytes=64)
+        def gather_words(h, tag):
+            pair = keep.tile([P, HALF], U32, name="pair%d" % h, tag=tag, align_bytes=64)
             nc.vector.tensor_copy(pair[:], tw[:].bitcast(U32).indirect(offsets[:, 32 * h : 32 * (h + 1)]))
-            if h == 0:
-                nc.vector.tensor_copy(
-                    gsc[:].rearrange("p (a t m) -> p a t m", a=PASSES, t=PACK),
-                    gsc_raw[:].rearrange("p (a m t) -> p a t m", a=PASSES, t=PACK),
-                )
+            return pair
+
+        def part_words(h, pair):
             parted = keep.tile([P, PASSES * HALF * 2], U8, name="parted%d" % h, align_bytes=64)
             nc.vector.tensor_copy(
                 parted[:].bitcast(U16).rearrange("p (d j) -> p d j", d=PASSES),
                 pair[:].bitcast(U16).rearrange("p (j d) -> p d j", d=PASSES),
             )
-            vw.append(parted)
+            return parted
 
-        carry = [keep.tile([P, PACK, HALF], F32, name="carry%d" % h) for h in range(HALVES)]
-        cand = [keep.tile([P, PACK, HALF], F32, name="cand%d" % h) for h in range(HALVES)]
-        kept = [keep.tile([P, PACK, HALF], F32, name="kept%d" % h) for h in range(HALVES)]
-        grouped = [keep.tile([P, PACK * N], BF16, name="whb%d" % a, align_bytes=64) for a in range(PASSES)]
+        pair0 = gather_words(0, "pair0")
+        gsc = keep.tile([P, PASSES * N], U8, name="gsc", align_bytes=64)
+        nc.vector.tensor_copy(
+            gsc[:].rearrange("p (a t m) -> p a t m", a=PASSES, t=PACK),
+            gsc_raw[:].rearrange("p (a m t) -> p a t m", a=PASSES, t=PACK),
+        )
+        vw = [part_words(0, pair0)]
+        wh1 = keep.tile([P, PACK * N], F32, name="wh1", tag="slot2", align_bytes=64)
+        load_wh(1, wh1[:])
+        wh_raw = (wh0[:], wh1[:])
+        negate_bias(0, "nbias0")
+        pair1 = gather_words(1, "slot1")
+        vw.append(part_words(1, pair1))
+
+        cand = keep.tile([P, PACK * J], F32, name="cand", align_bytes=64)
+        kept = keep.tile([P, PACK * J], F32, name="kept", align_bytes=64)
+        grouped = [keep.tile([P, PACK * N], BF16, name="whb%d" % a, tag="slot%d" % (4 + a), align_bytes=64) for a in range(PASSES)]
         hw = [keep.tile([P, N], U32, name="hw%d" % a, align_bytes=64) for a in range(PASSES)]
         hs = [keep.tile([P, N], U8, name="hs%d" % a, align_bytes=64) for a in range(PASSES)]
 
-        def round_wh(a, u):
+        def round_wh(a, u, copy):
             dst = grouped[a][:].rearrange("p (t m j) -> p m j t", t=PACK, j=PACK)
-            src = wh_raw[a][:].rearrange("p j (m t) -> p m j t", t=PACK)
-            nc.scalar.copy(dst[:, 64 * u : 64 * (u + 1)], src[:, 64 * u : 64 * (u + 1)])
+            src = wh_raw[a].rearrange("p (j m t) -> p m j t", j=PACK, t=PACK)
+            copy(dst[:, 64 * u : 64 * (u + 1)], src[:, 64 * u : 64 * (u + 1)])
 
         def quantise_wh(a):
             nc.vector.quantize_mx(out=hw[a][:].bitcast(FP8X4), scales=hs[a][:], in_=grouped[a][:])
 
         def gate(t, h):
             acc = psum.tile([P, HALF], F32, name="acc")
-            for a in range(PASSES):
+            for a in (1, 0):
                 col = a * N + t * P
                 nc.tensor.matmul_mx(
                     out=acc[:],
@@ -121,56 +146,67 @@ def tile_list_hwayt_tanhP_kernel(
                     lhsT_scale=gsc[:, col : col + P],
                     rhs=vw[h][:, 2 * a * HALF : 2 * (a + 1) * HALF].bitcast(FP4X4),
                     rhs_scale=vs[a][:, h * HALF : (h + 1) * HALF],
-                    start=(a == 0),
-                    stop=(a == PASSES - 1),
+                    start=(a == 1),
+                    stop=(a == 0),
                 )
-            nc.scalar.activation(carry[h][:, t, :], acc[:], ACT.Sigmoid, bias=nbias[:, t : t + 1], scale=-1.0)
+            c0 = t * J + h * HALF
+            nc.scalar.activation(carry[:, c0 : c0 + HALF], acc[:], ACT.Sigmoid, bias=nbias[t], scale=-1.0)
 
         def candidate(t, h):
             acc = psum.tile([P, HALF], F32, name="acc")
-            for a in range(PASSES):
+            for a in (1, 0):
                 nc.tensor.matmul_mx(
                     out=acc[:],
                     lhsT=hw[a][:, t * P : (t + 1) * P].bitcast(FP8X4),
                     lhsT_scale=hs[a][:, t * P : (t + 1) * P],
                     rhs=vw[h][:, 2 * a * HALF : 2 * (a + 1) * HALF].bitcast(FP4X4),
                     rhs_scale=vs[a][:, h * HALF : (h + 1) * HALF],
-                    start=(a == 0),
-                    stop=(a == PASSES - 1),
+                    start=(a == 1),
+                    stop=(a == 0),
                 )
-            nc.scalar.activation(cand[h][:, t, :], acc[:], ACT.Tanh)
+            c0 = t * J + h * HALF
+            nc.scalar.activation(cand[:, c0 : c0 + HALF], acc[:], ACT.Tanh)
 
-        def gather_carry(t, h):
+        def gather_carry(rows, t, j0, width):
+            c0 = t * J + j0
             nc.vector.tensor_tensor(
-                kept[h][:, t, :], r_sb[t][:].indirect(offsets[:, 32 * h : 32 * (h + 1)]), carry[h][:, t, :], ALU.mult
+                kept[:, c0 : c0 + width],
+                rows[:].indirect(offsets[:, j0 // 16 : (j0 + width) // 16]),
+                carry[:, c0 : c0 + width],
+                ALU.mult,
             )
 
-        round_wh(0, 0)
+        round_wh(0, 0, nc.scalar.copy)
         gate(0, 0)
-        round_wh(0, 1)
+        round_wh(0, 1, nc.scalar.copy)
+        r1 = load_r(1, "r1")
+        gate(1, 0)
         gate(0, 1)
-        for h in range(HALVES):
-            gather_carry(0, h)
+        gate(1, 1)
         quantise_wh(0)
+        r2 = load_r(2, "r2")
         for h in range(HALVES):
-            gate(1, h)
-        round_wh(1, 0)
-        round_wh(1, 1)
+            gather_carry(r0, 0, h * HALF, HALF)
+        r3 = load_r(3, "r3")
+        round_wh(1, 0, nc.scalar.copy)
+        round_wh(1, 1, nc.vector.tensor_copy)
+        quantise_wh(1)
+        negate_bias(2, "slot2")
         for t in range(2, PACK):
             for h in range(HALVES):
                 gate(t, h)
-        for h in range(HALVES):
-            gather_carry(1, h)
-        quantise_wh(1)
+        gather_carry(r1, 1, 0, J)
         for h in range(HALVES):
             for t in range(PACK):
                 candidate(t, h)
-        for h in range(HALVES):
-            gather_carry(2, h)
+        gather_carry(r2, 2, 0, J)
 
         y_rows = out_0.rearrange("(p t) j -> p t j", t=PACK)
         y_words = out_1[0].rearrange("p j i -> p (j i)").bitcast(I32)
         y_scales = keep.tile([P, J], U8, name="y_scales", align_bytes=64)
+        carry_t = carry[:].rearrange("p (t j) -> p t j", t=PACK)
+        cand_t = cand[:].rearrange("p (t j) -> p t j", t=PACK)
+        kept_t = kept[:].rearrange("p (t j) -> p t j", t=PACK)
 
         def quantise(c0, width, rounded):
             y_codes = keep.tile([P, width], I32, name="y_codes%d" % c0, align_bytes=64)
@@ -179,15 +215,14 @@ def tile_list_hwayt_tanhP_kernel(
 
         pending = None
         for c0, width in CHUNKS:
-            h = c0 // HALF
-            cols = slice(c0 - h * HALF, c0 - h * HALF + width)
+            cols = slice(c0, c0 + width)
             if c0 % HALF == 0:
-                gather_carry(PACK - 1, h)
+                gather_carry(r3, PACK - 1, c0, HALF)
             gated = keep.tile([P, PACK, width], F32, name="gated%d" % c0)
-            nc.vector.scalar_tensor_tensor(gated[:], carry[h][:, :, cols], 1.0, cand[h][:, :, cols], ALU.subtract, ALU.mult)
+            nc.vector.scalar_tensor_tensor(gated[:], carry_t[:, :, cols], 1.0, cand_t[:, :, cols], ALU.subtract, ALU.mult)
             y = keep.tile([P, PACK, width], F32, name="y%d" % c0)
-            nc.vector.tensor_tensor(y[:], kept[h][:, :, cols], gated[:], ALU.subtract)
-            nc.sync.dma_start(y_rows[:, :, c0 : c0 + width], y[:])
+            nc.vector.tensor_tensor(y[:], kept_t[:, :, cols], gated[:], ALU.subtract)
+            nc.sync.dma_start(y_rows[:, :, cols], y[:])
             rounded = keep.tile([P, PACK * width], BF16, name="rounded%d" % c0, align_bytes=64)
             dst = rounded[:].rearrange("p (c i t) -> p c t i", t=PACK, i=4)
             src = y[:].rearrange("p t (c i) -> p c t i", i=4)

@@ -1,6 +1,7 @@
 from contextlib import ExitStack
 
 import concourse.mybir as mybir
+from concourse.masks import make_identity
 
 K, N, T, J = 1024, 512, 2048, 1024
 FLOPS = 2 * 2 * K * N * J
@@ -21,6 +22,8 @@ PACK = 4
 PASSES = K // (P * PACK)
 HALF = 512
 HALVES = J // HALF
+PE_SLICES = 3
+PE_CHUNKS = 2
 CHUNKS = ((0, 256), (256, 256), (512, 256), (768, 128), (896, 128))
 
 
@@ -33,8 +36,7 @@ def tile_list_hwayt_tanhP_kernel(
         psum = ctx.enter_context(tc.psum_pool(name="psum", bufs=8))
 
         tsc = keep.tile([P, T], U8, name="tsc", align_bytes=64)
-        nc.vector.memset(tsc[:, : T // 2].bitcast(I32), 0)
-        nc.gpsimd.memset(tsc[:, T // 2 :].bitcast(I32), 0)
+        nc.vector.memset(tsc[:].bitcast(I32), 0)
         gsc_raw = keep.tile([P, PASSES * N], U8, name="gsc_raw", tag="slot1", align_bytes=64)
         nc.vector.memset(gsc_raw[:].bitcast(I32), 0)
         vs1 = keep.tile([P, J], U8, name="vs1", align_bytes=64)
@@ -42,11 +44,9 @@ def tile_list_hwayt_tanhP_kernel(
 
         offsets = keep.tile([P, J // 16], U16, name="offsets")
         nc.sync.dma_start(offsets[:], offs)
-        for q in range(4):
-            nc.sync.dma_start(
-                tsc[32 * q : 32 * q + 8, :].bitcast(I32),
-                tab_scales[:, 4 * q : 4 * q + 4, :].bitcast(I32),
-            )
+        scale_rows = tab_scales.bitcast(I32).rearrange("a (q r) c -> r q a c", r=4)
+        for r in range(4):
+            nc.sync.dma_start(tsc[r:P:16, :].bitcast(I32), scale_rows[r])
         gw_raw = keep.tile([P, PASSES, N // 2], I32, name="gw_raw", align_bytes=64)
         nc.sync.dma_start(gw_raw[:], wg_words.bitcast(I32).rearrange("a p n -> p a n"))
         tw = keep.tile([P, T], I32, name="tw", align_bytes=64)
@@ -74,12 +74,14 @@ def tile_list_hwayt_tanhP_kernel(
 
         nbias = {}
 
-        def negate_bias(t0, tag):
-            pair = keep.tile([P, 2], F32, name="nbias%d" % t0, tag=tag, align_bytes=64)
-            nc.vector.tensor_scalar(pair[:], bias[:, t0 : t0 + 2], -1.0, None, ALU.mult)
-            nbias[t0] = pair[:, 0:1]
-            nbias[t0 + 1] = pair[:, 1:2]
+        def negate_bias(t0, t1, tag):
+            cols = keep.tile([P, t1 - t0], F32, name="nbias%d" % t0, tag=tag, align_bytes=64)
+            nc.scalar.mul(cols[:], bias[:, t0:t1], -1.0)
+            for t in range(t0, t1):
+                nbias[t] = cols[:, t - t0 : t - t0 + 1]
 
+        ident = keep.tile([P, P], F32, name="ident", align_bytes=64)
+        make_identity(nc, ident[:])
         warm = keep.tile([P, 1], F32, name="warm")
         nc.vector.memset(warm[:], 0.0)
         nc.scalar.activation(warm[:], warm[:], ACT.Sigmoid)
@@ -91,9 +93,11 @@ def tile_list_hwayt_tanhP_kernel(
 
         vs0 = keep.tile([P, J], U8, name="vs0", align_bytes=64)
         nc.vector.tensor_copy(vs0[:], tsc[:].indirect(offsets[:]))
-        nc.sync.dma_start(vs1[0:112, :].bitcast(I32), vs0[4:116, :].bitcast(I32))
+        r0 = keep.tile([P, T], F32, name="r0", align_bytes=64)
+        nc.sync.dma_start(r0[:, : T // 2], r_rows[0][:, : T // 2])
+        nc.sync.dma_start(vs1[0:112, :].bitcast(I32), vs0[16:128, :].bitcast(I32))
+        nc.sync.dma_start(r0[:, T // 2 :], r_rows[0][:, T // 2 :])
         vs = (vs0, vs1)
-        r0 = load_r(0, "r0")
 
         def gather_words(h, tag):
             pair = keep.tile([P, HALF], U32, name="pair%d" % h, tag=tag, align_bytes=64)
@@ -115,10 +119,15 @@ def tile_list_hwayt_tanhP_kernel(
             gsc_raw[:].rearrange("p (a m t) -> p a t m", a=PASSES, t=PACK),
         )
         vw = [part_words(0, pair0)]
-        wh1 = keep.tile([P, PACK * N], F32, name="wh1", tag="slot2", align_bytes=64)
-        load_wh(1, wh1[:])
-        wh_raw = (wh0[:], wh1[:])
-        negate_bias(0, "nbias0")
+        wh1_rows = wh[512:1024, :].rearrange("(p j) n -> p j n", j=PACK)
+        wh1 = []
+        for u in range(2):
+            cols = keep.tile([P, PACK, N // 2], F32, name="wh1_%d" % u, tag="wh1_%d" % u, align_bytes=64)
+            nc.sync.dma_start(cols[:], wh1_rows[:, :, u * N // 2 : (u + 1) * N // 2])
+            wh1.append(cols[:])
+        wh0_cols = wh0[:].rearrange("p (j n) -> p j n", j=PACK)
+        wh_raw = ((wh0_cols[:, :, : N // 2], wh0_cols[:, :, N // 2 :]), wh1)
+        negate_bias(0, 1, "nbias0")
         pair1 = gather_words(1, "slot1")
         vw.append(part_words(1, pair1))
 
@@ -130,8 +139,7 @@ def tile_list_hwayt_tanhP_kernel(
 
         def round_wh(a, u, copy):
             dst = grouped[a][:].rearrange("p (t m j) -> p m j t", t=PACK, j=PACK)
-            src = wh_raw[a].rearrange("p (j m t) -> p m j t", j=PACK, t=PACK)
-            copy(dst[:, 64 * u : 64 * (u + 1)], src[:, 64 * u : 64 * (u + 1)])
+            copy(dst[:, 64 * u : 64 * (u + 1)], wh_raw[a][u].rearrange("p j (m t) -> p m j t", t=PACK))
 
         def quantise_wh(a):
             nc.vector.quantize_mx(out=hw[a][:].bitcast(FP8X4), scales=hs[a][:], in_=grouped[a][:])
@@ -165,7 +173,7 @@ def tile_list_hwayt_tanhP_kernel(
                     stop=(a == 0),
                 )
             c0 = t * J + h * HALF
-            nc.scalar.activation(cand[:, c0 : c0 + HALF], acc[:], ACT.Tanh)
+            nc.scalar.activation(cand[:, c0 : c0 + HALF], acc[:], ACT.Tanh, scale=-1.0)
 
         def gather_carry(rows, t, j0, width):
             c0 = t * J + j0
@@ -180,19 +188,17 @@ def tile_list_hwayt_tanhP_kernel(
         gate(0, 0)
         round_wh(0, 1, nc.scalar.copy)
         r1 = load_r(1, "r1")
-        gate(1, 0)
         gate(0, 1)
-        gate(1, 1)
         quantise_wh(0)
         r2 = load_r(2, "r2")
         for h in range(HALVES):
             gather_carry(r0, 0, h * HALF, HALF)
         r3 = load_r(3, "r3")
         round_wh(1, 0, nc.scalar.copy)
+        negate_bias(1, PACK, "wh1_0")
         round_wh(1, 1, nc.vector.tensor_copy)
         quantise_wh(1)
-        negate_bias(2, "slot2")
-        for t in range(2, PACK):
+        for t in range(1, PACK):
             for h in range(HALVES):
                 gate(t, h)
         gather_carry(r1, 1, 0, J)
@@ -213,27 +219,68 @@ def tile_list_hwayt_tanhP_kernel(
             nc.vector.quantize_mx(out=y_codes[:].bitcast(FP8X4), scales=y_scales[:, c0 : c0 + width], in_=rounded[:])
             nc.sync.dma_start(y_words[:, c0 : c0 + width], y_codes[:])
 
-        pending = None
-        for c0, width in CHUNKS:
+        gated = {}
+        rounded = {}
+
+        def gate_candidate(c):
+            c0, width = CHUNKS[c]
             cols = slice(c0, c0 + width)
-            if c0 % HALF == 0:
-                gather_carry(r3, PACK - 1, c0, HALF)
-            gated = keep.tile([P, PACK, width], F32, name="gated%d" % c0)
-            nc.vector.scalar_tensor_tensor(gated[:], carry_t[:, :, cols], 1.0, cand_t[:, :, cols], ALU.subtract, ALU.mult)
-            y = keep.tile([P, PACK, width], F32, name="y%d" % c0)
-            nc.vector.tensor_tensor(y[:], kept_t[:, :, cols], gated[:], ALU.subtract)
-            nc.sync.dma_start(y_rows[:, :, cols], y[:])
-            rounded = keep.tile([P, PACK * width], BF16, name="rounded%d" % c0, align_bytes=64)
-            dst = rounded[:].rearrange("p (c i t) -> p c t i", t=PACK, i=4)
-            src = y[:].rearrange("p t (c i) -> p c t i", i=4)
-            if pending is not None:
-                quantise(*pending)
-            if c0 + width == J:
-                nc.vector.tensor_copy(dst, src)
-            else:
-                nc.scalar.copy(dst, src)
-            pending = (c0, width, rounded)
-        quantise(*pending)
+            gated[c] = keep.tile([P, PACK, width], F32, name="gated%d" % c0)
+            nc.vector.scalar_tensor_tensor(gated[c][:], carry_t[:, :, cols], 1.0, cand_t[:, :, cols], ALU.subtract, ALU.mult)
+
+        def combine(c):
+            c0, width = CHUNKS[c]
+            cols = slice(c0, c0 + width)
+            t0 = PE_SLICES if c < PE_CHUNKS else 0
+            nc.vector.tensor_tensor(y[c][:, t0:, :], kept_t[:, t0:, cols], gated[c][:, t0:, :], ALU.add)
+            nc.sync.dma_start(y_rows[:, :, cols], y[c][:])
+
+        def add_turned(c, b):
+            j0 = CHUNKS[c][0] + b * P
+            acc = psum.tile([P, HALF], F32, name="acc")
+            for t in range(PE_SLICES):
+                block = acc[:, t * P : (t + 1) * P]
+                nc.tensor.matmul(block, gated[c][:, t, b * P : (b + 1) * P], ident[:], is_transpose=True, start=True, stop=False)
+                nc.tensor.matmul(block, kept_t[:, t, j0 : j0 + P], ident[:], is_transpose=True, start=False, stop=True)
+            turned = keep.tile([P, PE_SLICES * P], F32, name="turned%d" % j0, align_bytes=64)
+            nc.scalar.copy(turned[:], acc[:, : PE_SLICES * P])
+            return turned
+
+        def turn_back(c, b, turned):
+            acc = psum.tile([P, HALF], F32, name="acc")
+            for t in range(PE_SLICES):
+                nc.tensor.transpose(acc[:, t * P : (t + 1) * P], turned[:, t * P : (t + 1) * P], ident[:])
+            nc.scalar.copy(
+                y[c][:, :PE_SLICES, b * P : (b + 1) * P], acc[:, : PE_SLICES * P].rearrange("p (t j) -> p t j", t=PE_SLICES)
+            )
+
+        def round_y(c, y, copy):
+            c0, width = CHUNKS[c]
+            rounded[c] = keep.tile([P, PACK * width], BF16, name="rounded%d" % c0, align_bytes=64)
+            copy(rounded[c][:].rearrange("p (c i t) -> p c t i", t=PACK, i=4), y[:].rearrange("p t (c i) -> p c t i", i=4))
+
+        y = [keep.tile([P, PACK, width], F32, name="y%d" % c0) for c0, width in CHUNKS]
+        last = len(CHUNKS) - 1
+        blocks = [(c, b) for c in range(PE_CHUNKS) for b in range(CHUNKS[c][1] // P)]
+        for c in range(PE_CHUNKS):
+            gate_candidate(c)
+        waiting = None
+        for c, b in blocks:
+            turned = add_turned(c, b)
+            if waiting is not None:
+                turn_back(*waiting)
+            waiting = (c, b, turned)
+        turn_back(*waiting)
+        for h in range(HALVES):
+            gather_carry(r3, PACK - 1, h * HALF, HALF)
+        for c in range(len(CHUNKS)):
+            if PE_CHUNKS <= c + 1 <= last:
+                gate_candidate(c + 1)
+            combine(c)
+            if c > 0:
+                quantise(*CHUNKS[c - 1], rounded[c - 1])
+            round_y(c, y[c], nc.vector.tensor_copy if c == last else nc.scalar.copy)
+        quantise(*CHUNKS[last], rounded[last])
         for q in range(4):
             eng = nc.sync if q % 2 == 0 else nc.scalar
             eng.dma_start(out_2[0, 4 * q : 4 * q + 4, :].bitcast(I32), y_scales[32 * q : 32 * q + 4, :].bitcast(I32))

@@ -19,12 +19,18 @@ ACT = mybir.ActivationFunctionType
 
 P = 128
 PACK = 4
-PASSES = K // (P * PACK)
+K_PASS = P * PACK
+PASSES = K // K_PASS
+QUADS = 4
+PLANE_ROWS = 4
+GROUP = 16
 HALF = 512
 HALVES = J // HALF
-PE_SLICES = 3
-PE_CHUNKS = 2
-CHUNKS = ((0, 256), (256, 256), (512, 256), (768, 128), (896, 128))
+SHIFT = 16
+EARLY = 2
+CHUNK = HALF // EARLY
+CHUNKS = J // CHUNK
+QUANTISE_LAG = 2
 
 
 def tile_list_hwayt_tanhP_kernel(
@@ -32,255 +38,232 @@ def tile_list_hwayt_tanhP_kernel(
 ):
     nc = tc.nc
     with ExitStack() as ctx:
-        keep = ctx.enter_context(tc.tile_pool(name="keep", bufs=1))
+        sbuf = ctx.enter_context(tc.tile_pool(name="sbuf", bufs=1))
         psum = ctx.enter_context(tc.psum_pool(name="psum", bufs=8))
 
-        tsc = keep.tile([P, T], U8, name="tsc", align_bytes=64)
-        nc.vector.memset(tsc[:].bitcast(I32), 0)
-        gsc_raw = keep.tile([P, PASSES * N], U8, name="gsc_raw", tag="slot1", align_bytes=64)
-        nc.vector.memset(gsc_raw[:].bitcast(I32), 0)
-        vs1 = keep.tile([P, J], U8, name="vs1", align_bytes=64)
-        nc.vector.memset(vs1[:].bitcast(I32), 0)
+        def list_part(j0, width):
+            return offsets[:, j0 // GROUP : (j0 + width) // GROUP]
 
-        offsets = keep.tile([P, J // 16], U16, name="offsets")
+        table_scales = sbuf.tile([P, T], U8, name="table_scales", align_bytes=64)
+        nc.vector.memset(table_scales[:].bitcast(I32), 0)
+        wg_scales_in = sbuf.tile([P, PASSES * N], U8, name="wg_scales_in", tag="wg_scales_in", align_bytes=64)
+        nc.vector.memset(wg_scales_in[:].bitcast(I32), 0)
+        v_plane1 = sbuf.tile([P, J], U8, name="v_plane1", align_bytes=64)
+        nc.vector.memset(v_plane1[:].bitcast(I32), 0)
+
+        offsets = sbuf.tile([P, J // GROUP], U16, name="offsets")
         nc.sync.dma_start(offsets[:], offs)
-        scale_rows = tab_scales.bitcast(I32).rearrange("a (q r) c -> r q a c", r=4)
-        for r in range(4):
-            nc.sync.dma_start(tsc[r:P:16, :].bitcast(I32), scale_rows[r])
-        gw_raw = keep.tile([P, PASSES, N // 2], I32, name="gw_raw", align_bytes=64)
-        nc.sync.dma_start(gw_raw[:], wg_words.bitcast(I32).rearrange("a p n -> p a n"))
-        tw = keep.tile([P, T], I32, name="tw", align_bytes=64)
-        nc.sync.dma_start(tw[:], tab_words[0].rearrange("p t b -> p (t b)").bitcast(I32))
-        for q in range(4):
+        table_scale_rows = tab_scales.bitcast(I32).rearrange("a (q r) c -> r q a c", r=PLANE_ROWS)
+        for r in range(PLANE_ROWS):
+            nc.sync.dma_start(table_scales[r:P:SHIFT, :].bitcast(I32), table_scale_rows[r])
+        wg_words_in = sbuf.tile([P, PASSES, N // 2], I32, name="wg_words_in", align_bytes=64)
+        nc.sync.dma_start(wg_words_in[:], wg_words.bitcast(I32).rearrange("a p n -> p a n"))
+        table_words = sbuf.tile([P, T], I32, name="table_words", align_bytes=64)
+        nc.sync.dma_start(table_words[:], tab_words[0].rearrange("p c b -> p (c b)").bitcast(I32))
+        for q in range(QUADS):
             nc.sync.dma_start(
-                gsc_raw[32 * q : 32 * q + 4, :].bitcast(I32).rearrange("r (a n) -> r a n", a=PASSES),
-                wg_scales[:, 4 * q : 4 * q + 4, :].bitcast(I32).rearrange("a r n -> r a n"),
+                wg_scales_in[32 * q : 32 * q + PLANE_ROWS, :].bitcast(I32).rearrange("r (a n) -> r a n", a=PASSES),
+                wg_scales[:, PLANE_ROWS * q : PLANE_ROWS * (q + 1), :].bitcast(I32).rearrange("a r n -> r a n"),
             )
-        bias = keep.tile([P, PACK], F32, name="bias")
+        bias = sbuf.tile([P, PACK], F32, name="bias")
         nc.sync.dma_start(bias[:], bg.rearrange("(p t) -> p t", t=PACK))
-        r_rows = rT.rearrange("(p t) c -> t p c", t=PACK)
-        carry = keep.tile([P, PACK * J], F32, name="carry", align_bytes=64)
 
-        def load_r(t, tag):
-            rows = keep.tile([P, T], F32, name="r%d" % t, tag=tag, align_bytes=64)
-            nc.sync.dma_start(rows[:], r_rows[t])
-            return rows
+        wh_rows = wh.rearrange("(a p i) n -> a p i n", p=P, i=PACK)
+        wh_first = sbuf.tile([P, PACK, N], F32, name="wh_first", align_bytes=64)
+        nc.sync.dma_start(wh_first[:], wh_rows[0])
+        wh_second = [sbuf.tile([P, PACK, N // 2], F32, name="wh_second%d" % u, align_bytes=64) for u in range(2)]
+        nc.sync.dma_start(wh_second[0][:], wh_rows[1][:, :, : N // 2])
 
-        def load_wh(a, rows):
-            nc.sync.dma_start(rows, wh[512 * a : 512 * (a + 1), :].rearrange("(p j) n -> p (j n)", j=PACK))
-
-        wh0 = keep.tile([P, PACK * N], F32, name="wh0", tag="slot3", align_bytes=64)
-        load_wh(0, wh0[:])
-
-        nbias = {}
-
-        def negate_bias(t0, t1, tag):
-            cols = keep.tile([P, t1 - t0], F32, name="nbias%d" % t0, tag=tag, align_bytes=64)
-            nc.scalar.mul(cols[:], bias[:, t0:t1], -1.0)
-            for t in range(t0, t1):
-                nbias[t] = cols[:, t - t0 : t - t0 + 1]
-
-        ident = keep.tile([P, P], F32, name="ident", align_bytes=64)
+        ident = sbuf.tile([P, P], F32, name="ident", align_bytes=64)
         make_identity(nc, ident[:])
-        warm = keep.tile([P, 1], F32, name="warm")
+        warm = sbuf.tile([P, 1], F32, name="warm")
         nc.vector.memset(warm[:], 0.0)
         nc.scalar.activation(warm[:], warm[:], ACT.Sigmoid)
-        gw = keep.tile([P, PASSES * N * 2], U8, name="gw", align_bytes=64)
+        minus_bias = sbuf.tile([P, PACK], F32, name="minus_bias")
+        nc.scalar.mul(minus_bias[:], bias[:], -1.0)
+
+        wg_codes = sbuf.tile([P, PASSES * N * 2], U8, name="wg_codes", align_bytes=64)
         nc.vector.tensor_copy(
-            gw[:].bitcast(U16).rearrange("p (a t m) -> p a t m", a=PASSES, t=PACK),
-            gw_raw[:].rearrange("p a n -> p (a n)").bitcast(U16).rearrange("p (a m t) -> p a t m", a=PASSES, t=PACK),
+            wg_codes[:].bitcast(U16).rearrange("p (a t m) -> p a t m", a=PASSES, t=PACK),
+            wg_words_in[:].rearrange("p a n -> p (a n)").bitcast(U16).rearrange("p (a m t) -> p a t m", a=PASSES, t=PACK),
         )
 
-        vs0 = keep.tile([P, J], U8, name="vs0", align_bytes=64)
-        nc.vector.tensor_copy(vs0[:], tsc[:].indirect(offsets[:]))
-        r0 = keep.tile([P, T], F32, name="r0", align_bytes=64)
-        nc.sync.dma_start(r0[:, : T // 2], r_rows[0][:, : T // 2])
-        nc.sync.dma_start(vs1[0:112, :].bitcast(I32), vs0[16:128, :].bitcast(I32))
-        nc.sync.dma_start(r0[:, T // 2 :], r_rows[0][:, T // 2 :])
-        vs = (vs0, vs1)
+        v_plane0 = sbuf.tile([P, J], U8, name="v_plane0", align_bytes=64)
+        nc.vector.tensor_copy(v_plane0[:], table_scales[:].indirect(offsets[:]))
+        nc.sync.dma_start(v_plane1[: P - SHIFT, :].bitcast(I32), v_plane0[SHIFT:, :].bitcast(I32))
+        v_planes = (v_plane0, v_plane1)
+
+        nc.sync.dma_start(wh_second[1][:], wh_rows[1][:, :, N // 2 :])
+        r_rows = rT.rearrange("(p t) c -> t p c", t=PACK)
+        r_slices = [sbuf.tile([P, T], F32, name="r%d" % t, tag="r%d" % t, align_bytes=64) for t in range(PACK)]
+        for t in range(PACK):
+            nc.sync.dma_start(r_slices[t][:], r_rows[t])
 
         def gather_words(h, tag):
-            pair = keep.tile([P, HALF], U32, name="pair%d" % h, tag=tag, align_bytes=64)
-            nc.vector.tensor_copy(pair[:], tw[:].bitcast(U32).indirect(offsets[:, 32 * h : 32 * (h + 1)]))
-            return pair
+            pairs = sbuf.tile([P, HALF], U32, name="pairs%d" % h, tag=tag, align_bytes=64)
+            nc.vector.tensor_copy(pairs[:], table_words[:].bitcast(U32).indirect(list_part(h * HALF, HALF)))
+            return pairs
 
-        def part_words(h, pair):
-            parted = keep.tile([P, PASSES * HALF * 2], U8, name="parted%d" % h, align_bytes=64)
+        def part_words(h, pairs):
+            parted = sbuf.tile([P, PASSES * HALF * 2], U8, name="v_codes%d" % h, align_bytes=64)
             nc.vector.tensor_copy(
-                parted[:].bitcast(U16).rearrange("p (d j) -> p d j", d=PASSES),
-                pair[:].bitcast(U16).rearrange("p (j d) -> p d j", d=PASSES),
+                parted[:].bitcast(U16).rearrange("p (a j) -> p a j", a=PASSES),
+                pairs[:].bitcast(U16).rearrange("p (j a) -> p a j", a=PASSES),
             )
             return parted
 
-        pair0 = gather_words(0, "pair0")
-        gsc = keep.tile([P, PASSES * N], U8, name="gsc", align_bytes=64)
+        pairs0 = gather_words(0, "pairs0")
+        wg_planes = sbuf.tile([P, PASSES * N], U8, name="wg_planes", align_bytes=64)
         nc.vector.tensor_copy(
-            gsc[:].rearrange("p (a t m) -> p a t m", a=PASSES, t=PACK),
-            gsc_raw[:].rearrange("p (a m t) -> p a t m", a=PASSES, t=PACK),
+            wg_planes[:].rearrange("p (a t m) -> p a t m", a=PASSES, t=PACK),
+            wg_scales_in[:].rearrange("p (a m t) -> p a t m", a=PASSES, t=PACK),
         )
-        vw = [part_words(0, pair0)]
-        wh1_rows = wh[512:1024, :].rearrange("(p j) n -> p j n", j=PACK)
-        wh1 = []
-        for u in range(2):
-            cols = keep.tile([P, PACK, N // 2], F32, name="wh1_%d" % u, tag="wh1_%d" % u, align_bytes=64)
-            nc.sync.dma_start(cols[:], wh1_rows[:, :, u * N // 2 : (u + 1) * N // 2])
-            wh1.append(cols[:])
-        wh0_cols = wh0[:].rearrange("p (j n) -> p j n", j=PACK)
-        wh_raw = ((wh0_cols[:, :, : N // 2], wh0_cols[:, :, N // 2 :]), wh1)
-        negate_bias(0, 1, "nbias0")
-        pair1 = gather_words(1, "slot1")
-        vw.append(part_words(1, pair1))
+        v_codes = [part_words(0, pairs0)]
+        v_codes.append(part_words(1, gather_words(1, "wg_scales_in")))
 
-        cand = keep.tile([P, PACK * J], F32, name="cand", align_bytes=64)
-        kept = keep.tile([P, PACK * J], F32, name="kept", align_bytes=64)
-        grouped = [keep.tile([P, PACK * N], BF16, name="whb%d" % a, tag="slot%d" % (4 + a), align_bytes=64) for a in range(PASSES)]
-        hw = [keep.tile([P, N], U32, name="hw%d" % a, align_bytes=64) for a in range(PASSES)]
-        hs = [keep.tile([P, N], U8, name="hs%d" % a, align_bytes=64) for a in range(PASSES)]
+        s_all = sbuf.tile([P, PACK * J], F32, name="s_all", align_bytes=64)
+        m_all = sbuf.tile([P, PACK * J], F32, name="m_all", align_bytes=64)
+        rs_all = sbuf.tile([P, PACK * J], F32, name="rs_all", align_bytes=64)
+        wh_bf16 = [sbuf.tile([P, PACK * N], BF16, name="wh_bf16_%d" % a, align_bytes=64) for a in range(PASSES)]
+        wh_codes = [sbuf.tile([P, N], U32, name="wh_codes%d" % a, align_bytes=64) for a in range(PASSES)]
+        wh_planes = [sbuf.tile([P, N], U8, name="wh_planes%d" % a, align_bytes=64) for a in range(PASSES)]
 
-        def round_wh(a, u, copy):
-            dst = grouped[a][:].rearrange("p (t m j) -> p m j t", t=PACK, j=PACK)
-            copy(dst[:, 64 * u : 64 * (u + 1)], wh_raw[a][u].rearrange("p j (m t) -> p m j t", t=PACK))
+        def round_wh(a, u, columns, copy):
+            dealt = wh_bf16[a][:].rearrange("p (t m i) -> p m i t", t=PACK, i=PACK)
+            copy(dealt[:, u * P // 2 : (u + 1) * P // 2], columns.rearrange("p i (m t) -> p m i t", t=PACK))
 
         def quantise_wh(a):
-            nc.vector.quantize_mx(out=hw[a][:].bitcast(FP8X4), scales=hs[a][:], in_=grouped[a][:])
+            nc.vector.quantize_mx(out=wh_codes[a][:].bitcast(FP8X4), scales=wh_planes[a][:], in_=wh_bf16[a][:])
+
+        def product(h, codes, planes):
+            acc = psum.tile([P, HALF], F32, name="acc")
+            for a in reversed(range(PASSES)):
+                nc.tensor.matmul_mx(
+                    out=acc[:],
+                    lhsT=codes[a],
+                    lhsT_scale=planes[a],
+                    rhs=v_codes[h][:, 2 * a * HALF : 2 * (a + 1) * HALF].bitcast(FP4X4),
+                    rhs_scale=v_planes[a][:, h * HALF : (h + 1) * HALF],
+                    start=(a == PASSES - 1),
+                    stop=(a == 0),
+                )
+            return acc
 
         def gate(t, h):
-            acc = psum.tile([P, HALF], F32, name="acc")
-            for a in (1, 0):
-                col = a * N + t * P
-                nc.tensor.matmul_mx(
-                    out=acc[:],
-                    lhsT=gw[:, 2 * col : 2 * (col + P)].bitcast(FP4X4),
-                    lhsT_scale=gsc[:, col : col + P],
-                    rhs=vw[h][:, 2 * a * HALF : 2 * (a + 1) * HALF].bitcast(FP4X4),
-                    rhs_scale=vs[a][:, h * HALF : (h + 1) * HALF],
-                    start=(a == 1),
-                    stop=(a == 0),
-                )
+            starts = [a * N + t * P for a in range(PASSES)]
+            acc = product(
+                h,
+                [wg_codes[:, 2 * n0 : 2 * (n0 + P)].bitcast(FP4X4) for n0 in starts],
+                [wg_planes[:, n0 : n0 + P] for n0 in starts],
+            )
             c0 = t * J + h * HALF
-            nc.scalar.activation(carry[:, c0 : c0 + HALF], acc[:], ACT.Sigmoid, bias=nbias[t], scale=-1.0)
+            nc.scalar.activation(s_all[:, c0 : c0 + HALF], acc[:], ACT.Sigmoid, bias=minus_bias[:, t : t + 1], scale=-1.0)
 
         def candidate(t, h):
-            acc = psum.tile([P, HALF], F32, name="acc")
-            for a in (1, 0):
-                nc.tensor.matmul_mx(
-                    out=acc[:],
-                    lhsT=hw[a][:, t * P : (t + 1) * P].bitcast(FP8X4),
-                    lhsT_scale=hs[a][:, t * P : (t + 1) * P],
-                    rhs=vw[h][:, 2 * a * HALF : 2 * (a + 1) * HALF].bitcast(FP4X4),
-                    rhs_scale=vs[a][:, h * HALF : (h + 1) * HALF],
-                    start=(a == 1),
-                    stop=(a == 0),
-                )
-            c0 = t * J + h * HALF
-            nc.scalar.activation(cand[:, c0 : c0 + HALF], acc[:], ACT.Tanh, scale=-1.0)
-
-        def gather_carry(rows, t, j0, width):
-            c0 = t * J + j0
-            nc.vector.tensor_tensor(
-                kept[:, c0 : c0 + width],
-                rows[:].indirect(offsets[:, j0 // 16 : (j0 + width) // 16]),
-                carry[:, c0 : c0 + width],
-                ALU.mult,
+            acc = product(
+                h,
+                [wh_codes[a][:, t * P : (t + 1) * P].bitcast(FP8X4) for a in range(PASSES)],
+                [wh_planes[a][:, t * P : (t + 1) * P] for a in range(PASSES)],
             )
+            c0 = t * J + h * HALF
+            nc.scalar.activation(m_all[:, c0 : c0 + HALF], acc[:], ACT.Tanh, scale=-1.0)
 
-        round_wh(0, 0, nc.scalar.copy)
-        gate(0, 0)
-        round_wh(0, 1, nc.scalar.copy)
-        r1 = load_r(1, "r1")
-        gate(0, 1)
+        def gather_r(t, j0, width):
+            cols = slice(t * J + j0, t * J + j0 + width)
+            nc.vector.tensor_tensor(rs_all[:, cols], r_slices[t][:].indirect(list_part(j0, width)), s_all[:, cols], ALU.mult)
+
+        round_wh(0, 0, wh_first[:, :, : N // 2], nc.scalar.copy)
+        round_wh(0, 1, wh_first[:, :, N // 2 :], nc.scalar.copy)
+        round_wh(1, 0, wh_second[0][:], nc.scalar.copy)
         quantise_wh(0)
-        r2 = load_r(2, "r2")
-        for h in range(HALVES):
-            gather_carry(r0, 0, h * HALF, HALF)
-        r3 = load_r(3, "r3")
-        round_wh(1, 0, nc.scalar.copy)
-        negate_bias(1, PACK, "wh1_0")
-        round_wh(1, 1, nc.vector.tensor_copy)
+        round_wh(1, 1, wh_second[1][:], nc.vector.tensor_copy)
         quantise_wh(1)
-        for t in range(1, PACK):
+        for t in range(PACK):
             for h in range(HALVES):
                 gate(t, h)
-        gather_carry(r1, 1, 0, J)
-        for h in range(HALVES):
-            for t in range(PACK):
+        for t in range(PACK):
+            for h in range(HALVES):
                 candidate(t, h)
-        gather_carry(r2, 2, 0, J)
+        for h in range(HALVES):
+            gather_r(0, h * HALF, HALF)
+        gather_r(1, 0, J)
 
+        s_t = s_all[:].rearrange("p (t j) -> p t j", t=PACK)
+        m_t = m_all[:].rearrange("p (t j) -> p t j", t=PACK)
+        rs_t = rs_all[:].rearrange("p (t j) -> p t j", t=PACK)
         y_rows = out_0.rearrange("(p t) j -> p t j", t=PACK)
         y_words = out_1[0].rearrange("p j i -> p (j i)").bitcast(I32)
-        y_scales = keep.tile([P, J], U8, name="y_scales", align_bytes=64)
-        carry_t = carry[:].rearrange("p (t j) -> p t j", t=PACK)
-        cand_t = cand[:].rearrange("p (t j) -> p t j", t=PACK)
-        kept_t = kept[:].rearrange("p (t j) -> p t j", t=PACK)
+        y_plane = sbuf.tile([P, J], U8, name="y_plane", align_bytes=64)
+        y = [sbuf.tile([P, PACK, CHUNK], F32, name="y%d" % c, align_bytes=64) for c in range(CHUNKS)]
+        y_bf16 = [sbuf.tile([P, PACK * CHUNK], BF16, name="y_bf16_%d" % c, align_bytes=64) for c in range(CHUNKS)]
 
-        def quantise(c0, width, rounded):
-            y_codes = keep.tile([P, width], I32, name="y_codes%d" % c0, align_bytes=64)
-            nc.vector.quantize_mx(out=y_codes[:].bitcast(FP8X4), scales=y_scales[:, c0 : c0 + width], in_=rounded[:])
-            nc.sync.dma_start(y_words[:, c0 : c0 + width], y_codes[:])
+        def chunk_cols(c):
+            return slice(c * CHUNK, (c + 1) * CHUNK)
 
-        gated = {}
-        rounded = {}
+        def multiply(dst, slices, cols):
+            nc.vector.scalar_tensor_tensor(dst, s_t[:, slices, cols], 1.0, m_t[:, slices, cols], ALU.subtract, ALU.mult)
 
-        def gate_candidate(c):
-            c0, width = CHUNKS[c]
-            cols = slice(c0, c0 + width)
-            gated[c] = keep.tile([P, PACK, width], F32, name="gated%d" % c0)
-            nc.vector.scalar_tensor_tensor(gated[c][:], carry_t[:, :, cols], 1.0, cand_t[:, :, cols], ALU.subtract, ALU.mult)
+        gated_early = sbuf.tile([P, EARLY, J], F32, name="gated_early", align_bytes=64)
+        for t in range(EARLY):
+            multiply(gated_early[:, t : t + 1, :], slice(t, t + 1), slice(0, J))
+        turn_blocks = [(t, b) for t in range(EARLY) for b in range(CHUNK // P)]
 
-        def combine(c):
-            c0, width = CHUNKS[c]
-            cols = slice(c0, c0 + width)
-            t0 = PE_SLICES if c < PE_CHUNKS else 0
-            nc.vector.tensor_tensor(y[c][:, t0:, :], kept_t[:, t0:, cols], gated[c][:, t0:, :], ALU.add)
-            nc.sync.dma_start(y_rows[:, :, cols], y[c][:])
-
-        def add_turned(c, b):
-            j0 = CHUNKS[c][0] + b * P
+        def add_turned(c):
             acc = psum.tile([P, HALF], F32, name="acc")
-            for t in range(PE_SLICES):
-                block = acc[:, t * P : (t + 1) * P]
-                nc.tensor.matmul(block, gated[c][:, t, b * P : (b + 1) * P], ident[:], is_transpose=True, start=True, stop=False)
-                nc.tensor.matmul(block, kept_t[:, t, j0 : j0 + P], ident[:], is_transpose=True, start=False, stop=True)
-            turned = keep.tile([P, PE_SLICES * P], F32, name="turned%d" % j0, align_bytes=64)
-            nc.scalar.copy(turned[:], acc[:, : PE_SLICES * P])
+            for place, (t, b) in enumerate(turn_blocks):
+                block = acc[:, place * P : (place + 1) * P]
+                cols = slice(c * CHUNK + b * P, c * CHUNK + (b + 1) * P)
+                nc.tensor.matmul(block, gated_early[:, t, cols], ident[:], is_transpose=True, start=True, stop=False)
+                nc.tensor.matmul(block, rs_t[:, t, cols], ident[:], is_transpose=True, start=False, stop=True)
+            turned = sbuf.tile([P, HALF], F32, name="turned%d" % c, align_bytes=64)
+            nc.scalar.copy(turned[:], acc[:])
             return turned
 
-        def turn_back(c, b, turned):
+        def turn_back(c, turned):
             acc = psum.tile([P, HALF], F32, name="acc")
-            for t in range(PE_SLICES):
-                nc.tensor.transpose(acc[:, t * P : (t + 1) * P], turned[:, t * P : (t + 1) * P], ident[:])
-            nc.scalar.copy(
-                y[c][:, :PE_SLICES, b * P : (b + 1) * P], acc[:, : PE_SLICES * P].rearrange("p (t j) -> p t j", t=PE_SLICES)
-            )
+            for place in range(len(turn_blocks)):
+                nc.tensor.transpose(acc[:, place * P : (place + 1) * P], turned[:, place * P : (place + 1) * P], ident[:])
+            nc.scalar.copy(y[c][:, :EARLY, :], acc[:].rearrange("p (t j) -> p t j", t=EARLY))
+            nc.scalar.dma_start(y_rows[:, :EARLY, chunk_cols(c)], y[c][:, :EARLY, :])
 
-        def round_y(c, y, copy):
-            c0, width = CHUNKS[c]
-            rounded[c] = keep.tile([P, PACK * width], BF16, name="rounded%d" % c0, align_bytes=64)
-            copy(rounded[c][:].rearrange("p (c i t) -> p c t i", t=PACK, i=4), y[:].rearrange("p t (c i) -> p c t i", i=4))
+        turned_sums = [add_turned(c) for c in range(CHUNKS)]
+        for c in range(CHUNKS):
+            turn_back(c, turned_sums[c])
 
-        y = [keep.tile([P, PACK, width], F32, name="y%d" % c0) for c0, width in CHUNKS]
-        last = len(CHUNKS) - 1
-        blocks = [(c, b) for c in range(PE_CHUNKS) for b in range(CHUNKS[c][1] // P)]
-        for c in range(PE_CHUNKS):
-            gate_candidate(c)
-        waiting = None
-        for c, b in blocks:
-            turned = add_turned(c, b)
-            if waiting is not None:
-                turn_back(*waiting)
-            waiting = (c, b, turned)
-        turn_back(*waiting)
+        late = slice(EARLY, PACK)
+        gather_r(PACK - 2, 0, J)
+
+        def add_late(c, gated):
+            nc.vector.tensor_tensor(y[c][:, late, :], rs_t[:, late, chunk_cols(c)], gated, ALU.add)
+            nc.sync.dma_start(y_rows[:, late, chunk_cols(c)], y[c][:, late, :])
+
+        def round_y(c):
+            copy = nc.vector.tensor_copy if c == CHUNKS - 1 else nc.scalar.copy
+            copy(y_bf16[c][:].rearrange("p (g i t) -> p g t i", t=PACK, i=4), y[c][:].rearrange("p t (g i) -> p g t i", i=4))
+
+        def quantise_y(c):
+            codes = sbuf.tile([P, CHUNK], I32, name="y_codes%d" % c, align_bytes=64)
+            nc.vector.quantize_mx(out=codes[:].bitcast(FP8X4), scales=y_plane[:, chunk_cols(c)], in_=y_bf16[c][:])
+            nc.sync.dma_start(y_words[:, chunk_cols(c)], codes[:])
+
+        per_half = HALF // CHUNK
         for h in range(HALVES):
-            gather_carry(r3, PACK - 1, h * HALF, HALF)
-        for c in range(len(CHUNKS)):
-            if PE_CHUNKS <= c + 1 <= last:
-                gate_candidate(c + 1)
-            combine(c)
-            if c > 0:
-                quantise(*CHUNKS[c - 1], rounded[c - 1])
-            round_y(c, y[c], nc.vector.tensor_copy if c == last else nc.scalar.copy)
-        quantise(*CHUNKS[last], rounded[last])
-        for q in range(4):
-            eng = nc.sync if q % 2 == 0 else nc.scalar
-            eng.dma_start(out_2[0, 4 * q : 4 * q + 4, :].bitcast(I32), y_scales[32 * q : 32 * q + 4, :].bitcast(I32))
+            gather_r(PACK - 1, h * HALF, HALF)
+            gated_late = sbuf.tile([P, per_half, PACK - EARLY, CHUNK], F32, name="gated_late%d" % h, tag="r%d" % (2 + h), align_bytes=64)
+            for i in range(per_half):
+                multiply(gated_late[:, i], late, chunk_cols(h * per_half + i))
+            for i in range(per_half):
+                c = h * per_half + i
+                add_late(c, gated_late[:, i])
+                if c >= QUANTISE_LAG:
+                    quantise_y(c - QUANTISE_LAG)
+                round_y(c)
+        for c in range(CHUNKS - QUANTISE_LAG, CHUNKS):
+            quantise_y(c)
+
+        for q in range(QUADS):
+            queue = nc.sync if q % 2 == 0 else nc.scalar
+            queue.dma_start(
+                out_2[0, PLANE_ROWS * q : PLANE_ROWS * (q + 1), :].bitcast(I32),
+                y_plane[32 * q : 32 * q + PLANE_ROWS, :].bitcast(I32),
+            )

@@ -39,7 +39,7 @@ def tile_list_hwayt_tanhP_kernel(
     nc = tc.nc
     with ExitStack() as ctx:
         sbuf = ctx.enter_context(tc.tile_pool(name="sbuf", bufs=1))
-        psum = ctx.enter_context(tc.psum_pool(name="psum", bufs=8))
+        psum = ctx.enter_context(tc.psum_pool(name="psum", bufs=1))
 
         def list_part(j0, width):
             return offsets[:, j0 // GROUP : (j0 + width) // GROUP]
@@ -71,7 +71,7 @@ def tile_list_hwayt_tanhP_kernel(
         wh_rows = wh.rearrange("(a p i) n -> a p i n", p=P, i=PACK)
         wh_first = sbuf.tile([P, PACK, N], F32, name="wh_first", align_bytes=64)
         nc.sync.dma_start(wh_first[:], wh_rows[0])
-        wh_second = [sbuf.tile([P, PACK, N // 2], F32, name="wh_second%d" % u, align_bytes=64) for u in range(2)]
+        wh_second = [sbuf.tile([P, PACK, N // 2], F32, name="wh_second%d" % u, tag="wh_second%d" % u, align_bytes=64) for u in range(2)]
         nc.sync.dma_start(wh_second[0][:], wh_rows[1][:, :, : N // 2])
 
         ident = sbuf.tile([P, P], F32, name="ident", align_bytes=64)
@@ -99,29 +99,21 @@ def tile_list_hwayt_tanhP_kernel(
         for t in range(PACK):
             nc.sync.dma_start(r_slices[t][:], r_rows[t])
 
-        def gather_words(h, tag):
-            pairs = sbuf.tile([P, HALF], U32, name="pairs%d" % h, tag=tag, align_bytes=64)
-            nc.vector.tensor_copy(pairs[:], table_words[:].bitcast(U32).indirect(list_part(h * HALF, HALF)))
-            return pairs
-
-        def part_words(h, pairs):
-            parted = sbuf.tile([P, PASSES * HALF * 2], U8, name="v_codes%d" % h, align_bytes=64)
-            nc.vector.tensor_copy(
-                parted[:].bitcast(U16).rearrange("p (a j) -> p a j", a=PASSES),
-                pairs[:].bitcast(U16).rearrange("p (j a) -> p a j", a=PASSES),
-            )
-            return parted
-
-        pairs0 = gather_words(0, "pairs0")
+        pairs = sbuf.tile([P, J], U32, name="pairs", align_bytes=64)
+        nc.vector.tensor_copy(pairs[:], table_words[:].bitcast(U32).indirect(offsets[:]))
         wg_planes = sbuf.tile([P, PASSES * N], U8, name="wg_planes", align_bytes=64)
         nc.vector.tensor_copy(
             wg_planes[:].rearrange("p (a t m) -> p a t m", a=PASSES, t=PACK),
             wg_scales_in[:].rearrange("p (a m t) -> p a t m", a=PASSES, t=PACK),
         )
-        v_codes = [part_words(0, pairs0)]
-        v_codes.append(part_words(1, gather_words(1, "wg_scales_in")))
+        parted = sbuf.tile([P, HALVES, PASSES * HALF * 2], U8, name="parted", tag="wg_scales_in", align_bytes=64)
+        v_codes = [parted[:, h, :] for h in range(HALVES)]
+        for h in range(HALVES):
+            nc.vector.tensor_copy(
+                v_codes[h].bitcast(U16).rearrange("p (a j) -> p a j", a=PASSES),
+                pairs[:, h * HALF : (h + 1) * HALF].bitcast(U16).rearrange("p (j a) -> p a j", a=PASSES),
+            )
 
-        s_all = sbuf.tile([P, PACK * J], F32, name="s_all", align_bytes=64)
         m_all = sbuf.tile([P, PACK * J], F32, name="m_all", align_bytes=64)
         rs_all = sbuf.tile([P, PACK * J], F32, name="rs_all", align_bytes=64)
         wh_bf16 = [sbuf.tile([P, PACK * N], BF16, name="wh_bf16_%d" % a, align_bytes=64) for a in range(PASSES)]
@@ -135,8 +127,12 @@ def tile_list_hwayt_tanhP_kernel(
         def quantise_wh(a):
             nc.vector.quantize_mx(out=wh_codes[a][:].bitcast(FP8X4), scales=wh_planes[a][:], in_=wh_bf16[a][:])
 
-        def product(h, codes, planes):
-            acc = psum.tile([P, HALF], F32, name="acc")
+        def bank(pair, h):
+            b = HALVES * pair + h
+            return psum.tile([P, HALF], F32, name="bank%d" % b, tag="bank%d" % b)
+
+        def product(h, pair, codes, planes):
+            acc = bank(pair, h)
             for a in reversed(range(PASSES)):
                 nc.tensor.matmul_mx(
                     out=acc[:],
@@ -153,6 +149,7 @@ def tile_list_hwayt_tanhP_kernel(
             starts = [a * N + t * P for a in range(PASSES)]
             acc = product(
                 h,
+                t,
                 [wg_codes[:, 2 * n0 : 2 * (n0 + P)].bitcast(FP4X4) for n0 in starts],
                 [wg_planes[:, n0 : n0 + P] for n0 in starts],
             )
@@ -162,6 +159,7 @@ def tile_list_hwayt_tanhP_kernel(
         def candidate(t, h):
             acc = product(
                 h,
+                (t + EARLY) % PACK,
                 [wh_codes[a][:, t * P : (t + 1) * P].bitcast(FP8X4) for a in range(PASSES)],
                 [wh_planes[a][:, t * P : (t + 1) * P] for a in range(PASSES)],
             )
@@ -178,15 +176,12 @@ def tile_list_hwayt_tanhP_kernel(
         quantise_wh(0)
         round_wh(1, 1, wh_second[1][:], nc.vector.tensor_copy)
         quantise_wh(1)
-        for t in range(PACK):
-            for h in range(HALVES):
-                gate(t, h)
-        for t in range(PACK):
-            for h in range(HALVES):
-                candidate(t, h)
-        for h in range(HALVES):
-            gather_r(0, h * HALF, HALF)
-        gather_r(1, 0, J)
+        s_all = sbuf.tile([P, PACK * J], F32, name="s_all", tag="wh_second0", align_bytes=64)
+        for first in (0, EARLY):
+            for stage in (gate, candidate):
+                for t in range(first, first + EARLY):
+                    for h in range(HALVES):
+                        stage(t, h)
 
         s_t = s_all[:].rearrange("p (t j) -> p t j", t=PACK)
         m_t = m_all[:].rearrange("p (t j) -> p t j", t=PACK)
@@ -194,7 +189,7 @@ def tile_list_hwayt_tanhP_kernel(
         y_rows = out_0.rearrange("(p t) j -> p t j", t=PACK)
         y_words = out_1[0].rearrange("p j i -> p (j i)").bitcast(I32)
         y_plane = sbuf.tile([P, J], U8, name="y_plane", align_bytes=64)
-        y = [sbuf.tile([P, PACK, CHUNK], F32, name="y%d" % c, align_bytes=64) for c in range(CHUNKS)]
+        y = [sbuf.tile([P, PACK, HALF], F32, name="y%d" % h, align_bytes=64) for h in range(HALVES)]
         y_bf16 = [sbuf.tile([P, PACK * CHUNK], BF16, name="y_bf16_%d" % c, align_bytes=64) for c in range(CHUNKS)]
 
         def chunk_cols(c):
@@ -203,50 +198,55 @@ def tile_list_hwayt_tanhP_kernel(
         def multiply(dst, slices, cols):
             nc.vector.scalar_tensor_tensor(dst, s_t[:, slices, cols], 1.0, m_t[:, slices, cols], ALU.subtract, ALU.mult)
 
+        per_half = HALF // CHUNK
+
+        def y_chunk(c):
+            return y[c // per_half][:, :, (c % per_half) * CHUNK : (c % per_half + 1) * CHUNK]
+
         gated_early = sbuf.tile([P, EARLY, J], F32, name="gated_early", align_bytes=64)
         for t in range(EARLY):
+            gather_r(t, 0, J)
             multiply(gated_early[:, t : t + 1, :], slice(t, t + 1), slice(0, J))
-        turn_blocks = [(t, b) for t in range(EARLY) for b in range(CHUNK // P)]
 
-        def add_turned(c):
-            acc = psum.tile([P, HALF], F32, name="acc")
-            for place, (t, b) in enumerate(turn_blocks):
-                block = acc[:, place * P : (place + 1) * P]
-                cols = slice(c * CHUNK + b * P, c * CHUNK + (b + 1) * P)
-                nc.tensor.matmul(block, gated_early[:, t, cols], ident[:], is_transpose=True, start=True, stop=False)
-                nc.tensor.matmul(block, rs_t[:, t, cols], ident[:], is_transpose=True, start=False, stop=True)
-            turned = sbuf.tile([P, HALF], F32, name="turned%d" % c, align_bytes=64)
+        def add_turned(t, h):
+            acc = bank(EARLY + t, h)
+            for n, term in enumerate((rs_t, gated_early)):
+                for b in range(HALF // P):
+                    cols = slice(h * HALF + b * P, h * HALF + (b + 1) * P)
+                    first, final = (n, b) == (0, 0), (n, b) == (1, HALF // P - 1)
+                    nc.tensor.matmul(acc[:, b * P : (b + 1) * P], term[:, t, cols], ident[:], is_transpose=True, start=first, stop=final)
+            turned = sbuf.tile([P, HALF], F32, name="turned%d_%d" % (t, h), align_bytes=64)
             nc.scalar.copy(turned[:], acc[:])
             return turned
 
-        def turn_back(c, turned):
-            acc = psum.tile([P, HALF], F32, name="acc")
-            for place in range(len(turn_blocks)):
-                nc.tensor.transpose(acc[:, place * P : (place + 1) * P], turned[:, place * P : (place + 1) * P], ident[:])
-            nc.scalar.copy(y[c][:, :EARLY, :], acc[:].rearrange("p (t j) -> p t j", t=EARLY))
-            nc.scalar.dma_start(y_rows[:, :EARLY, chunk_cols(c)], y[c][:, :EARLY, :])
+        def turn_back(t, h, turned):
+            acc = bank(EARLY + t, h)
+            for b in range(HALF // P):
+                nc.tensor.transpose(acc[:, b * P : (b + 1) * P], turned[:, b * P : (b + 1) * P], ident[:])
+            nc.scalar.copy(y[h][:, t, :], acc[:])
 
-        turned_sums = [add_turned(c) for c in range(CHUNKS)]
-        for c in range(CHUNKS):
-            turn_back(c, turned_sums[c])
+        turned_sums = {(t, h): add_turned(t, h) for t in range(EARLY) for h in range(HALVES)}
+        for h in range(HALVES):
+            for t in range(EARLY):
+                turn_back(t, h, turned_sums[t, h])
+            nc.scalar.dma_start(y_rows[:, :EARLY, h * HALF : (h + 1) * HALF], y[h][:, :EARLY, :])
 
         late = slice(EARLY, PACK)
         gather_r(PACK - 2, 0, J)
 
         def add_late(c, gated):
-            nc.vector.tensor_tensor(y[c][:, late, :], rs_t[:, late, chunk_cols(c)], gated, ALU.add)
-            nc.sync.dma_start(y_rows[:, late, chunk_cols(c)], y[c][:, late, :])
+            nc.vector.tensor_tensor(y_chunk(c)[:, late, :], rs_t[:, late, chunk_cols(c)], gated, ALU.add)
+            nc.sync.dma_start(y_rows[:, late, chunk_cols(c)], y_chunk(c)[:, late, :])
 
         def round_y(c):
             copy = nc.vector.tensor_copy if c == CHUNKS - 1 else nc.scalar.copy
-            copy(y_bf16[c][:].rearrange("p (g i t) -> p g t i", t=PACK, i=4), y[c][:].rearrange("p t (g i) -> p g t i", i=4))
+            copy(y_bf16[c][:].rearrange("p (g i t) -> p g t i", t=PACK, i=4), y_chunk(c).rearrange("p t (g i) -> p g t i", i=4))
 
         def quantise_y(c):
             codes = sbuf.tile([P, CHUNK], I32, name="y_codes%d" % c, align_bytes=64)
             nc.vector.quantize_mx(out=codes[:].bitcast(FP8X4), scales=y_plane[:, chunk_cols(c)], in_=y_bf16[c][:])
             nc.sync.dma_start(y_words[:, chunk_cols(c)], codes[:])
 
-        per_half = HALF // CHUNK
         for h in range(HALVES):
             gather_r(PACK - 1, h * HALF, HALF)
             gated_late = sbuf.tile([P, per_half, PACK - EARLY, CHUNK], F32, name="gated_late%d" % h, tag="r%d" % (2 + h), align_bytes=64)
@@ -257,7 +257,8 @@ def tile_list_hwayt_tanhP_kernel(
                 add_late(c, gated_late[:, i])
                 if c >= QUANTISE_LAG:
                     quantise_y(c - QUANTISE_LAG)
-                round_y(c)
+            for i in range(per_half):
+                round_y(h * per_half + i)
         for c in range(CHUNKS - QUANTISE_LAG, CHUNKS):
             quantise_y(c)
 

@@ -74,11 +74,11 @@ def tile_list_hwayt_tanhP_kernel(
         wh_second = [sbuf.tile([P, PACK, N // 2], F32, name="wh_second%d" % u, tag="wh_second%d" % u, align_bytes=64) for u in range(2)]
         nc.sync.dma_start(wh_second[0][:], wh_rows[1][:, :, : N // 2])
 
-        ident = sbuf.tile([P, P], F32, name="ident", align_bytes=64)
-        make_identity(nc, ident[:])
-        warm = sbuf.tile([P, 1], F32, name="warm")
+        warm = sbuf.tile([P, 1], F32, name="warm", tag="warm", align_bytes=64)
         nc.vector.memset(warm[:], 0.0)
         nc.scalar.activation(warm[:], warm[:], ACT.Sigmoid)
+        ident = sbuf.tile([P, P], F32, name="ident", tag="warm", align_bytes=64)
+        make_identity(nc, ident[:])
         minus_bias = sbuf.tile([P, PACK], F32, name="minus_bias")
         nc.scalar.mul(minus_bias[:], bias[:], -1.0)
 
@@ -247,18 +247,21 @@ def tile_list_hwayt_tanhP_kernel(
             nc.vector.quantize_mx(out=codes[:].bitcast(FP8X4), scales=y_plane[:, chunk_cols(c)], in_=y_bf16[c][:])
             nc.sync.dma_start(y_words[:, chunk_cols(c)], codes[:])
 
-        for h in range(HALVES):
-            gather_r(PACK - 1, h * HALF, HALF)
-            gated_late = sbuf.tile([P, per_half, PACK - EARLY, CHUNK], F32, name="gated_late%d" % h, tag="r%d" % (2 + h), align_bytes=64)
-            for i in range(per_half):
-                multiply(gated_late[:, i], late, chunk_cols(h * per_half + i))
-            for i in range(per_half):
-                c = h * per_half + i
-                add_late(c, gated_late[:, i])
-                if c >= QUANTISE_LAG:
-                    quantise_y(c - QUANTISE_LAG)
-            for i in range(per_half):
-                round_y(h * per_half + i)
+        gated_first = sbuf.tile([P, PACK - EARLY, HALF], F32, name="gated_first", align_bytes=64)
+        multiply(gated_first[:], late, slice(0, HALF))
+        gather_r(PACK - 1, 0, J)
+        for c in range(per_half):
+            add_late(c, gated_first[:, :, chunk_cols(c)])
+        for c in range(per_half):
+            round_y(c)
+        gated_second = sbuf.tile([P, per_half, PACK - EARLY, CHUNK], F32, name="gated_second", tag="r3", align_bytes=64)
+        for i in range(per_half):
+            multiply(gated_second[:, i], late, chunk_cols(per_half + i))
+        for i in range(per_half):
+            add_late(per_half + i, gated_second[:, i])
+            quantise_y(i)
+        for c in range(per_half, CHUNKS):
+            round_y(c)
         for c in range(CHUNKS - QUANTISE_LAG, CHUNKS):
             quantise_y(c)
 

@@ -23,13 +23,13 @@ K_PASS = P * PACK
 PASSES = K // K_PASS
 QUADS = 4
 PLANE_ROWS = 4
-GROUP = 16
 HALF = 512
 HALVES = J // HALF
 SHIFT = 16
 EARLY = 2
-CHUNK = HALF // EARLY
+CHUNK = 256
 CHUNKS = J // CHUNK
+PER_HALF = HALF // CHUNK
 QUANTISE_LAG = 2
 
 
@@ -41,9 +41,6 @@ def tile_list_hwayt_tanhP_kernel(
         sbuf = ctx.enter_context(tc.tile_pool(name="sbuf", bufs=1))
         psum = ctx.enter_context(tc.psum_pool(name="psum", bufs=1))
 
-        def list_part(j0, width):
-            return offsets[:, j0 // GROUP : (j0 + width) // GROUP]
-
         table_scales = sbuf.tile([P, T], U8, name="table_scales", align_bytes=64)
         nc.vector.memset(table_scales[:].bitcast(I32), 0)
         wg_scales_in = sbuf.tile([P, PASSES * N], U8, name="wg_scales_in", tag="wg_scales_in", align_bytes=64)
@@ -51,7 +48,7 @@ def tile_list_hwayt_tanhP_kernel(
         v_plane1 = sbuf.tile([P, J], U8, name="v_plane1", align_bytes=64)
         nc.vector.memset(v_plane1[:].bitcast(I32), 0)
 
-        offsets = sbuf.tile([P, J // GROUP], U16, name="offsets")
+        offsets = sbuf.tile(list(offs.shape), U16, name="offsets")
         nc.sync.dma_start(offsets[:], offs)
         table_scale_rows = tab_scales.bitcast(I32).rearrange("a (q r) c -> r q a c", r=PLANE_ROWS)
         for r in range(PLANE_ROWS):
@@ -71,7 +68,9 @@ def tile_list_hwayt_tanhP_kernel(
         wh_rows = wh.rearrange("(a p i) n -> a p i n", p=P, i=PACK)
         wh_first = sbuf.tile([P, PACK, N], F32, name="wh_first", align_bytes=64)
         nc.sync.dma_start(wh_first[:], wh_rows[0])
-        wh_second = [sbuf.tile([P, PACK, N // 2], F32, name="wh_second%d" % u, tag="wh_second%d" % u, align_bytes=64) for u in range(2)]
+        wh_second = [
+            sbuf.tile([P, PACK, N // 2], F32, name="wh_second%d" % u, tag="wh_second%d" % u, align_bytes=64) for u in range(2)
+        ]
         nc.sync.dma_start(wh_second[0][:], wh_rows[1][:, :, : N // 2])
 
         warm = sbuf.tile([P, 1], F32, name="warm", tag="warm", align_bytes=64)
@@ -95,7 +94,7 @@ def tile_list_hwayt_tanhP_kernel(
 
         nc.sync.dma_start(wh_second[1][:], wh_rows[1][:, :, N // 2 :])
         r_rows = rT.rearrange("(p t) c -> t p c", t=PACK)
-        r_slices = [sbuf.tile([P, T], F32, name="r%d" % t, tag="r%d" % t, align_bytes=64) for t in range(PACK)]
+        r_slices = [sbuf.tile([P, T], F32, name="r%d" % t, align_bytes=64) for t in range(PACK)]
         for t in range(PACK):
             nc.sync.dma_start(r_slices[t][:], r_rows[t])
 
@@ -114,8 +113,8 @@ def tile_list_hwayt_tanhP_kernel(
                 pairs[:, h * HALF : (h + 1) * HALF].bitcast(U16).rearrange("p (j a) -> p a j", a=PASSES),
             )
 
-        m_all = sbuf.tile([P, PACK * J], F32, name="m_all", align_bytes=64)
-        rs_all = sbuf.tile([P, PACK * J], F32, name="rs_all", align_bytes=64)
+        m_all = sbuf.tile([P, PACK, J], F32, name="m_all", align_bytes=64)
+        rs_all = sbuf.tile([P, PACK, J], F32, name="rs_all", align_bytes=64)
         wh_bf16 = [sbuf.tile([P, PACK * N], BF16, name="wh_bf16_%d" % a, align_bytes=64) for a in range(PASSES)]
         wh_codes = [sbuf.tile([P, N], U32, name="wh_codes%d" % a, align_bytes=64) for a in range(PASSES)]
         wh_planes = [sbuf.tile([P, N], U8, name="wh_planes%d" % a, align_bytes=64) for a in range(PASSES)]
@@ -126,6 +125,9 @@ def tile_list_hwayt_tanhP_kernel(
 
         def quantise_wh(a):
             nc.vector.quantize_mx(out=wh_codes[a][:].bitcast(FP8X4), scales=wh_planes[a][:], in_=wh_bf16[a][:])
+
+        def half_cols(h):
+            return slice(h * HALF, (h + 1) * HALF)
 
         def bank(pair, h):
             b = HALVES * pair + h
@@ -139,7 +141,7 @@ def tile_list_hwayt_tanhP_kernel(
                     lhsT=codes[a],
                     lhsT_scale=planes[a],
                     rhs=v_codes[h][:, 2 * a * HALF : 2 * (a + 1) * HALF].bitcast(FP4X4),
-                    rhs_scale=v_planes[a][:, h * HALF : (h + 1) * HALF],
+                    rhs_scale=v_planes[a][:, half_cols(h)],
                     start=(a == PASSES - 1),
                     stop=(a == 0),
                 )
@@ -153,8 +155,7 @@ def tile_list_hwayt_tanhP_kernel(
                 [wg_codes[:, 2 * n0 : 2 * (n0 + P)].bitcast(FP4X4) for n0 in starts],
                 [wg_planes[:, n0 : n0 + P] for n0 in starts],
             )
-            c0 = t * J + h * HALF
-            nc.scalar.activation(s_all[:, c0 : c0 + HALF], acc[:], ACT.Sigmoid, bias=minus_bias[:, t : t + 1], scale=-1.0)
+            nc.scalar.activation(s_all[:, t, half_cols(h)], acc[:], ACT.Sigmoid, bias=minus_bias[:, t : t + 1], scale=-1.0)
 
         def candidate(t, h):
             acc = product(
@@ -163,12 +164,10 @@ def tile_list_hwayt_tanhP_kernel(
                 [wh_codes[a][:, t * P : (t + 1) * P].bitcast(FP8X4) for a in range(PASSES)],
                 [wh_planes[a][:, t * P : (t + 1) * P] for a in range(PASSES)],
             )
-            c0 = t * J + h * HALF
-            nc.scalar.activation(m_all[:, c0 : c0 + HALF], acc[:], ACT.Tanh, scale=-1.0)
+            nc.scalar.activation(m_all[:, t, half_cols(h)], acc[:], ACT.Tanh, scale=-1.0)
 
-        def gather_r(t, j0, width):
-            cols = slice(t * J + j0, t * J + j0 + width)
-            nc.vector.tensor_tensor(rs_all[:, cols], r_slices[t][:].indirect(list_part(j0, width)), s_all[:, cols], ALU.mult)
+        def gather_r(t):
+            nc.vector.tensor_tensor(rs_all[:, t, :], r_slices[t][:].indirect(offsets[:]), s_all[:, t, :], ALU.mult)
 
         round_wh(0, 0, wh_first[:, :, : N // 2], nc.scalar.copy)
         round_wh(0, 1, wh_first[:, :, N // 2 :], nc.scalar.copy)
@@ -176,46 +175,45 @@ def tile_list_hwayt_tanhP_kernel(
         quantise_wh(0)
         round_wh(1, 1, wh_second[1][:], nc.vector.tensor_copy)
         quantise_wh(1)
-        s_all = sbuf.tile([P, PACK * J], F32, name="s_all", tag="wh_second0", align_bytes=64)
+        s_all = sbuf.tile([P, PACK, J], F32, name="s_all", tag="wh_second0", align_bytes=64)
         for first in (0, EARLY):
             for stage in (gate, candidate):
                 for t in range(first, first + EARLY):
                     for h in range(HALVES):
                         stage(t, h)
 
-        s_t = s_all[:].rearrange("p (t j) -> p t j", t=PACK)
-        m_t = m_all[:].rearrange("p (t j) -> p t j", t=PACK)
-        rs_t = rs_all[:].rearrange("p (t j) -> p t j", t=PACK)
         y_rows = out_0.rearrange("(p t) j -> p t j", t=PACK)
         y_words = out_1[0].rearrange("p j i -> p (j i)").bitcast(I32)
         y_plane = sbuf.tile([P, J], U8, name="y_plane", align_bytes=64)
         y = [sbuf.tile([P, PACK, HALF], F32, name="y%d" % h, align_bytes=64) for h in range(HALVES)]
-        y_bf16 = [sbuf.tile([P, PACK * CHUNK], BF16, name="y_bf16_%d" % c, align_bytes=64) for c in range(CHUNKS)]
+        y_codes = sbuf.tile([P, J], I32, name="y_codes", align_bytes=64)
+        y_bf16 = [
+            sbuf.tile([P, PACK * CHUNK], BF16, name="y_bf16_%d" % c, tag="y_bf16_%d" % (c % (CHUNKS - 1)), align_bytes=64)
+            for c in range(CHUNKS)
+        ]
 
         def chunk_cols(c):
             return slice(c * CHUNK, (c + 1) * CHUNK)
 
         def multiply(dst, slices, cols):
-            nc.vector.scalar_tensor_tensor(dst, s_t[:, slices, cols], 1.0, m_t[:, slices, cols], ALU.subtract, ALU.mult)
-
-        per_half = HALF // CHUNK
+            nc.vector.scalar_tensor_tensor(dst, s_all[:, slices, cols], 1.0, m_all[:, slices, cols], ALU.subtract, ALU.mult)
 
         def y_chunk(c):
-            return y[c // per_half][:, :, (c % per_half) * CHUNK : (c % per_half + 1) * CHUNK]
+            return y[c // PER_HALF][:, :, (c % PER_HALF) * CHUNK : (c % PER_HALF + 1) * CHUNK]
 
         gated_early = sbuf.tile([P, EARLY, J], F32, name="gated_early", align_bytes=64)
         for t in range(EARLY):
-            gather_r(t, 0, J)
+            gather_r(t)
             multiply(gated_early[:, t : t + 1, :], slice(t, t + 1), slice(0, J))
 
         def add_turned(t, h):
             acc = bank(EARLY + t, h)
-            for n, term in enumerate((rs_t, gated_early)):
+            for n, term in enumerate((rs_all, gated_early)):
                 for b in range(HALF // P):
                     cols = slice(h * HALF + b * P, h * HALF + (b + 1) * P)
                     first, final = (n, b) == (0, 0), (n, b) == (1, HALF // P - 1)
                     nc.tensor.matmul(acc[:, b * P : (b + 1) * P], term[:, t, cols], ident[:], is_transpose=True, start=first, stop=final)
-            turned = sbuf.tile([P, HALF], F32, name="turned%d_%d" % (t, h), align_bytes=64)
+            turned = sbuf.tile([P, HALF], F32, name="turned%d_%d" % (t, h), tag="turned%d_%d" % (t, h), align_bytes=64)
             nc.scalar.copy(turned[:], acc[:])
             return turned
 
@@ -229,39 +227,46 @@ def tile_list_hwayt_tanhP_kernel(
         for h in range(HALVES):
             for t in range(EARLY):
                 turn_back(t, h, turned_sums[t, h])
-            nc.scalar.dma_start(y_rows[:, :EARLY, h * HALF : (h + 1) * HALF], y[h][:, :EARLY, :])
+            nc.scalar.dma_start(y_rows[:, :EARLY, half_cols(h)], y[h][:, :EARLY, :])
 
         late = slice(EARLY, PACK)
-        gather_r(PACK - 2, 0, J)
+        for t in range(EARLY, PACK):
+            gather_r(t)
+
+        def stored_with(c):
+            if c >= PER_HALF:
+                return chunk_cols(c)
+            return half_cols(0) if c == PER_HALF - 1 else None
 
         def add_late(c, gated):
-            nc.vector.tensor_tensor(y_chunk(c)[:, late, :], rs_t[:, late, chunk_cols(c)], gated, ALU.add)
-            nc.sync.dma_start(y_rows[:, late, chunk_cols(c)], y_chunk(c)[:, late, :])
+            nc.vector.tensor_tensor(y_chunk(c)[:, late, :], rs_all[:, late, chunk_cols(c)], gated, ALU.add)
+            cols = stored_with(c)
+            if cols:
+                h = c // PER_HALF
+                nc.sync.dma_start(y_rows[:, late, cols], y[h][:, late, cols.start - h * HALF : cols.stop - h * HALF])
 
         def round_y(c):
             copy = nc.vector.tensor_copy if c == CHUNKS - 1 else nc.scalar.copy
             copy(y_bf16[c][:].rearrange("p (g i t) -> p g t i", t=PACK, i=4), y_chunk(c).rearrange("p t (g i) -> p g t i", i=4))
 
         def quantise_y(c):
-            codes = sbuf.tile([P, CHUNK], I32, name="y_codes%d" % c, align_bytes=64)
-            nc.vector.quantize_mx(out=codes[:].bitcast(FP8X4), scales=y_plane[:, chunk_cols(c)], in_=y_bf16[c][:])
-            nc.sync.dma_start(y_words[:, chunk_cols(c)], codes[:])
+            nc.vector.quantize_mx(out=y_codes[:, chunk_cols(c)].bitcast(FP8X4), scales=y_plane[:, chunk_cols(c)], in_=y_bf16[c][:])
+            cols = stored_with(c)
+            if cols:
+                nc.sync.dma_start(y_words[:, cols], y_codes[:, cols])
 
-        gated_first = sbuf.tile([P, PACK - EARLY, HALF], F32, name="gated_first", align_bytes=64)
-        multiply(gated_first[:], late, slice(0, HALF))
-        gather_r(PACK - 1, 0, J)
-        for c in range(per_half):
-            add_late(c, gated_first[:, :, chunk_cols(c)])
-        for c in range(per_half):
-            round_y(c)
-        gated_second = sbuf.tile([P, per_half, PACK - EARLY, CHUNK], F32, name="gated_second", tag="r3", align_bytes=64)
-        for i in range(per_half):
-            multiply(gated_second[:, i], late, chunk_cols(per_half + i))
-        for i in range(per_half):
-            add_late(per_half + i, gated_second[:, i])
-            quantise_y(i)
-        for c in range(per_half, CHUNKS):
-            round_y(c)
+        places = ("turned0_0", "turned%d_%d" % (EARLY - 1, HALVES - 1))
+        for h in range(HALVES):
+            chunks = range(h * PER_HALF, (h + 1) * PER_HALF)
+            gated_late = sbuf.tile([P, PER_HALF, PACK - EARLY, CHUNK], F32, name="gated_late%d" % h, tag=places[h], align_bytes=64)
+            for i, c in enumerate(chunks):
+                multiply(gated_late[:, i], late, chunk_cols(c))
+            for i, c in enumerate(chunks):
+                add_late(c, gated_late[:, i])
+                if c >= QUANTISE_LAG:
+                    quantise_y(c - QUANTISE_LAG)
+            for c in chunks:
+                round_y(c)
         for c in range(CHUNKS - QUANTISE_LAG, CHUNKS):
             quantise_y(c)
 

@@ -43,18 +43,19 @@ def tile_list_hwayt_tanhP_kernel(
 
         table_scales = sbuf.tile([P, T], U8, name="table_scales", align_bytes=64)
         nc.vector.memset(table_scales[:].bitcast(I32), 0)
-        wg_scales_in = sbuf.tile([P, PASSES * N], U8, name="wg_scales_in", tag="wg_scales_in", align_bytes=64)
+        head = ctx.enter_context(tc.tile_pool(name="head", bufs=1))
+        wg_scales_in = head.tile([P, PASSES * N], U8, name="wg_scales_in", align_bytes=64, offset=1536)
         nc.vector.memset(wg_scales_in[:].bitcast(I32), 0)
         v_plane1 = sbuf.tile([P, J], U8, name="v_plane1", align_bytes=64)
         nc.vector.memset(v_plane1[:].bitcast(I32), 0)
 
+        wg_words_in = sbuf.tile([P, PASSES, N // 2], I32, name="wg_words_in", align_bytes=64)
+        nc.sync.dma_start(wg_words_in[:], wg_words.bitcast(I32).rearrange("a p n -> p a n"))
         offsets = sbuf.tile(list(offs.shape), U16, name="offsets")
         nc.sync.dma_start(offsets[:], offs)
         table_scale_rows = tab_scales.bitcast(I32).rearrange("a (q r) c -> r q a c", r=PLANE_ROWS)
         for r in range(PLANE_ROWS):
             nc.sync.dma_start(table_scales[r:P:SHIFT, :].bitcast(I32), table_scale_rows[r])
-        wg_words_in = sbuf.tile([P, PASSES, N // 2], I32, name="wg_words_in", align_bytes=64)
-        nc.sync.dma_start(wg_words_in[:], wg_words.bitcast(I32).rearrange("a p n -> p a n"))
         table_words = sbuf.tile([P, T], I32, name="table_words", align_bytes=64)
         nc.sync.dma_start(table_words[:], tab_words[0].rearrange("p c b -> p (c b)").bitcast(I32))
         for q in range(QUADS):
@@ -62,24 +63,18 @@ def tile_list_hwayt_tanhP_kernel(
                 wg_scales_in[32 * q : 32 * q + PLANE_ROWS, :].bitcast(I32).rearrange("r (a n) -> r a n", a=PASSES),
                 wg_scales[:, PLANE_ROWS * q : PLANE_ROWS * (q + 1), :].bitcast(I32).rearrange("a r n -> r a n"),
             )
-        bias = sbuf.tile([P, PACK], F32, name="bias")
-        nc.sync.dma_start(bias[:], bg.rearrange("(p t) -> p t", t=PACK))
 
         wh_rows = wh.rearrange("(a p i) n -> a p i n", p=P, i=PACK)
-        wh_first = sbuf.tile([P, PACK, N], F32, name="wh_first", align_bytes=64)
+        wh_first = sbuf.tile([P, PACK, N], F32, name="wh_first", tag="wh_first", align_bytes=64)
         nc.sync.dma_start(wh_first[:], wh_rows[0])
-        wh_second = [
-            sbuf.tile([P, PACK, N // 2], F32, name="wh_second%d" % u, tag="wh_second%d" % u, align_bytes=64) for u in range(2)
-        ]
-        nc.sync.dma_start(wh_second[0][:], wh_rows[1][:, :, : N // 2])
+        wh_second = sbuf.tile([P, PACK, N], F32, name="wh_second", align_bytes=64)
+        nc.sync.dma_start(wh_second[:, : PACK // 2, :], wh_rows[1][:, : PACK // 2, :])
 
         warm = sbuf.tile([P, 1], F32, name="warm", tag="warm", align_bytes=64)
         nc.vector.memset(warm[:], 0.0)
         nc.scalar.activation(warm[:], warm[:], ACT.Sigmoid)
         ident = sbuf.tile([P, P], F32, name="ident", tag="warm", align_bytes=64)
         make_identity(nc, ident[:])
-        minus_bias = sbuf.tile([P, PACK], F32, name="minus_bias")
-        nc.scalar.mul(minus_bias[:], bias[:], -1.0)
 
         wg_codes = sbuf.tile([P, PASSES * N * 2], U8, name="wg_codes", align_bytes=64)
         nc.vector.tensor_copy(
@@ -92,25 +87,35 @@ def tile_list_hwayt_tanhP_kernel(
         nc.sync.dma_start(v_plane1[: P - SHIFT, :].bitcast(I32), v_plane0[SHIFT:, :].bitcast(I32))
         v_planes = (v_plane0, v_plane1)
 
-        nc.sync.dma_start(wh_second[1][:], wh_rows[1][:, :, N // 2 :])
+        nc.sync.dma_start(wh_second[:, PACK // 2 :, :], wh_rows[1][:, PACK // 2 :, :])
+        bias = sbuf.tile([P, PACK], F32, name="bias")
+        nc.sync.dma_start(bias[:], bg.rearrange("(p t) -> p t", t=PACK))
         r_rows = rT.rearrange("(p t) c -> t p c", t=PACK)
         r_slices = [sbuf.tile([P, T], F32, name="r%d" % t, align_bytes=64) for t in range(PACK)]
         for t in range(PACK):
             nc.sync.dma_start(r_slices[t][:], r_rows[t])
 
-        pairs = sbuf.tile([P, J], U32, name="pairs", align_bytes=64)
-        nc.vector.tensor_copy(pairs[:], table_words[:].bitcast(U32).indirect(offsets[:]))
+        pairs = [
+            sbuf.tile([P, HALF], U32, name="pairs0", align_bytes=64),
+            head.tile([P, HALF], U32, name="pairs1", align_bytes=64, offset=2048),
+        ]
+        nc.vector.tensor_copy(pairs[0][:], table_words[:].bitcast(U32).indirect(offsets[:, :32]))
         wg_planes = sbuf.tile([P, PASSES * N], U8, name="wg_planes", align_bytes=64)
         nc.vector.tensor_copy(
             wg_planes[:].rearrange("p (a t m) -> p a t m", a=PASSES, t=PACK),
             wg_scales_in[:].rearrange("p (a m t) -> p a t m", a=PASSES, t=PACK),
         )
-        parted = sbuf.tile([P, HALVES, PASSES * HALF * 2], U8, name="parted", tag="wg_scales_in", align_bytes=64)
-        v_codes = [parted[:, h, :] for h in range(HALVES)]
+        parted = [
+            head.tile([P, PASSES * HALF * 2], U8, name="parted0", align_bytes=64, offset=0),
+            sbuf.tile([P, PASSES * HALF * 2], U8, name="parted1", align_bytes=64),
+        ]
+        v_codes = [parted[h][:] for h in range(HALVES)]
         for h in range(HALVES):
+            if h == 1:
+                nc.vector.tensor_copy(pairs[1][:], table_words[:].bitcast(U32).indirect(offsets[:, 32:]))
             nc.vector.tensor_copy(
                 v_codes[h].bitcast(U16).rearrange("p (a j) -> p a j", a=PASSES),
-                pairs[:, h * HALF : (h + 1) * HALF].bitcast(U16).rearrange("p (j a) -> p a j", a=PASSES),
+                pairs[h][:].bitcast(U16).rearrange("p (j a) -> p a j", a=PASSES),
             )
 
         m_all = sbuf.tile([P, PACK, J], F32, name="m_all", align_bytes=64)
@@ -119,12 +124,12 @@ def tile_list_hwayt_tanhP_kernel(
         wh_codes = [sbuf.tile([P, N], U32, name="wh_codes%d" % a, align_bytes=64) for a in range(PASSES)]
         wh_planes = [sbuf.tile([P, N], U8, name="wh_planes%d" % a, align_bytes=64) for a in range(PASSES)]
 
-        def round_wh(a, u, columns, copy):
+        def round_wh(a, m0, m1, t0, t1, rows, copy):
             dealt = wh_bf16[a][:].rearrange("p (t m i) -> p m i t", t=PACK, i=PACK)
-            copy(dealt[:, u * P // 2 : (u + 1) * P // 2], columns.rearrange("p i (m t) -> p m i t", t=PACK))
+            copy(dealt[:, m0:m1, :, t0:t1], rows[:].rearrange("p i (m t) -> p m i t", t=PACK)[:, m0:m1, :, t0:t1])
 
-        def quantise_wh(a):
-            nc.vector.quantize_mx(out=wh_codes[a][:].bitcast(FP8X4), scales=wh_planes[a][:], in_=wh_bf16[a][:])
+        def quantise_wh(a, n0, n1):
+            nc.vector.quantize_mx(out=wh_codes[a][:, n0:n1].bitcast(FP8X4), scales=wh_planes[a][:, n0:n1], in_=wh_bf16[a][:, PACK * n0 : PACK * n1])
 
         def half_cols(h):
             return slice(h * HALF, (h + 1) * HALF)
@@ -133,34 +138,35 @@ def tile_list_hwayt_tanhP_kernel(
             b = HALVES * pair + h
             return psum.tile([P, HALF], F32, name="bank%d" % b, tag="bank%d" % b)
 
-        def product(h, pair, codes, planes):
+        def product(h, pair, codes, planes, opening=1):
             acc = bank(pair, h)
-            for a in reversed(range(PASSES)):
+            for a in (opening, 1 - opening):
                 nc.tensor.matmul_mx(
                     out=acc[:],
                     lhsT=codes[a],
                     lhsT_scale=planes[a],
                     rhs=v_codes[h][:, 2 * a * HALF : 2 * (a + 1) * HALF].bitcast(FP4X4),
                     rhs_scale=v_planes[a][:, half_cols(h)],
-                    start=(a == PASSES - 1),
-                    stop=(a == 0),
+                    start=(a == opening),
+                    stop=(a != opening),
                 )
             return acc
 
-        def gate(t, h):
+        def gate(t, h, pair):
             starts = [a * N + t * P for a in range(PASSES)]
             acc = product(
                 h,
-                t,
+                pair,
                 [wg_codes[:, 2 * n0 : 2 * (n0 + P)].bitcast(FP4X4) for n0 in starts],
                 [wg_planes[:, n0 : n0 + P] for n0 in starts],
+                0 if h == 0 and t < 2 else 1,
             )
             nc.scalar.activation(s_all[:, t, half_cols(h)], acc[:], ACT.Sigmoid, bias=minus_bias[:, t : t + 1], scale=-1.0)
 
-        def candidate(t, h):
+        def candidate(t, h, pair):
             acc = product(
                 h,
-                (t + EARLY) % PACK,
+                pair,
                 [wh_codes[a][:, t * P : (t + 1) * P].bitcast(FP8X4) for a in range(PASSES)],
                 [wh_planes[a][:, t * P : (t + 1) * P] for a in range(PASSES)],
             )
@@ -169,18 +175,19 @@ def tile_list_hwayt_tanhP_kernel(
         def gather_r(t):
             nc.vector.tensor_tensor(rs_all[:, t, :], r_slices[t][:].indirect(offsets[:]), s_all[:, t, :], ALU.mult)
 
-        round_wh(0, 0, wh_first[:, :, : N // 2], nc.scalar.copy)
-        round_wh(0, 1, wh_first[:, :, N // 2 :], nc.scalar.copy)
-        round_wh(1, 0, wh_second[0][:], nc.scalar.copy)
-        quantise_wh(0)
-        round_wh(1, 1, wh_second[1][:], nc.vector.tensor_copy)
-        quantise_wh(1)
-        s_all = sbuf.tile([P, PACK, J], F32, name="s_all", tag="wh_second0", align_bytes=64)
-        for first in (0, EARLY):
-            for stage in (gate, candidate):
-                for t in range(first, first + EARLY):
-                    for h in range(HALVES):
-                        stage(t, h)
+        round_wh(0, 0, P, 0, PACK, wh_first, nc.scalar.copy)
+        quantise_wh(0, 0, N)
+        round_wh(1, 0, P, 0, 2, wh_second, nc.vector.tensor_copy)
+        round_wh(1, 0, P // 2, 2, PACK, wh_second, nc.vector.tensor_copy)
+        round_wh(1, P // 2, P, 2, PACK, wh_second, nc.scalar.copy)
+        quantise_wh(1, 0, N // 2)
+        quantise_wh(1, N // 2, N)
+        minus_bias = sbuf.tile([P, PACK], F32, name="minus_bias")
+        nc.scalar.mul(minus_bias[:], bias[:], -1.0)
+        s_all = sbuf.tile([P, PACK, J], F32, name="s_all", tag="wh_first", align_bytes=64)
+        for stage, t, pair in ((gate, 0, 0), (gate, 1, 1), (gate, 2, 2), (candidate, 0, 3), (candidate, 1, 0), (gate, 3, 3)):
+            for h in range(HALVES):
+                stage(t, h, pair)
 
         y_rows = out_0.rearrange("(p t) j -> p t j", t=PACK)
         y_words = out_1[0].rearrange("p j i -> p (j i)").bitcast(I32)
@@ -201,14 +208,16 @@ def tile_list_hwayt_tanhP_kernel(
         def y_chunk(c):
             return y[c // PER_HALF][:, :, (c % PER_HALF) * CHUNK : (c % PER_HALF + 1) * CHUNK]
 
-        gated_early = sbuf.tile([P, EARLY, J], F32, name="gated_early", align_bytes=64)
         for t in range(EARLY):
-            gather_r(t)
-            multiply(gated_early[:, t : t + 1, :], slice(t, t + 1), slice(0, J))
+            for h in range(HALVES):
+                nc.vector.tensor_tensor(rs_all[:, t, half_cols(h)], r_slices[t][:].indirect(offsets[:, 32 * h : 32 * (h + 1)]), s_all[:, t, half_cols(h)], ALU.mult)
+            for h in range(HALVES):
+                multiply(s_all[:, t : t + 1, half_cols(h)], slice(t, t + 1), half_cols(h))
+        sum_pair = (2, 1)
 
         def add_turned(t, h):
-            acc = bank(EARLY + t, h)
-            for n, term in enumerate((rs_all, gated_early)):
+            acc = bank(sum_pair[t], h)
+            for n, term in enumerate((rs_all, s_all)):
                 for b in range(HALF // P):
                     cols = slice(h * HALF + b * P, h * HALF + (b + 1) * P)
                     first, final = (n, b) == (0, 0), (n, b) == (1, HALF // P - 1)
@@ -218,20 +227,28 @@ def tile_list_hwayt_tanhP_kernel(
             return turned
 
         def turn_back(t, h, turned):
-            acc = bank(EARLY + t, h)
+            acc = bank(sum_pair[t], h)
             for b in range(HALF // P):
                 nc.tensor.transpose(acc[:, b * P : (b + 1) * P], turned[:, b * P : (b + 1) * P], ident[:])
             nc.scalar.copy(y[h][:, t, :], acc[:])
 
-        turned_sums = {(t, h): add_turned(t, h) for t in range(EARLY) for h in range(HALVES)}
-        for h in range(HALVES):
-            for t in range(EARLY):
-                turn_back(t, h, turned_sums[t, h])
-            nc.scalar.dma_start(y_rows[:, :EARLY, half_cols(h)], y[h][:, :EARLY, :])
+        for t in range(EARLY):
+            turned_sums = [add_turned(t, h) for h in range(HALVES)]
+            if t == 0:
+                for h in range(HALVES):
+                    candidate(2, h, 3)
+            else:
+                for h in range(HALVES):
+                    candidate(3, h, 2)
+            for h in range(HALVES):
+                turn_back(t, h, turned_sums[h])
+                if t == EARLY - 1:
+                    nc.scalar.dma_start(y_rows[:, :EARLY, half_cols(h)], y[h][:, :EARLY, :])
 
         late = slice(EARLY, PACK)
-        for t in range(EARLY, PACK):
-            gather_r(t)
+        gather_r(2)
+        for h in range(HALVES):
+            nc.vector.tensor_tensor(rs_all[:, 3, half_cols(h)], r_slices[3][:].indirect(offsets[:, 32 * h : 32 * (h + 1)]), s_all[:, 3, half_cols(h)], ALU.mult)
 
         def stored_with(c):
             if c >= PER_HALF:
@@ -258,11 +275,15 @@ def tile_list_hwayt_tanhP_kernel(
         places = ("turned0_0", "turned%d_%d" % (EARLY - 1, HALVES - 1))
         for h in range(HALVES):
             chunks = range(h * PER_HALF, (h + 1) * PER_HALF)
-            gated_late = sbuf.tile([P, PER_HALF, PACK - EARLY, CHUNK], F32, name="gated_late%d" % h, tag=places[h], align_bytes=64)
+            if h == 0:
+                gated_late = [s_all[:, late, chunk_cols(c)] for c in chunks]
+            else:
+                second = sbuf.tile([P, PER_HALF, PACK - EARLY, CHUNK], F32, name="gated_late%d" % h, tag=places[h], align_bytes=64)
+                gated_late = [second[:, i] for i in range(PER_HALF)]
             for i, c in enumerate(chunks):
-                multiply(gated_late[:, i], late, chunk_cols(c))
+                multiply(gated_late[i], late, chunk_cols(c))
             for i, c in enumerate(chunks):
-                add_late(c, gated_late[:, i])
+                add_late(c, gated_late[i])
                 if c >= QUANTISE_LAG:
                     quantise_y(c - QUANTISE_LAG)
             for c in chunks:

@@ -43,8 +43,7 @@ def tile_list_hwayt_tanhP_kernel(
 
         table_scales = sbuf.tile([P, T], U8, name="table_scales", align_bytes=64)
         nc.vector.memset(table_scales[:].bitcast(I32), 0)
-        head = ctx.enter_context(tc.tile_pool(name="head", bufs=1))
-        wg_scales_in = head.tile([P, PASSES * N], U8, name="wg_scales_in", align_bytes=64, offset=1536)
+        wg_scales_in = sbuf.tile([P, PASSES * N], U8, name="wg_scales_in", align_bytes=64)
         nc.vector.memset(wg_scales_in[:].bitcast(I32), 0)
         v_plane1 = sbuf.tile([P, J], U8, name="v_plane1", align_bytes=64)
         nc.vector.memset(v_plane1[:].bitcast(I32), 0)
@@ -87,36 +86,31 @@ def tile_list_hwayt_tanhP_kernel(
         nc.sync.dma_start(v_plane1[: P - SHIFT, :].bitcast(I32), v_plane0[SHIFT:, :].bitcast(I32))
         v_planes = (v_plane0, v_plane1)
 
-        nc.sync.dma_start(wh_second[:, PACK // 2 :, :], wh_rows[1][:, PACK // 2 :, :])
         bias = sbuf.tile([P, PACK], F32, name="bias")
         nc.sync.dma_start(bias[:], bg.rearrange("(p t) -> p t", t=PACK))
+        nc.sync.dma_start(wh_second[:, PACK // 2 :, :], wh_rows[1][:, PACK // 2 :, :])
         r_rows = rT.rearrange("(p t) c -> t p c", t=PACK)
         r_slices = [sbuf.tile([P, T], F32, name="r%d" % t, align_bytes=64) for t in range(PACK)]
         for t in range(PACK):
             nc.sync.dma_start(r_slices[t][:], r_rows[t])
 
-        pairs = [
-            sbuf.tile([P, HALF], U32, name="pairs0", align_bytes=64),
-            head.tile([P, HALF], U32, name="pairs1", align_bytes=64, offset=2048),
-        ]
-        nc.vector.tensor_copy(pairs[0][:], table_words[:].bitcast(U32).indirect(offsets[:, :32]))
         wg_planes = sbuf.tile([P, PASSES * N], U8, name="wg_planes", align_bytes=64)
-        nc.vector.tensor_copy(
+        nc.gpsimd.tensor_copy(
             wg_planes[:].rearrange("p (a t m) -> p a t m", a=PASSES, t=PACK),
             wg_scales_in[:].rearrange("p (a m t) -> p a t m", a=PASSES, t=PACK),
         )
-        parted = [
-            head.tile([P, PASSES * HALF * 2], U8, name="parted0", align_bytes=64, offset=0),
-            sbuf.tile([P, PASSES * HALF * 2], U8, name="parted1", align_bytes=64),
-        ]
+        parted = [sbuf.tile([P, PASSES * HALF * 2], U8, name="parted%d" % h, align_bytes=64) for h in range(HALVES)]
         v_codes = [parted[h][:] for h in range(HALVES)]
         for h in range(HALVES):
-            if h == 1:
-                nc.vector.tensor_copy(pairs[1][:], table_words[:].bitcast(U32).indirect(offsets[:, 32:]))
-            nc.vector.tensor_copy(
-                v_codes[h].bitcast(U16).rearrange("p (a j) -> p a j", a=PASSES),
-                pairs[h][:].bitcast(U16).rearrange("p (j a) -> p a j", a=PASSES),
-            )
+            pairs = [sbuf.tile([P, CHUNK], U32, name="pairs%d_%d" % (h, i), tag="pairs%d" % i, align_bytes=64) for i in range(PER_HALF)]
+            for i in range(PER_HALF):
+                c = h * PER_HALF + i
+                nc.vector.tensor_copy(pairs[i][:], table_words[:].bitcast(U32).indirect(offsets[:, 16 * c : 16 * (c + 1)]))
+            for i in range(PER_HALF):
+                nc.vector.tensor_copy(
+                    v_codes[h].bitcast(U16).rearrange("p (a j) -> p a j", a=PASSES)[:, :, i * CHUNK : (i + 1) * CHUNK],
+                    pairs[i][:].bitcast(U16).rearrange("p (j a) -> p a j", a=PASSES),
+                )
 
         m_all = sbuf.tile([P, PACK, J], F32, name="m_all", align_bytes=64)
         rs_all = sbuf.tile([P, PACK, J], F32, name="rs_all", align_bytes=64)
@@ -159,7 +153,7 @@ def tile_list_hwayt_tanhP_kernel(
                 pair,
                 [wg_codes[:, 2 * n0 : 2 * (n0 + P)].bitcast(FP4X4) for n0 in starts],
                 [wg_planes[:, n0 : n0 + P] for n0 in starts],
-                0 if h == 0 and t < 2 else 1,
+                0 if h == 0 and t < 3 else 1,
             )
             nc.scalar.activation(s_all[:, t, half_cols(h)], acc[:], ACT.Sigmoid, bias=minus_bias[:, t : t + 1], scale=-1.0)
 
@@ -175,11 +169,11 @@ def tile_list_hwayt_tanhP_kernel(
         def gather_r(t):
             nc.vector.tensor_tensor(rs_all[:, t, :], r_slices[t][:].indirect(offsets[:]), s_all[:, t, :], ALU.mult)
 
-        round_wh(0, 0, P, 0, PACK, wh_first, nc.scalar.copy)
+        round_wh(0, 0, 96, 0, PACK, wh_first, nc.scalar.copy)
+        round_wh(0, 96, P, 0, PACK, wh_first, nc.vector.tensor_copy)
         quantise_wh(0, 0, N)
         round_wh(1, 0, P, 0, 2, wh_second, nc.vector.tensor_copy)
-        round_wh(1, 0, P // 2, 2, PACK, wh_second, nc.vector.tensor_copy)
-        round_wh(1, P // 2, P, 2, PACK, wh_second, nc.scalar.copy)
+        round_wh(1, 0, P, 2, PACK, wh_second, nc.vector.tensor_copy)
         quantise_wh(1, 0, N // 2)
         quantise_wh(1, N // 2, N)
         minus_bias = sbuf.tile([P, PACK], F32, name="minus_bias")
@@ -213,15 +207,16 @@ def tile_list_hwayt_tanhP_kernel(
                 nc.vector.tensor_tensor(rs_all[:, t, half_cols(h)], r_slices[t][:].indirect(offsets[:, 32 * h : 32 * (h + 1)]), s_all[:, t, half_cols(h)], ALU.mult)
             for h in range(HALVES):
                 multiply(s_all[:, t : t + 1, half_cols(h)], slice(t, t + 1), half_cols(h))
-        sum_pair = (2, 1)
+        sum_pair = (2, 1, 0)
 
         def add_turned(t, h):
             acc = bank(sum_pair[t], h)
-            for n, term in enumerate((rs_all, s_all)):
+            terms = (rs_all[:, t, :], s_all[:, t, :]) if t < 2 else (m_all[:, 1, :], rs_all[:, t, :])
+            for n, term in enumerate(terms):
                 for b in range(HALF // P):
                     cols = slice(h * HALF + b * P, h * HALF + (b + 1) * P)
                     first, final = (n, b) == (0, 0), (n, b) == (1, HALF // P - 1)
-                    nc.tensor.matmul(acc[:, b * P : (b + 1) * P], term[:, t, cols], ident[:], is_transpose=True, start=first, stop=final)
+                    nc.tensor.matmul(acc[:, b * P : (b + 1) * P], term[:, cols], ident[:], is_transpose=True, start=first, stop=final)
             turned = sbuf.tile([P, HALF], F32, name="turned%d_%d" % (t, h), tag="turned%d_%d" % (t, h), align_bytes=64)
             nc.scalar.copy(turned[:], acc[:])
             return turned
@@ -243,10 +238,13 @@ def tile_list_hwayt_tanhP_kernel(
             for h in range(HALVES):
                 turn_back(t, h, turned_sums[h])
                 if t == EARLY - 1:
-                    nc.scalar.dma_start(y_rows[:, :EARLY, half_cols(h)], y[h][:, :EARLY, :])
+                    nc.sync.dma_start(y_rows[:, :EARLY, half_cols(h)], y[h][:, :EARLY, :])
 
         late = slice(EARLY, PACK)
-        gather_r(2)
+        multiply(m_all[:, 1:2, half_cols(0)], slice(2, 3), half_cols(0))
+        for h in range(HALVES):
+            nc.vector.tensor_tensor(rs_all[:, 2, half_cols(h)], r_slices[2][:].indirect(offsets[:, 32 * h : 32 * (h + 1)]), s_all[:, 2, half_cols(h)], ALU.mult)
+        turn_back(2, 0, add_turned(2, 0))
         for h in range(HALVES):
             nc.vector.tensor_tensor(rs_all[:, 3, half_cols(h)], r_slices[3][:].indirect(offsets[:, 32 * h : 32 * (h + 1)]), s_all[:, 3, half_cols(h)], ALU.mult)
 
@@ -256,7 +254,8 @@ def tile_list_hwayt_tanhP_kernel(
             return half_cols(0) if c == PER_HALF - 1 else None
 
         def add_late(c, gated):
-            nc.vector.tensor_tensor(y_chunk(c)[:, late, :], rs_all[:, late, chunk_cols(c)], gated, ALU.add)
+            rows = late if c >= PER_HALF else slice(3, 4)
+            nc.vector.tensor_tensor(y_chunk(c)[:, rows, :], rs_all[:, rows, chunk_cols(c)], gated, ALU.add)
             cols = stored_with(c)
             if cols:
                 h = c // PER_HALF
@@ -272,16 +271,16 @@ def tile_list_hwayt_tanhP_kernel(
             if cols:
                 nc.sync.dma_start(y_words[:, cols], y_codes[:, cols])
 
-        places = ("turned0_0", "turned%d_%d" % (EARLY - 1, HALVES - 1))
+        places = ("turned0_0", "turned2_0")
         for h in range(HALVES):
             chunks = range(h * PER_HALF, (h + 1) * PER_HALF)
             if h == 0:
-                gated_late = [s_all[:, late, chunk_cols(c)] for c in chunks]
+                gated_late = [s_all[:, 3:4, chunk_cols(c)] for c in chunks]
             else:
                 second = sbuf.tile([P, PER_HALF, PACK - EARLY, CHUNK], F32, name="gated_late%d" % h, tag=places[h], align_bytes=64)
                 gated_late = [second[:, i] for i in range(PER_HALF)]
             for i, c in enumerate(chunks):
-                multiply(gated_late[i], late, chunk_cols(c))
+                multiply(gated_late[i], late if h else slice(3, 4), chunk_cols(c))
             for i, c in enumerate(chunks):
                 add_late(c, gated_late[i])
                 if c >= QUANTISE_LAG:

@@ -26,7 +26,11 @@ PLANE_ROWS = 4
 HALF = 512
 HALVES = J // HALF
 SHIFT = 16
+PER_COLUMN = 16
 EARLY = 2
+SHARED = EARLY
+LAST = PACK - 1
+SCALAR_M = 96
 CHUNK = 256
 CHUNKS = J // CHUNK
 PER_HALF = HALF // CHUNK
@@ -99,18 +103,36 @@ def tile_list_hwayt_tanhP_kernel(
             wg_planes[:].rearrange("p (a t m) -> p a t m", a=PASSES, t=PACK),
             wg_scales_in[:].rearrange("p (a m t) -> p a t m", a=PASSES, t=PACK),
         )
-        parted = [sbuf.tile([P, PASSES * HALF * 2], U8, name="parted%d" % h, align_bytes=64) for h in range(HALVES)]
-        v_codes = [parted[h][:] for h in range(HALVES)]
-        for h in range(HALVES):
-            pairs = [sbuf.tile([P, CHUNK], U32, name="pairs%d_%d" % (h, i), tag="pairs%d" % i, align_bytes=64) for i in range(PER_HALF)]
-            for i in range(PER_HALF):
-                c = h * PER_HALF + i
-                nc.vector.tensor_copy(pairs[i][:], table_words[:].bitcast(U32).indirect(offsets[:, 16 * c : 16 * (c + 1)]))
-            for i in range(PER_HALF):
-                nc.vector.tensor_copy(
-                    v_codes[h].bitcast(U16).rearrange("p (a j) -> p a j", a=PASSES)[:, :, i * CHUNK : (i + 1) * CHUNK],
-                    pairs[i][:].bitcast(U16).rearrange("p (j a) -> p a j", a=PASSES),
-                )
+
+        def half_cols(h):
+            return slice(h * HALF, (h + 1) * HALF)
+
+        def chunk_cols(c):
+            return slice(c * CHUNK, (c + 1) * CHUNK)
+
+        def entries(cols):
+            return offsets[:, cols.start // PER_COLUMN : cols.stop // PER_COLUMN]
+
+        v_codes = [sbuf.tile([P, PASSES * HALF * 2], U8, name="v_codes%d" % h, align_bytes=64) for h in range(HALVES)]
+        pairs = {}
+
+        def gather_words(c):
+            pairs[c] = sbuf.tile([P, CHUNK], U32, name="pairs%d" % c, tag="pairs%d" % (c % (CHUNKS - 1)), align_bytes=64)
+            nc.vector.tensor_copy(pairs[c][:], table_words[:].bitcast(U32).indirect(entries(chunk_cols(c))))
+
+        def part_words(c):
+            nc.vector.tensor_copy(
+                v_codes[c // PER_HALF][:].bitcast(U16).rearrange("p (a j) -> p a j", a=PASSES)[:, :, chunk_cols(c % PER_HALF)],
+                pairs[c][:].bitcast(U16).rearrange("p (j a) -> p a j", a=PASSES),
+            )
+
+        for c in range(CHUNKS - 1):
+            gather_words(c)
+        for c in range(PER_HALF):
+            part_words(c)
+        gather_words(CHUNKS - 1)
+        for c in range(PER_HALF, CHUNKS):
+            part_words(c)
 
         m_all = sbuf.tile([P, PACK, J], F32, name="m_all", align_bytes=64)
         rs_all = sbuf.tile([P, PACK, J], F32, name="rs_all", align_bytes=64)
@@ -118,21 +140,21 @@ def tile_list_hwayt_tanhP_kernel(
         wh_codes = [sbuf.tile([P, N], U32, name="wh_codes%d" % a, align_bytes=64) for a in range(PASSES)]
         wh_planes = [sbuf.tile([P, N], U8, name="wh_planes%d" % a, align_bytes=64) for a in range(PASSES)]
 
-        def round_wh(a, m0, m1, t0, t1, rows, copy):
+        def round_wh(a, rows, ms, slices, copy):
             dealt = wh_bf16[a][:].rearrange("p (t m i) -> p m i t", t=PACK, i=PACK)
-            copy(dealt[:, m0:m1, :, t0:t1], rows[:].rearrange("p i (m t) -> p m i t", t=PACK)[:, m0:m1, :, t0:t1])
+            copy(dealt[:, ms, :, slices], rows[:].rearrange("p i (m t) -> p m i t", t=PACK)[:, ms, :, slices])
 
-        def quantise_wh(a, n0, n1):
-            nc.vector.quantize_mx(out=wh_codes[a][:, n0:n1].bitcast(FP8X4), scales=wh_planes[a][:, n0:n1], in_=wh_bf16[a][:, PACK * n0 : PACK * n1])
-
-        def half_cols(h):
-            return slice(h * HALF, (h + 1) * HALF)
+        def quantise_wh(a, slices):
+            n0, n1 = slices.start * P, slices.stop * P
+            nc.vector.quantize_mx(
+                out=wh_codes[a][:, n0:n1].bitcast(FP8X4), scales=wh_planes[a][:, n0:n1], in_=wh_bf16[a][:, PACK * n0 : PACK * n1]
+            )
 
         def bank(pair, h):
             b = HALVES * pair + h
             return psum.tile([P, HALF], F32, name="bank%d" % b, tag="bank%d" % b)
 
-        def product(h, pair, codes, planes, opening=1):
+        def product(h, pair, codes, planes, opening):
             acc = bank(pair, h)
             for a in (opening, 1 - opening):
                 nc.tensor.matmul_mx(
@@ -153,7 +175,7 @@ def tile_list_hwayt_tanhP_kernel(
                 pair,
                 [wg_codes[:, 2 * n0 : 2 * (n0 + P)].bitcast(FP4X4) for n0 in starts],
                 [wg_planes[:, n0 : n0 + P] for n0 in starts],
-                0 if h == 0 and t < 3 else 1,
+                0 if h == 0 and t < LAST else 1,
             )
             nc.scalar.activation(s_all[:, t, half_cols(h)], acc[:], ACT.Sigmoid, bias=minus_bias[:, t : t + 1], scale=-1.0)
 
@@ -163,23 +185,23 @@ def tile_list_hwayt_tanhP_kernel(
                 pair,
                 [wh_codes[a][:, t * P : (t + 1) * P].bitcast(FP8X4) for a in range(PASSES)],
                 [wh_planes[a][:, t * P : (t + 1) * P] for a in range(PASSES)],
+                1,
             )
             nc.scalar.activation(m_all[:, t, half_cols(h)], acc[:], ACT.Tanh, scale=-1.0)
 
-        def gather_r(t):
-            nc.vector.tensor_tensor(rs_all[:, t, :], r_slices[t][:].indirect(offsets[:]), s_all[:, t, :], ALU.mult)
-
-        round_wh(0, 0, 96, 0, PACK, wh_first, nc.scalar.copy)
-        round_wh(0, 96, P, 0, PACK, wh_first, nc.vector.tensor_copy)
-        quantise_wh(0, 0, N)
-        round_wh(1, 0, P, 0, 2, wh_second, nc.vector.tensor_copy)
-        round_wh(1, 0, P, 2, PACK, wh_second, nc.vector.tensor_copy)
-        quantise_wh(1, 0, N // 2)
-        quantise_wh(1, N // 2, N)
+        all_m, all_slices = slice(0, P), slice(0, PACK)
+        slice_pairs = (slice(0, PACK // 2), slice(PACK // 2, PACK))
+        round_wh(0, wh_first, slice(0, SCALAR_M), all_slices, nc.scalar.copy)
+        round_wh(0, wh_first, slice(SCALAR_M, P), all_slices, nc.vector.tensor_copy)
+        quantise_wh(0, all_slices)
+        for slices in slice_pairs:
+            round_wh(1, wh_second, all_m, slices, nc.vector.tensor_copy)
+        for slices in slice_pairs:
+            quantise_wh(1, slices)
         minus_bias = sbuf.tile([P, PACK], F32, name="minus_bias")
         nc.scalar.mul(minus_bias[:], bias[:], -1.0)
         s_all = sbuf.tile([P, PACK, J], F32, name="s_all", tag="wh_first", align_bytes=64)
-        for stage, t, pair in ((gate, 0, 0), (gate, 1, 1), (gate, 2, 2), (candidate, 0, 3), (candidate, 1, 0), (gate, 3, 3)):
+        for stage, t, pair in ((gate, 0, 0), (gate, 1, 1), (gate, 2, 2), (candidate, 0, 3), (candidate, 1, 0), (gate, LAST, 3)):
             for h in range(HALVES):
                 stage(t, h, pair)
 
@@ -193,8 +215,13 @@ def tile_list_hwayt_tanhP_kernel(
             for c in range(CHUNKS)
         ]
 
-        def chunk_cols(c):
-            return slice(c * CHUNK, (c + 1) * CHUNK)
+        def one(t):
+            return slice(t, t + 1)
+
+        def gather_r(t):
+            for h in range(HALVES):
+                cols = half_cols(h)
+                nc.vector.tensor_tensor(rs_all[:, t, cols], r_slices[t][:].indirect(entries(cols)), s_all[:, t, cols], ALU.mult)
 
         def multiply(dst, slices, cols):
             nc.vector.scalar_tensor_tensor(dst, s_all[:, slices, cols], 1.0, m_all[:, slices, cols], ALU.subtract, ALU.mult)
@@ -202,16 +229,8 @@ def tile_list_hwayt_tanhP_kernel(
         def y_chunk(c):
             return y[c // PER_HALF][:, :, (c % PER_HALF) * CHUNK : (c % PER_HALF + 1) * CHUNK]
 
-        for t in range(EARLY):
-            for h in range(HALVES):
-                nc.vector.tensor_tensor(rs_all[:, t, half_cols(h)], r_slices[t][:].indirect(offsets[:, 32 * h : 32 * (h + 1)]), s_all[:, t, half_cols(h)], ALU.mult)
-            for h in range(HALVES):
-                multiply(s_all[:, t : t + 1, half_cols(h)], slice(t, t + 1), half_cols(h))
-        sum_pair = (2, 1, 0)
-
-        def add_turned(t, h):
-            acc = bank(sum_pair[t], h)
-            terms = (rs_all[:, t, :], s_all[:, t, :]) if t < 2 else (m_all[:, 1, :], rs_all[:, t, :])
+        def add_turned(t, h, pair, terms):
+            acc = bank(pair, h)
             for n, term in enumerate(terms):
                 for b in range(HALF // P):
                     cols = slice(h * HALF + b * P, h * HALF + (b + 1) * P)
@@ -221,32 +240,34 @@ def tile_list_hwayt_tanhP_kernel(
             nc.scalar.copy(turned[:], acc[:])
             return turned
 
-        def turn_back(t, h, turned):
-            acc = bank(sum_pair[t], h)
+        def turn_back(t, h, pair, turned):
+            acc = bank(pair, h)
             for b in range(HALF // P):
                 nc.tensor.transpose(acc[:, b * P : (b + 1) * P], turned[:, b * P : (b + 1) * P], ident[:])
             nc.scalar.copy(y[h][:, t, :], acc[:])
 
         for t in range(EARLY):
-            turned_sums = [add_turned(t, h) for h in range(HALVES)]
-            if t == 0:
-                for h in range(HALVES):
-                    candidate(2, h, 3)
-            else:
-                for h in range(HALVES):
-                    candidate(3, h, 2)
+            gather_r(t)
             for h in range(HALVES):
-                turn_back(t, h, turned_sums[h])
+                multiply(s_all[:, one(t), half_cols(h)], one(t), half_cols(h))
+
+        for t, sum_pair, late_t, late_pair in ((0, 2, SHARED, 3), (1, 1, LAST, 2)):
+            turned_sums = [add_turned(t, h, sum_pair, (rs_all[:, t, :], s_all[:, t, :])) for h in range(HALVES)]
+            for h in range(HALVES):
+                candidate(late_t, h, late_pair)
+            for h in range(HALVES):
+                turn_back(t, h, sum_pair, turned_sums[h])
                 if t == EARLY - 1:
                     nc.sync.dma_start(y_rows[:, :EARLY, half_cols(h)], y[h][:, :EARLY, :])
 
+        before = SHARED - 1
+        multiply(m_all[:, one(before), half_cols(0)], one(SHARED), half_cols(0))
+        gather_r(SHARED)
+        turn_back(SHARED, 0, 0, add_turned(SHARED, 0, 0, (m_all[:, before, :], rs_all[:, SHARED, :])))
+        gather_r(LAST)
+
         late = slice(EARLY, PACK)
-        multiply(m_all[:, 1:2, half_cols(0)], slice(2, 3), half_cols(0))
-        for h in range(HALVES):
-            nc.vector.tensor_tensor(rs_all[:, 2, half_cols(h)], r_slices[2][:].indirect(offsets[:, 32 * h : 32 * (h + 1)]), s_all[:, 2, half_cols(h)], ALU.mult)
-        turn_back(2, 0, add_turned(2, 0))
-        for h in range(HALVES):
-            nc.vector.tensor_tensor(rs_all[:, 3, half_cols(h)], r_slices[3][:].indirect(offsets[:, 32 * h : 32 * (h + 1)]), s_all[:, 3, half_cols(h)], ALU.mult)
+        left = (one(LAST), late)
 
         def stored_with(c):
             if c >= PER_HALF:
@@ -254,11 +275,10 @@ def tile_list_hwayt_tanhP_kernel(
             return half_cols(0) if c == PER_HALF - 1 else None
 
         def add_late(c, gated):
-            rows = late if c >= PER_HALF else slice(3, 4)
-            nc.vector.tensor_tensor(y_chunk(c)[:, rows, :], rs_all[:, rows, chunk_cols(c)], gated, ALU.add)
+            h = c // PER_HALF
+            nc.vector.tensor_tensor(y_chunk(c)[:, left[h], :], rs_all[:, left[h], chunk_cols(c)], gated, ALU.add)
             cols = stored_with(c)
             if cols:
-                h = c // PER_HALF
                 nc.sync.dma_start(y_rows[:, late, cols], y[h][:, late, cols.start - h * HALF : cols.stop - h * HALF])
 
         def round_y(c):
@@ -271,16 +291,17 @@ def tile_list_hwayt_tanhP_kernel(
             if cols:
                 nc.sync.dma_start(y_words[:, cols], y_codes[:, cols])
 
-        places = ("turned0_0", "turned2_0")
         for h in range(HALVES):
             chunks = range(h * PER_HALF, (h + 1) * PER_HALF)
             if h == 0:
-                gated_late = [s_all[:, 3:4, chunk_cols(c)] for c in chunks]
+                gated_late = [s_all[:, left[h], chunk_cols(c)] for c in chunks]
             else:
-                second = sbuf.tile([P, PER_HALF, PACK - EARLY, CHUNK], F32, name="gated_late%d" % h, tag=places[h], align_bytes=64)
+                second = sbuf.tile(
+                    [P, PER_HALF, PACK - EARLY, CHUNK], F32, name="gated_second", tag="turned%d_0" % SHARED, align_bytes=64
+                )
                 gated_late = [second[:, i] for i in range(PER_HALF)]
             for i, c in enumerate(chunks):
-                multiply(gated_late[i], late if h else slice(3, 4), chunk_cols(c))
+                multiply(gated_late[i], left[h], chunk_cols(c))
             for i, c in enumerate(chunks):
                 add_late(c, gated_late[i])
                 if c >= QUANTISE_LAG:

@@ -117,7 +117,7 @@ def tile_list_hwayt_tanhP_kernel(
         pairs = {}
 
         def gather_words(c):
-            pairs[c] = sbuf.tile([P, CHUNK], U32, name="pairs%d" % c, tag="pairs%d" % (c % (CHUNKS - 1)), align_bytes=64)
+            pairs[c] = sbuf.tile([P, CHUNK], U32, name="pairs%d" % c, tag="pairs%d" % (c % PER_HALF), align_bytes=64)
             nc.vector.tensor_copy(pairs[c][:], table_words[:].bitcast(U32).indirect(entries(chunk_cols(c))))
 
         def part_words(c):
@@ -126,13 +126,11 @@ def tile_list_hwayt_tanhP_kernel(
                 pairs[c][:].bitcast(U16).rearrange("p (j a) -> p a j", a=PASSES),
             )
 
-        for c in range(CHUNKS - 1):
-            gather_words(c)
-        for c in range(PER_HALF):
-            part_words(c)
-        gather_words(CHUNKS - 1)
-        for c in range(PER_HALF, CHUNKS):
-            part_words(c)
+        for h in range(HALVES):
+            for c in range(h * PER_HALF, (h + 1) * PER_HALF):
+                gather_words(c)
+            for c in range(h * PER_HALF, (h + 1) * PER_HALF):
+                part_words(c)
 
         m_all = sbuf.tile([P, PACK, J], F32, name="m_all", align_bytes=64)
         rs_all = sbuf.tile([P, PACK, J], F32, name="rs_all", align_bytes=64)
@@ -192,7 +190,14 @@ def tile_list_hwayt_tanhP_kernel(
         all_m, all_slices = slice(0, P), slice(0, PACK)
         slice_pairs = (slice(0, PACK // 2), slice(PACK // 2, PACK))
         round_wh(0, wh_first, slice(0, SCALAR_M), all_slices, nc.scalar.copy)
-        round_wh(0, wh_first, slice(SCALAR_M, P), all_slices, nc.vector.tensor_copy)
+        nc.gpsimd.tensor_scalar(
+            wh_bf16[0][:].rearrange("p (t m i) -> p t m i", t=PACK, i=PACK)[:, :, SCALAR_M:, :],
+            wh_first[:].rearrange("p i (m t) -> p t m i", t=PACK)[:, :, SCALAR_M:, :],
+            1.0,
+            0.0,
+            ALU.mult,
+            ALU.add,
+        )
         quantise_wh(0, all_slices)
         for slices in slice_pairs:
             round_wh(1, wh_second, all_m, slices, nc.vector.tensor_copy)

@@ -30,7 +30,7 @@ PER_COLUMN = 16
 EARLY = 2
 SHARED = EARLY
 LAST = PACK - 1
-SCALAR_M = 96
+SCALAR_M = 80
 CHUNK = 256
 CHUNKS = J // CHUNK
 PER_HALF = HALF // CHUNK
@@ -66,6 +66,8 @@ def tile_list_hwayt_tanhP_kernel(
                 wg_scales_in[32 * q : 32 * q + PLANE_ROWS, :].bitcast(I32).rearrange("r (a n) -> r a n", a=PASSES),
                 wg_scales[:, PLANE_ROWS * q : PLANE_ROWS * (q + 1), :].bitcast(I32).rearrange("a r n -> r a n"),
             )
+        bias = sbuf.tile([P, PACK], F32, name="bias")
+        nc.sync.dma_start(bias[:], bg.rearrange("(p t) -> p t", t=PACK))
 
         wh_rows = wh.rearrange("(a p i) n -> a p i n", p=P, i=PACK)
         wh_first = sbuf.tile([P, PACK, N], F32, name="wh_first", tag="wh_first", align_bytes=64)
@@ -90,8 +92,6 @@ def tile_list_hwayt_tanhP_kernel(
         nc.sync.dma_start(v_plane1[: P - SHIFT, :].bitcast(I32), v_plane0[SHIFT:, :].bitcast(I32))
         v_planes = (v_plane0, v_plane1)
 
-        bias = sbuf.tile([P, PACK], F32, name="bias")
-        nc.sync.dma_start(bias[:], bg.rearrange("(p t) -> p t", t=PACK))
         nc.sync.dma_start(wh_second[:, PACK // 2 :, :], wh_rows[1][:, PACK // 2 :, :])
         r_rows = rT.rearrange("(p t) c -> t p c", t=PACK)
         r_slices = [sbuf.tile([P, T], F32, name="r%d" % t, align_bytes=64) for t in range(PACK)]
@@ -173,7 +173,7 @@ def tile_list_hwayt_tanhP_kernel(
                 pair,
                 [wg_codes[:, 2 * n0 : 2 * (n0 + P)].bitcast(FP4X4) for n0 in starts],
                 [wg_planes[:, n0 : n0 + P] for n0 in starts],
-                0 if h == 0 and t < LAST else 1,
+                0 if h == 0 and t < EARLY else 1,
             )
             nc.scalar.activation(s_all[:, t, half_cols(h)], acc[:], ACT.Sigmoid, bias=minus_bias[:, t : t + 1], scale=-1.0)
 

@@ -132,8 +132,6 @@ def tile_list_hwayt_tanhP_kernel(
             for c in range(h * PER_HALF, (h + 1) * PER_HALF):
                 part_words(c)
 
-        m_all = sbuf.tile([P, PACK, J], F32, name="m_all", align_bytes=64)
-        rs_all = sbuf.tile([P, PACK, J], F32, name="rs_all", align_bytes=64)
         wh_bf16 = [sbuf.tile([P, PACK * N], BF16, name="wh_bf16_%d" % a, align_bytes=64) for a in range(PASSES)]
         wh_codes = [sbuf.tile([P, N], U32, name="wh_codes%d" % a, align_bytes=64) for a in range(PASSES)]
         wh_planes = [sbuf.tile([P, N], U8, name="wh_planes%d" % a, align_bytes=64) for a in range(PASSES)]
@@ -148,44 +146,8 @@ def tile_list_hwayt_tanhP_kernel(
                 out=wh_codes[a][:, n0:n1].bitcast(FP8X4), scales=wh_planes[a][:, n0:n1], in_=wh_bf16[a][:, PACK * n0 : PACK * n1]
             )
 
-        def bank(pair, h):
-            b = HALVES * pair + h
+        def bank(b):
             return psum.tile([P, HALF], F32, name="bank%d" % b, tag="bank%d" % b)
-
-        def product(h, pair, codes, planes, opening):
-            acc = bank(pair, h)
-            for a in (opening, 1 - opening):
-                nc.tensor.matmul_mx(
-                    out=acc[:],
-                    lhsT=codes[a],
-                    lhsT_scale=planes[a],
-                    rhs=v_codes[h][:, 2 * a * HALF : 2 * (a + 1) * HALF].bitcast(FP4X4),
-                    rhs_scale=v_planes[a][:, half_cols(h)],
-                    start=(a == opening),
-                    stop=(a != opening),
-                )
-            return acc
-
-        def gate(t, h, pair):
-            starts = [a * N + t * P for a in range(PASSES)]
-            acc = product(
-                h,
-                pair,
-                [wg_codes[:, 2 * n0 : 2 * (n0 + P)].bitcast(FP4X4) for n0 in starts],
-                [wg_planes[:, n0 : n0 + P] for n0 in starts],
-                0 if h == 0 and t < EARLY else 1,
-            )
-            nc.scalar.activation(s_all[:, t, half_cols(h)], acc[:], ACT.Sigmoid, bias=minus_bias[:, t : t + 1], scale=-1.0)
-
-        def candidate(t, h, pair):
-            acc = product(
-                h,
-                pair,
-                [wh_codes[a][:, t * P : (t + 1) * P].bitcast(FP8X4) for a in range(PASSES)],
-                [wh_planes[a][:, t * P : (t + 1) * P] for a in range(PASSES)],
-                1,
-            )
-            nc.scalar.activation(m_all[:, t, half_cols(h)], acc[:], ACT.Tanh, scale=-1.0)
 
         all_m, all_slices = slice(0, P), slice(0, PACK)
         slice_pairs = (slice(0, PACK // 2), slice(PACK // 2, PACK))
@@ -205,116 +167,185 @@ def tile_list_hwayt_tanhP_kernel(
             quantise_wh(1, slices)
         minus_bias = sbuf.tile([P, PACK], F32, name="minus_bias")
         nc.scalar.mul(minus_bias[:], bias[:], -1.0)
-        s_all = sbuf.tile([P, PACK, J], F32, name="s_all", tag="wh_first", align_bytes=64)
-        for stage, t, pair in ((gate, 0, 0), (gate, 1, 1), (gate, 2, 2), (candidate, 0, 3), (candidate, 1, 0), (gate, LAST, 3)):
+
+        s, rs, gated, gated_tile = {}, {}, {}, {}
+        for t in range(PACK):
             for h in range(HALVES):
-                stage(t, h, pair)
+                s[t, h] = sbuf.tile([P, HALF], F32, name="s%d_%d" % (t, h), tag="s%d_%d" % (t, h), align_bytes=64)[:]
+        for t, h in ((0, 0), (1, 0), (2, 0), (3, 0), (0, 1), (1, 1)):
+            rs[t, h] = sbuf.tile([P, HALF], F32, name="rs%d_%d" % (t, h), align_bytes=64)[:]
+
+        def new_gated(h, tag):
+            tile = sbuf.tile([P, PACK, HALF], F32, name="gated%d" % h, tag=tag, align_bytes=64)
+            gated_tile[h] = tile
+            for t in range(PACK):
+                gated[t, h] = tile[:, t, :].rearrange("p (b j) -> p b j", j=P)
+
+        m_turned = [sbuf.tile([P, N], F32, name="m_turned%d" % b, align_bytes=64) for b in range(J // P)]
+
+        def blocks(ap):
+            return ap.rearrange("p (b j) -> p b j", j=P)
+
+        def gate(t, h, b):
+            acc = bank(b)
+            opening = 0 if h == 0 and t < 2 else 1
+            for a in (opening, 1 - opening):
+                n0 = a * N + t * P
+                nc.tensor.matmul_mx(
+                    out=acc[:],
+                    lhsT=wg_codes[:, 2 * n0 : 2 * (n0 + P)].bitcast(FP4X4),
+                    lhsT_scale=wg_planes[:, n0 : n0 + P],
+                    rhs=v_codes[h][:, 2 * a * HALF : 2 * (a + 1) * HALF].bitcast(FP4X4),
+                    rhs_scale=v_planes[a][:, half_cols(h)],
+                    start=(a == opening),
+                    stop=(a != opening),
+                )
+            nc.scalar.activation(s[t, h], acc[:], ACT.Sigmoid, bias=minus_bias[:, t : t + 1], scale=-1.0)
+
+        def candidate(jb, b):
+            acc = bank(b)
+            h, j0 = divmod(jb * P, HALF)
+            for a in (1, 0):
+                nc.tensor.matmul_mx(
+                    out=acc[:],
+                    lhsT=v_codes[h][:, 2 * (a * HALF + j0) : 2 * (a * HALF + j0 + P)].bitcast(FP4X4),
+                    lhsT_scale=v_planes[a][:, jb * P : (jb + 1) * P],
+                    rhs=wh_codes[a][:].bitcast(FP8X4),
+                    rhs_scale=wh_planes[a][:],
+                    start=(a == 1),
+                    stop=(a == 0),
+                )
+            nc.scalar.activation(m_turned[jb][:], acc[:], ACT.Tanh, scale=-1.0)
+
+        m = {}
+
+        def turn_m(t, h):
+            m[t, h] = bank(1 + t)
+            for b in range(HALF // P):
+                nc.tensor.transpose(m[t, h][:, b * P : (b + 1) * P], m_turned[h * PACK + b][:, t * P : (t + 1) * P], ident[:])
 
         y_rows = out_0.rearrange("(p t) j -> p t j", t=PACK)
         y_words = out_1[0].rearrange("p j i -> p (j i)").bitcast(I32)
         y_plane = sbuf.tile([P, J], U8, name="y_plane", align_bytes=64)
         y = [sbuf.tile([P, PACK, HALF], F32, name="y%d" % h, align_bytes=64) for h in range(HALVES)]
         y_codes = sbuf.tile([P, J], I32, name="y_codes", align_bytes=64)
-        y_bf16 = [
-            sbuf.tile([P, PACK * CHUNK], BF16, name="y_bf16_%d" % c, tag="y_bf16_%d" % (c % (CHUNKS - 1)), align_bytes=64)
-            for c in range(CHUNKS)
-        ]
+        y_bf16 = [sbuf.tile([P, PACK * CHUNK], BF16, name="y_bf16_%d" % c, tag="y_bf16_%d" % (c % 3), align_bytes=64) for c in range(CHUNKS)]
 
-        def one(t):
-            return slice(t, t + 1)
+        def gather_r(t, h):
+            nc.vector.tensor_tensor(rs[t, h], r_slices[t][:].indirect(entries(half_cols(h))), s[t, h], ALU.mult)
 
-        def gather_r(t):
-            for h in range(HALVES):
-                cols = half_cols(h)
-                nc.vector.tensor_tensor(rs_all[:, t, cols], r_slices[t][:].indirect(entries(cols)), s_all[:, t, cols], ALU.mult)
+        def multiply(t, h):
+            nc.vector.scalar_tensor_tensor(gated[t, h], blocks(s[t, h]), 1.0, blocks(m[t, h][:]), ALU.subtract, ALU.mult)
 
-        def multiply(dst, slices, cols):
-            nc.vector.scalar_tensor_tensor(dst, s_all[:, slices, cols], 1.0, m_all[:, slices, cols], ALU.subtract, ALU.mult)
+        def store_rows(slices, cols):
+            h = cols.start // HALF
+            nc.sync.dma_start(y_rows[:, slices, cols], y[h][:, slices, cols.start - h * HALF : cols.stop - h * HALF])
 
-        def y_chunk(c):
-            return y[c // PER_HALF][:, :, (c % PER_HALF) * CHUNK : (c % PER_HALF + 1) * CHUNK]
+        def add_gpsimd(t, h):
+            nc.gpsimd.tensor_tensor(blocks(y[h][:, t, :]), blocks(rs[t, h]), gated[t, h], ALU.add)
 
-        def add_turned(t, h, pair, terms):
-            acc = bank(pair, h)
-            for n, term in enumerate(terms):
-                for b in range(HALF // P):
-                    cols = slice(h * HALF + b * P, h * HALF + (b + 1) * P)
-                    first, final = (n, b) == (0, 0), (n, b) == (1, HALF // P - 1)
-                    nc.tensor.matmul(acc[:, b * P : (b + 1) * P], term[:, cols], ident[:], is_transpose=True, start=first, stop=final)
-            turned = sbuf.tile([P, HALF], F32, name="turned%d_%d" % (t, h), tag="turned%d_%d" % (t, h), align_bytes=64)
-            nc.scalar.copy(turned[:], acc[:])
-            return turned
+        def add_turned(t, h, b, turned):
+            acc = bank(b)
+            for n, term in enumerate((gated[t, h], blocks(rs[t, h]))):
+                for k in range(HALF // P):
+                    first, final = (n, k) == (0, 0), (n, k) == (1, HALF // P - 1)
+                    nc.tensor.matmul(acc[:, k * P : (k + 1) * P], term[:, k, :], ident[:], is_transpose=True, start=first, stop=final)
+            nc.scalar.copy(turned, acc[:])
 
-        def turn_back(t, h, pair, turned):
-            acc = bank(pair, h)
-            for b in range(HALF // P):
-                nc.tensor.transpose(acc[:, b * P : (b + 1) * P], turned[:, b * P : (b + 1) * P], ident[:])
+        def turn_back(t, h, b, turned):
+            acc = bank(b)
+            for k in range(HALF // P):
+                nc.tensor.transpose(acc[:, k * P : (k + 1) * P], turned[:, k * P : (k + 1) * P], ident[:])
             nc.scalar.copy(y[h][:, t, :], acc[:])
 
-        for t in range(EARLY):
-            gather_r(t)
-            for h in range(HALVES):
-                multiply(s_all[:, one(t), half_cols(h)], one(t), half_cols(h))
+        def y_chunk(c):
+            return y[c // PER_HALF][:, :, chunk_cols(c % PER_HALF)]
 
-        for t, sum_pair, late_t, late_pair in ((0, 2, SHARED, 3), (1, 1, LAST, 2)):
-            turned_sums = [add_turned(t, h, sum_pair, (rs_all[:, t, :], s_all[:, t, :])) for h in range(HALVES)]
-            for h in range(HALVES):
-                candidate(late_t, h, late_pair)
-            for h in range(HALVES):
-                turn_back(t, h, sum_pair, turned_sums[h])
-                if t == EARLY - 1:
-                    nc.sync.dma_start(y_rows[:, :EARLY, half_cols(h)], y[h][:, :EARLY, :])
-
-        before = SHARED - 1
-        multiply(m_all[:, one(before), half_cols(0)], one(SHARED), half_cols(0))
-        gather_r(SHARED)
-        turn_back(SHARED, 0, 0, add_turned(SHARED, 0, 0, (m_all[:, before, :], rs_all[:, SHARED, :])))
-        gather_r(LAST)
-
-        late = slice(EARLY, PACK)
-        left = (one(LAST), late)
-
-        def stored_with(c):
-            if c >= PER_HALF:
-                return chunk_cols(c)
-            return half_cols(0) if c == PER_HALF - 1 else None
-
-        def add_late(c, gated):
-            h = c // PER_HALF
-            nc.vector.tensor_tensor(y_chunk(c)[:, left[h], :], rs_all[:, left[h], chunk_cols(c)], gated, ALU.add)
-            cols = stored_with(c)
-            if cols:
-                nc.sync.dma_start(y_rows[:, late, cols], y[h][:, late, cols.start - h * HALF : cols.stop - h * HALF])
-
-        def round_y(c):
-            copy = nc.vector.tensor_copy if c == CHUNKS - 1 else nc.scalar.copy
+        def round_y(c, copy):
             copy(y_bf16[c][:].rearrange("p (g i t) -> p g t i", t=PACK, i=4), y_chunk(c).rearrange("p t (g i) -> p g t i", i=4))
 
         def quantise_y(c):
             nc.vector.quantize_mx(out=y_codes[:, chunk_cols(c)].bitcast(FP8X4), scales=y_plane[:, chunk_cols(c)], in_=y_bf16[c][:])
-            cols = stored_with(c)
-            if cols:
-                nc.sync.dma_start(y_words[:, cols], y_codes[:, cols])
 
-        for h in range(HALVES):
-            chunks = range(h * PER_HALF, (h + 1) * PER_HALF)
-            if h == 0:
-                gated_late = [s_all[:, left[h], chunk_cols(c)] for c in chunks]
-            else:
-                second = sbuf.tile(
-                    [P, PER_HALF, PACK - EARLY, CHUNK], F32, name="gated_second", tag="turned%d_0" % SHARED, align_bytes=64
+        def one(t):
+            return slice(t, t + 1)
+
+        def candidate_rows(t, b):
+            acc = bank(b)
+            for a in (1, 0):
+                nc.tensor.matmul_mx(
+                    out=acc[:],
+                    lhsT=wh_codes[a][:, t * P : (t + 1) * P].bitcast(FP8X4),
+                    lhsT_scale=wh_planes[a][:, t * P : (t + 1) * P],
+                    rhs=v_codes[0][:, 2 * a * HALF : 2 * (a + 1) * HALF].bitcast(FP4X4),
+                    rhs_scale=v_planes[a][:, half_cols(0)],
+                    start=(a == 1),
+                    stop=(a == 0),
                 )
-                gated_late = [second[:, i] for i in range(PER_HALF)]
-            for i, c in enumerate(chunks):
-                multiply(gated_late[i], left[h], chunk_cols(c))
-            for i, c in enumerate(chunks):
-                add_late(c, gated_late[i])
-                if c >= QUANTISE_LAG:
-                    quantise_y(c - QUANTISE_LAG)
-            for c in chunks:
-                round_y(c)
-        for c in range(CHUNKS - QUANTISE_LAG, CHUNKS):
+            m[t, 0] = sbuf.tile([P, HALF], F32, name="m%d" % t, align_bytes=64)
+            nc.scalar.activation(m[t, 0][:], acc[:], ACT.Tanh, scale=-1.0)
+
+        for t, h, b in ((0, 0, 0), (0, 1, 1), (1, 0, 2), (2, 0, 3), (3, 0, 4)):
+            gate(t, h, b)
+        for t, b in enumerate((6, 7, 0, 1)):
+            candidate_rows(t, b)
+        for jb, b in zip(range(4, 8), (2, 3, 4, 6)):
+            candidate(jb, b)
+        for t, b in ((1, 5), (2, 7), (3, 0)):
+            gate(t, 1, b)
+        gather_r(0, 0)
+        gather_r(0, 1)
+        for t in range(PACK):
+            gated[t, 0] = blocks(m[t, 0][:])
+            multiply(t, 0)
+        gather_r(1, 0)
+        gather_r(1, 1)
+        gather_r(2, 0)
+        gather_r(3, 0)
+        turned = [sbuf.tile([P, HALF], F32, name="turned%d" % i, align_bytes=64) for i in range(4)]
+        add_turned(0, 0, 6, turned[0][:])
+        for t in range(PACK):
+            turn_m(t, 1)
+        add_turned(1, 0, 5, turned[1][:])
+        turn_back(0, 0, 7, turned[0][:])
+        add_turned(2, 0, 6, turned[2][:])
+        turn_back(1, 0, 0, turned[1][:])
+        store_rows(slice(0, 2), half_cols(0))
+        turn_back(2, 0, 5, turned[2][:])
+        add_gpsimd(3, 0)
+        store_rows(slice(2, 4), half_cols(0))
+        new_gated(1, "s3_0")
+        for t in (1, 0, 2, 3):
+            multiply(t, 1)
+        add_gpsimd(0, 1)
+        nc.gpsimd.dma_start(y_rows[:, :1, half_cols(1)], y[1][:, :1, :])
+        add_turned(1, 1, 7, turned[3][:])
+        turn_back(1, 1, 6, turned[3][:])
+        for c in range(PER_HALF):
+            round_y(c, nc.scalar.copy)
+        rs[2, 1] = sbuf.tile([P, HALF], F32, name="rs2_1", tag="s0_1", align_bytes=64)[:]
+        gather_r(2, 1)
+        rs_both = sbuf.tile([P, HALF], F32, name="rs_last", tag="s1_1", align_bytes=64)
+        rs_last = [rs_both[:, chunk_cols(i)] for i in range(PER_HALF)]
+
+        def gather_last(i):
+            cols = chunk_cols(PER_HALF + i)
+            nc.vector.tensor_tensor(rs_last[i][:], r_slices[LAST][:].indirect(entries(cols)), s[LAST, 1][:, chunk_cols(i)], ALU.mult)
+
+        gather_last(0)
+        nc.vector.tensor_tensor(y[1][:, 2, :], rs[2, 1], gated_tile[1][:, 2, :], ALU.add)
+        gather_last(1)
+        for i in range(PER_HALF):
+            nc.vector.tensor_tensor(y[1][:, LAST, chunk_cols(i)], rs_last[i][:], gated_tile[1][:, LAST, chunk_cols(i)], ALU.add)
+            store_rows(slice(1, PACK), chunk_cols(PER_HALF + i))
+        for c in range(PER_HALF):
             quantise_y(c)
+        nc.sync.dma_start(y_words[:, half_cols(0)], y_codes[:, half_cols(0)])
+        round_y(3, nc.vector.tensor_copy)
+        round_y(2, nc.scalar.copy)
+        for c in (2, 3):
+            quantise_y(c)
+            nc.sync.dma_start(y_words[:, chunk_cols(c)], y_codes[:, chunk_cols(c)])
 
         for q in range(QUADS):
             queue = nc.sync if q % 2 == 0 else nc.scalar

@@ -34,6 +34,7 @@ SCALAR_M = 80
 CHUNK = 256
 CHUNKS = J // CHUNK
 PER_HALF = HALF // CHUNK
+VECTOR_G = 48
 QUANTISE_LAG = 2
 
 
@@ -82,7 +83,7 @@ def tile_list_hwayt_tanhP_kernel(
         make_identity(nc, ident[:])
 
         wg_codes = sbuf.tile([P, PASSES * N * 2], U8, name="wg_codes", align_bytes=64)
-        nc.vector.tensor_copy(
+        nc.scalar.copy(
             wg_codes[:].bitcast(U16).rearrange("p (a t m) -> p a t m", a=PASSES, t=PACK),
             wg_words_in[:].rearrange("p a n -> p (a n)").bitcast(U16).rearrange("p (a m t) -> p a t m", a=PASSES, t=PACK),
         )
@@ -169,11 +170,17 @@ def tile_list_hwayt_tanhP_kernel(
         nc.scalar.mul(minus_bias[:], bias[:], -1.0)
 
         s, rs, gated, gated_tile = {}, {}, {}, {}
-        for t in range(PACK):
-            for h in range(HALVES):
-                s[t, h] = sbuf.tile([P, HALF], F32, name="s%d_%d" % (t, h), tag="s%d_%d" % (t, h), align_bytes=64)[:]
-        for t, h in ((0, 0), (1, 0), (2, 0), (3, 0), (0, 1), (1, 1)):
-            rs[t, h] = sbuf.tile([P, HALF], F32, name="rs%d_%d" % (t, h), align_bytes=64)[:]
+        s_first = sbuf.tile([P, 2, J], F32, name="s_first", align_bytes=64)
+        rs_first = sbuf.tile([P, 2, J], F32, name="rs_first", align_bytes=64)
+        s_late = [sbuf.tile([P, 2, HALF], F32, name="s_late%d" % h, tag="s_late%d" % h, align_bytes=64) for h in range(HALVES)]
+        m_first = sbuf.tile([P, PACK, HALF], F32, name="m_first", align_bytes=64)
+        for h in range(HALVES):
+            for t in range(2):
+                s[t, h] = s_first[:, t, half_cols(h)]
+                rs[t, h] = rs_first[:, t, half_cols(h)]
+                s[2 + t, h] = s_late[h][:, t, :]
+        for t in (2, 3):
+            rs[t, 0] = sbuf.tile([P, HALF], F32, name="rs%d_0" % t, align_bytes=64)[:]
 
         def new_gated(h, tag):
             tile = sbuf.tile([P, PACK, HALF], F32, name="gated%d" % h, tag=tag, align_bytes=64)
@@ -261,8 +268,11 @@ def tile_list_hwayt_tanhP_kernel(
         def y_chunk(c):
             return y[c // PER_HALF][:, :, chunk_cols(c % PER_HALF)]
 
-        def round_y(c, copy):
-            copy(y_bf16[c][:].rearrange("p (g i t) -> p g t i", t=PACK, i=4), y_chunk(c).rearrange("p t (g i) -> p g t i", i=4))
+        def round_y(c, copy, groups=slice(0, CHUNK // 4)):
+            copy(
+                y_bf16[c][:].rearrange("p (g i t) -> p g t i", t=PACK, i=4)[:, groups],
+                y_chunk(c).rearrange("p t (g i) -> p g t i", i=4)[:, groups],
+            )
 
         def quantise_y(c):
             nc.vector.quantize_mx(out=y_codes[:, chunk_cols(c)].bitcast(FP8X4), scales=y_plane[:, chunk_cols(c)], in_=y_bf16[c][:])
@@ -282,24 +292,28 @@ def tile_list_hwayt_tanhP_kernel(
                     start=(a == 1),
                     stop=(a == 0),
                 )
-            m[t, 0] = sbuf.tile([P, HALF], F32, name="m%d" % t, align_bytes=64)
-            nc.scalar.activation(m[t, 0][:], acc[:], ACT.Tanh, scale=-1.0)
+            nc.scalar.activation(m_first[:, t, :], acc[:], ACT.Tanh, scale=-1.0)
 
-        for t, h, b in ((0, 0, 0), (0, 1, 1), (1, 0, 2), (2, 0, 3), (3, 0, 4)):
+        for t, h, b in ((0, 0, 0), (0, 1, 1), (1, 0, 2), (1, 1, 3)):
             gate(t, h, b)
-        for t, b in enumerate((6, 7, 0, 1)):
-            candidate_rows(t, b)
-        for jb, b in zip(range(4, 8), (2, 3, 4, 6)):
-            candidate(jb, b)
-        for t, b in ((1, 5), (2, 7), (3, 0)):
-            gate(t, 1, b)
-        gather_r(0, 0)
-        gather_r(0, 1)
+        candidate_rows(0, 6)
+        candidate_rows(1, 7)
+        gate(2, 0, 4)
+        gate(3, 0, 5)
+        candidate(4, 0)
+        candidate(5, 1)
+        candidate_rows(2, 2)
+        candidate_rows(3, 3)
+        candidate(6, 4)
+        candidate(7, 6)
+        gate(2, 1, 7)
+        gate(3, 1, 0)
+        nc.vector.tensor_tensor(rs_first[:, 0, :], r_slices[0][:].indirect(offsets[:]), s_first[:, 0, :], ALU.mult)
+        nc.vector.scalar_tensor_tensor(m_first[:, :2, :], s_first[:, :, half_cols(0)], 1.0, m_first[:, :2, :], ALU.subtract, ALU.mult)
+        nc.vector.scalar_tensor_tensor(m_first[:, 2:, :], s_late[0][:], 1.0, m_first[:, 2:, :], ALU.subtract, ALU.mult)
         for t in range(PACK):
-            gated[t, 0] = blocks(m[t, 0][:])
-            multiply(t, 0)
-        gather_r(1, 0)
-        gather_r(1, 1)
+            gated[t, 0] = blocks(m_first[:, t, :])
+        nc.vector.tensor_tensor(rs_first[:, 1, :], r_slices[1][:].indirect(offsets[:]), s_first[:, 1, :], ALU.mult)
         gather_r(2, 0)
         gather_r(3, 0)
         turned = [sbuf.tile([P, HALF], F32, name="turned%d" % i, align_bytes=64) for i in range(4)]
@@ -314,7 +328,7 @@ def tile_list_hwayt_tanhP_kernel(
         turn_back(2, 0, 5, turned[2][:])
         add_gpsimd(3, 0)
         store_rows(slice(2, 4), half_cols(0))
-        new_gated(1, "s3_0")
+        new_gated(1, "s_late0")
         for t in (1, 0, 2, 3):
             multiply(t, 1)
         add_gpsimd(0, 1)
@@ -323,26 +337,21 @@ def tile_list_hwayt_tanhP_kernel(
         turn_back(1, 1, 6, turned[3][:])
         for c in range(PER_HALF):
             round_y(c, nc.scalar.copy)
-        rs[2, 1] = sbuf.tile([P, HALF], F32, name="rs2_1", tag="s0_1", align_bytes=64)[:]
+        rs[2, 1] = s[0, 1]
         gather_r(2, 1)
-        rs_both = sbuf.tile([P, HALF], F32, name="rs_last", tag="s1_1", align_bytes=64)
-        rs_last = [rs_both[:, chunk_cols(i)] for i in range(PER_HALF)]
-
-        def gather_last(i):
-            cols = chunk_cols(PER_HALF + i)
-            nc.vector.tensor_tensor(rs_last[i][:], r_slices[LAST][:].indirect(entries(cols)), s[LAST, 1][:, chunk_cols(i)], ALU.mult)
-
-        gather_last(0)
-        nc.vector.tensor_tensor(y[1][:, 2, :], rs[2, 1], gated_tile[1][:, 2, :], ALU.add)
-        gather_last(1)
         for i in range(PER_HALF):
-            nc.vector.tensor_tensor(y[1][:, LAST, chunk_cols(i)], rs_last[i][:], gated_tile[1][:, LAST, chunk_cols(i)], ALU.add)
-            store_rows(slice(1, PACK), chunk_cols(PER_HALF + i))
+            part = chunk_cols(i)
+            cols = chunk_cols(PER_HALF + i)
+            nc.vector.tensor_tensor(s[1, 1][:, part], r_slices[LAST][:].indirect(entries(cols)), s[LAST, 1][:, part], ALU.mult)
+            nc.vector.tensor_tensor(y[1][:, 2, part], rs[2, 1][:, part], gated_tile[1][:, 2, part], ALU.add)
+            nc.vector.tensor_tensor(y[1][:, LAST, part], s[1, 1][:, part], gated_tile[1][:, LAST, part], ALU.add)
+            store_rows(slice(1, PACK), cols)
         for c in range(PER_HALF):
             quantise_y(c)
         nc.sync.dma_start(y_words[:, half_cols(0)], y_codes[:, half_cols(0)])
-        round_y(3, nc.vector.tensor_copy)
         round_y(2, nc.scalar.copy)
+        round_y(3, nc.vector.tensor_copy, slice(0, VECTOR_G))
+        round_y(3, nc.scalar.copy, slice(VECTOR_G, CHUNK // 4))
         for c in (2, 3):
             quantise_y(c)
             nc.sync.dma_start(y_words[:, chunk_cols(c)], y_codes[:, chunk_cols(c)])

@@ -50,16 +50,15 @@ def tile_list_hwayt_tanhP_kernel(
         nc.vector.memset(table_scales[:].bitcast(I32), 0)
         wg_scales_in = sbuf.tile([P, PASSES * N], U8, name="wg_scales_in", align_bytes=64)
         nc.vector.memset(wg_scales_in[:].bitcast(I32), 0)
-        v_plane1 = sbuf.tile([P, J], U8, name="v_plane1", align_bytes=64)
-        nc.vector.memset(v_plane1[:].bitcast(I32), 0)
+        v_both = sbuf.tile([P, PASSES * J], U8, name="v_both", align_bytes=64)
+        nc.vector.memset(v_both[:].bitcast(I32), 0)
 
         wg_words_in = sbuf.tile([P, PASSES, N // 2], I32, name="wg_words_in", align_bytes=64)
         nc.sync.dma_start(wg_words_in[:], wg_words.bitcast(I32).rearrange("a p n -> p a n"))
         offsets = sbuf.tile(list(offs.shape), U16, name="offsets")
         nc.sync.dma_start(offsets[:], offs)
-        table_scale_rows = tab_scales.bitcast(I32).rearrange("a (q r) c -> r q a c", r=PLANE_ROWS)
-        for r in range(PLANE_ROWS):
-            nc.sync.dma_start(table_scales[r:P:SHIFT, :].bitcast(I32), table_scale_rows[r])
+        for a in range(PASSES):
+            nc.sync.dma_start(table_scales[4 * a : P : 8, :].bitcast(I32), tab_scales[a].bitcast(I32))
         table_words = sbuf.tile([P, T], I32, name="table_words", align_bytes=64)
         nc.sync.dma_start(table_words[:], tab_words[0].rearrange("p c b -> p (c b)").bitcast(I32))
         for q in range(QUADS):
@@ -74,7 +73,7 @@ def tile_list_hwayt_tanhP_kernel(
         wh_first = sbuf.tile([P, PACK, N], F32, name="wh_first", tag="wh_first", align_bytes=64)
         nc.sync.dma_start(wh_first[:], wh_rows[0])
         wh_second = sbuf.tile([P, PACK, N], F32, name="wh_second", align_bytes=64)
-        nc.sync.dma_start(wh_second[:, : PACK // 2, :], wh_rows[1][:, : PACK // 2, :])
+        nc.sync.dma_start(wh_second[:, :1, :], wh_rows[1][:, :1, :])
 
         warm = sbuf.tile([P, 1], F32, name="warm", tag="warm", align_bytes=64)
         nc.vector.memset(warm[:], 0.0)
@@ -90,10 +89,13 @@ def tile_list_hwayt_tanhP_kernel(
 
         v_plane0 = sbuf.tile([P, J], U8, name="v_plane0", align_bytes=64)
         nc.vector.tensor_copy(v_plane0[:], table_scales[:].indirect(offsets[:]))
-        nc.sync.dma_start(v_plane1[: P - SHIFT, :].bitcast(I32), v_plane0[SHIFT:, :].bitcast(I32))
-        v_planes = (v_plane0, v_plane1)
+        for q in range(QUADS):
+            nc.sync.dma_start(
+                v_both[32 * q : 32 * q + PLANE_ROWS, :].bitcast(I32), v_plane0[32 * q : 32 * (q + 1) : 4, :].bitcast(I32)
+            )
+        v_planes = (v_both[:, :J], v_both[:, J:])
 
-        nc.sync.dma_start(wh_second[:, PACK // 2 :, :], wh_rows[1][:, PACK // 2 :, :])
+        nc.sync.dma_start(wh_second[:, 1:, :], wh_rows[1][:, 1:, :])
         r_rows = rT.rearrange("(p t) c -> t p c", t=PACK)
         r_slices = [sbuf.tile([P, T], F32, name="r%d" % t, align_bytes=64) for t in range(PACK)]
         for t in range(PACK):
@@ -188,7 +190,8 @@ def tile_list_hwayt_tanhP_kernel(
             for t in range(PACK):
                 gated[t, h] = tile[:, t, :].rearrange("p (b j) -> p b j", j=P)
 
-        m_turned = [sbuf.tile([P, N], F32, name="m_turned%d" % b, align_bytes=64) for b in range(J // P)]
+        m_late = sbuf.tile([P, HALF // P, N], F32, name="m_late", align_bytes=64)
+        m_turned = {HALF // P + b: m_late[:, b, :] for b in range(HALF // P)}
 
         def blocks(ap):
             return ap.rearrange("p (b j) -> p b j", j=P)
@@ -222,7 +225,7 @@ def tile_list_hwayt_tanhP_kernel(
                     start=(a == 1),
                     stop=(a == 0),
                 )
-            nc.scalar.activation(m_turned[jb][:], acc[:], ACT.Tanh, scale=-1.0)
+            nc.scalar.activation(m_turned[jb], acc[:], ACT.Tanh, scale=-1.0)
 
         m = {}
 
@@ -309,7 +312,8 @@ def tile_list_hwayt_tanhP_kernel(
         gate(2, 1, 7)
         gate(3, 1, 0)
         nc.vector.tensor_tensor(rs_first[:, 0, :], r_slices[0][:].indirect(offsets[:]), s_first[:, 0, :], ALU.mult)
-        nc.vector.scalar_tensor_tensor(m_first[:, :2, :], s_first[:, :, half_cols(0)], 1.0, m_first[:, :2, :], ALU.subtract, ALU.mult)
+        for t in range(2):
+            nc.vector.scalar_tensor_tensor(m_first[:, t, :], s[t, 0], 1.0, m_first[:, t, :], ALU.subtract, ALU.mult)
         nc.vector.scalar_tensor_tensor(m_first[:, 2:, :], s_late[0][:], 1.0, m_first[:, 2:, :], ALU.subtract, ALU.mult)
         for t in range(PACK):
             gated[t, 0] = blocks(m_first[:, t, :])
@@ -318,33 +322,46 @@ def tile_list_hwayt_tanhP_kernel(
         gather_r(3, 0)
         turned = [sbuf.tile([P, HALF], F32, name="turned%d" % i, align_bytes=64) for i in range(4)]
         add_turned(0, 0, 6, turned[0][:])
-        for t in range(PACK):
+        s_turned = bank(2)
+        for b in range(HALF // P):
+            nc.tensor.transpose(s_turned[:, b * P : (b + 1) * P], s[1, 1][:, b * P : (b + 1) * P], ident[:])
+        for t in (0, 2, 3):
             turn_m(t, 1)
         add_turned(1, 0, 5, turned[1][:])
         turn_back(0, 0, 7, turned[0][:])
         add_turned(2, 0, 6, turned[2][:])
         turn_back(1, 0, 0, turned[1][:])
+        acc = bank(7)
+        for b in range(HALF // P):
+            nc.tensor.transpose(acc[:, b * P : (b + 1) * P], rs[1, 1][:, b * P : (b + 1) * P], ident[:])
+        nc.scalar.copy(turned[3][:], acc[:])
         store_rows(slice(0, 2), half_cols(0))
         turn_back(2, 0, 5, turned[2][:])
         add_gpsimd(3, 0)
         store_rows(slice(2, 4), half_cols(0))
         new_gated(1, "s_late0")
-        for t in (1, 0, 2, 3):
+        nc.vector.scalar_tensor_tensor(gated[1, 1], blocks(s_turned[:]), 1.0, m_late[:, :, P : 2 * P], ALU.subtract, ALU.mult)
+        for t in (0, 2, 3):
             multiply(t, 1)
         add_gpsimd(0, 1)
         nc.gpsimd.dma_start(y_rows[:, :1, half_cols(1)], y[1][:, :1, :])
-        add_turned(1, 1, 7, turned[3][:])
-        turn_back(1, 1, 6, turned[3][:])
+        acc = bank(0)
+        for n, term in enumerate((blocks(turned[3][:]), gated[1, 1])):
+            for k in range(HALF // P):
+                first, final = (n, k) == (0, 0), (n, k) == (1, HALF // P - 1)
+                nc.tensor.matmul(acc[:, k * P : (k + 1) * P], term[:, k, :], ident[:], is_transpose=True, start=first, stop=final)
+        nc.scalar.copy(y[1][:, 1, :], acc[:])
         for c in range(PER_HALF):
             round_y(c, nc.scalar.copy)
         rs[2, 1] = s[0, 1]
+        rs_last = m_late[:, 0, P : 3 * P], m_late[:, 1, P : 3 * P]
         gather_r(2, 1)
         for i in range(PER_HALF):
             part = chunk_cols(i)
             cols = chunk_cols(PER_HALF + i)
-            nc.vector.tensor_tensor(s[1, 1][:, part], r_slices[LAST][:].indirect(entries(cols)), s[LAST, 1][:, part], ALU.mult)
+            nc.vector.tensor_tensor(rs_last[i], r_slices[LAST][:].indirect(entries(cols)), s[LAST, 1][:, part], ALU.mult)
             nc.vector.tensor_tensor(y[1][:, 2, part], rs[2, 1][:, part], gated_tile[1][:, 2, part], ALU.add)
-            nc.vector.tensor_tensor(y[1][:, LAST, part], s[1, 1][:, part], gated_tile[1][:, LAST, part], ALU.add)
+            nc.vector.tensor_tensor(y[1][:, LAST, part], rs_last[i], gated_tile[1][:, LAST, part], ALU.add)
             store_rows(slice(1, PACK), cols)
         for c in range(PER_HALF):
             quantise_y(c)

@@ -47,7 +47,7 @@ def tile_list_hwayt_tanhP_kernel(
         psum = ctx.enter_context(tc.psum_pool(name="psum", bufs=1))
 
         table_scales = sbuf.tile([P, T], U8, name="table_scales", align_bytes=64)
-        nc.vector.memset(table_scales[:].bitcast(I32), 0)
+        nc.gpsimd.memset(table_scales[:].bitcast(I32), 0)
         wg_scales_in = sbuf.tile([P, PASSES * N], U8, name="wg_scales_in", align_bytes=64)
         nc.vector.memset(wg_scales_in[:].bitcast(I32), 0)
         v_both = sbuf.tile([P, PASSES * J], U8, name="v_both", align_bytes=64)
@@ -366,7 +366,8 @@ def tile_list_hwayt_tanhP_kernel(
         for c in range(PER_HALF):
             quantise_y(c)
         nc.sync.dma_start(y_words[:, half_cols(0)], y_codes[:, half_cols(0)])
-        round_y(2, nc.scalar.copy)
+        round_y(2, nc.scalar.copy, slice(0, VECTOR_G))
+        round_y(2, nc.vector.tensor_copy, slice(VECTOR_G, CHUNK // 4))
         round_y(3, nc.vector.tensor_copy, slice(0, VECTOR_G))
         round_y(3, nc.scalar.copy, slice(VECTOR_G, CHUNK // 4))
         for c in (2, 3):

from contextlib import ExitStack

import concourse.mybir as mybir
from concourse.masks import make_identity

K, N, T, J = 1024, 512, 2048, 1024
FLOPS = 2 * 2 * K * N * J

F32 = mybir.dt.float32
BF16 = mybir.dt.bfloat16
I32 = mybir.dt.int32
U32 = mybir.dt.uint32
U16 = mybir.dt.uint16
U8 = mybir.dt.uint8
FP8X4 = mybir.dt.float8_e4m3fn_x4
FP4X4 = mybir.dt.float4_e2m1fn_x4
ALU = mybir.AluOpType
ACT = mybir.ActivationFunctionType

P = 128
PACK = 4
K_PASS = P * PACK
PASSES = K // K_PASS
QUADS = 4
PLANE_ROWS = 4
HALF = 512
HALVES = J // HALF
SHIFT = 16
PER_COLUMN = 16
EARLY = 2
SHARED = EARLY
LAST = PACK - 1
SCALAR_M = 80
CHUNK = 256
CHUNKS = J // CHUNK
PER_HALF = HALF // CHUNK
VECTOR_G = 48
QUANTISE_LAG = 2


def tile_list_hwayt_tanhP_kernel(
    tc, tab_words, tab_scales, wg_words, wg_scales, wh, bg, rT, offs, out_0, out_1, out_2
):
    nc = tc.nc
    with ExitStack() as ctx:
        sbuf = ctx.enter_context(tc.tile_pool(name="sbuf", bufs=1))
        psum = ctx.enter_context(tc.psum_pool(name="psum", bufs=1))

        table_scales = sbuf.tile([P, T], U8, name="table_scales", align_bytes=64)
        nc.gpsimd.memset(table_scales[:].bitcast(I32), 0)
        wg_scales_in = sbuf.tile([P, PASSES * N], U8, name="wg_scales_in", align_bytes=64)
        nc.vector.memset(wg_scales_in[:].bitcast(I32), 0)
        v_both = sbuf.tile([P, PASSES * J], U8, name="v_both", align_bytes=64)
        nc.vector.memset(v_both[:].bitcast(I32), 0)

        wg_words_in = sbuf.tile([P, PASSES, N // 2], I32, name="wg_words_in", align_bytes=64)
        nc.sync.dma_start(wg_words_in[:], wg_words.bitcast(I32).rearrange("a p n -> p a n"))
        offsets = sbuf.tile(list(offs.shape), U16, name="offsets")
        nc.sync.dma_start(offsets[:], offs)
        for a in range(PASSES):
            nc.sync.dma_start(table_scales[4 * a : P : 8, :].bitcast(I32), tab_scales[a].bitcast(I32))
        table_words = sbuf.tile([P, T], I32, name="table_words", align_bytes=64)
        nc.sync.dma_start(table_words[:], tab_words[0].rearrange("p c b -> p (c b)").bitcast(I32))
        for q in range(QUADS):
            nc.sync.dma_start(
                wg_scales_in[32 * q : 32 * q + PLANE_ROWS, :].bitcast(I32).rearrange("r (a n) -> r a n", a=PASSES),
                wg_scales[:, PLANE_ROWS * q : PLANE_ROWS * (q + 1), :].bitcast(I32).rearrange("a r n -> r a n"),
            )
        bias = sbuf.tile([P, PACK], F32, name="bias")
        nc.sync.dma_start(bias[:], bg.rearrange("(p t) -> p t", t=PACK))

        wh_rows = wh.rearrange("(a p i) n -> a p i n", p=P, i=PACK)
        wh_first = sbuf.tile([P, PACK, N], F32, name="wh_first", tag="wh_first", align_bytes=64)
        nc.sync.dma_start(wh_first[:], wh_rows[0])
        wh_second = sbuf.tile([P, PACK, N], F32, name="wh_second", align_bytes=64)
        nc.sync.dma_start(wh_second[:, :1, :], wh_rows[1][:, :1, :])

        warm = sbuf.tile([P, 1], F32, name="warm", tag="warm", align_bytes=64)
        nc.vector.memset(warm[:], 0.0)
        nc.scalar.activation(warm[:], warm[:], ACT.Sigmoid)
        ident = sbuf.tile([P, P], F32, name="ident", tag="warm", align_bytes=64)
        make_identity(nc, ident[:])

        wg_codes = sbuf.tile([P, PASSES * N * 2], U8, name="wg_codes", align_bytes=64)
        nc.scalar.copy(
            wg_codes[:].bitcast(U16).rearrange("p (a t m) -> p a t m", a=PASSES, t=PACK),
            wg_words_in[:].rearrange("p a n -> p (a n)").bitcast(U16).rearrange("p (a m t) -> p a t m", a=PASSES, t=PACK),
        )

        v_plane0 = sbuf.tile([P, J], U8, name="v_plane0", align_bytes=64)
        nc.vector.tensor_copy(v_plane0[:], table_scales[:].indirect(offsets[:]))
        for q in range(QUADS):
            nc.sync.dma_start(
                v_both[32 * q : 32 * q + PLANE_ROWS, :].bitcast(I32), v_plane0[32 * q : 32 * (q + 1) : 4, :].bitcast(I32)
            )
        v_planes = (v_both[:, :J], v_both[:, J:])

        nc.sync.dma_start(wh_second[:, 1:, :], wh_rows[1][:, 1:, :])
        r_rows = rT.rearrange("(p t) c -> t p c", t=PACK)
        r_slices = [sbuf.tile([P, T], F32, name="r%d" % t, align_bytes=64) for t in range(PACK)]
        for t in range(PACK):
            nc.sync.dma_start(r_slices[t][:], r_rows[t])

        wg_planes = sbuf.tile([P, PASSES * N], U8, name="wg_planes", align_bytes=64)
        nc.gpsimd.tensor_copy(
            wg_planes[:].rearrange("p (a t m) -> p a t m", a=PASSES, t=PACK),
            wg_scales_in[:].rearrange("p (a m t) -> p a t m", a=PASSES, t=PACK),
        )

        def half_cols(h):
            return slice(h * HALF, (h + 1) * HALF)

        def chunk_cols(c):
            return slice(c * CHUNK, (c + 1) * CHUNK)

        def entries(cols):
            return offsets[:, cols.start // PER_COLUMN : cols.stop // PER_COLUMN]

        v_codes = [sbuf.tile([P, PASSES * HALF * 2], U8, name="v_codes%d" % h, align_bytes=64) for h in range(HALVES)]
        pairs = {}

        def gather_words(c):
            pairs[c] = sbuf.tile([P, CHUNK], U32, name="pairs%d" % c, tag="pairs%d" % (c % PER_HALF), align_bytes=64)
            nc.vector.tensor_copy(pairs[c][:], table_words[:].bitcast(U32).indirect(entries(chunk_cols(c))))

        def part_words(c):
            nc.vector.tensor_copy(
                v_codes[c // PER_HALF][:].bitcast(U16).rearrange("p (a j) -> p a j", a=PASSES)[:, :, chunk_cols(c % PER_HALF)],
                pairs[c][:].bitcast(U16).rearrange("p (j a) -> p a j", a=PASSES),
            )

        for h in range(HALVES):
            for c in range(h * PER_HALF, (h + 1) * PER_HALF):
                gather_words(c)
            for c in range(h * PER_HALF, (h + 1) * PER_HALF):
                part_words(c)

        wh_bf16 = [sbuf.tile([P, PACK * N], BF16, name="wh_bf16_%d" % a, align_bytes=64) for a in range(PASSES)]
        wh_codes = [sbuf.tile([P, N], U32, name="wh_codes%d" % a, align_bytes=64) for a in range(PASSES)]
        wh_planes = [sbuf.tile([P, N], U8, name="wh_planes%d" % a, align_bytes=64) for a in range(PASSES)]

        def round_wh(a, rows, ms, slices, copy):
            dealt = wh_bf16[a][:].rearrange("p (t m i) -> p m i t", t=PACK, i=PACK)
            copy(dealt[:, ms, :, slices], rows[:].rearrange("p i (m t) -> p m i t", t=PACK)[:, ms, :, slices])

        def quantise_wh(a, slices):
            n0, n1 = slices.start * P, slices.stop * P
            nc.vector.quantize_mx(
                out=wh_codes[a][:, n0:n1].bitcast(FP8X4), scales=wh_planes[a][:, n0:n1], in_=wh_bf16[a][:, PACK * n0 : PACK * n1]
            )

        def bank(b):
            return psum.tile([P, HALF], F32, name="bank%d" % b, tag="bank%d" % b)

        all_m, all_slices = slice(0, P), slice(0, PACK)
        slice_pairs = (slice(0, PACK // 2), slice(PACK // 2, PACK))
        round_wh(0, wh_first, slice(0, SCALAR_M), all_slices, nc.scalar.copy)
        nc.gpsimd.tensor_scalar(
            wh_bf16[0][:].rearrange("p (t m i) -> p t m i", t=PACK, i=PACK)[:, :, SCALAR_M:, :],
            wh_first[:].rearrange("p i (m t) -> p t m i", t=PACK)[:, :, SCALAR_M:, :],
            1.0,
            0.0,
            ALU.mult,
            ALU.add,
        )
        quantise_wh(0, all_slices)
        for slices in slice_pairs:
            round_wh(1, wh_second, all_m, slices, nc.vector.tensor_copy)
        for slices in slice_pairs:
            quantise_wh(1, slices)
        minus_bias = sbuf.tile([P, PACK], F32, name="minus_bias")
        nc.scalar.mul(minus_bias[:], bias[:], -1.0)

        s, rs, gated, gated_tile = {}, {}, {}, {}
        s_first = sbuf.tile([P, 2, J], F32, name="s_first", align_bytes=64)
        rs_first = sbuf.tile([P, 2, J], F32, name="rs_first", align_bytes=64)
        s_late = [sbuf.tile([P, 2, HALF], F32, name="s_late%d" % h, tag="s_late%d" % h, align_bytes=64) for h in range(HALVES)]
        m_first = sbuf.tile([P, PACK, HALF], F32, name="m_first", align_bytes=64)
        for h in range(HALVES):
            for t in range(2):
                s[t, h] = s_first[:, t, half_cols(h)]
                rs[t, h] = rs_first[:, t, half_cols(h)]
                s[2 + t, h] = s_late[h][:, t, :]
        for t in (2, 3):
            rs[t, 0] = sbuf.tile([P, HALF], F32, name="rs%d_0" % t, align_bytes=64)[:]

        def new_gated(h, tag):
            tile = sbuf.tile([P, PACK, HALF], F32, name="gated%d" % h, tag=tag, align_bytes=64)
            gated_tile[h] = tile
            for t in range(PACK):
                gated[t, h] = tile[:, t, :].rearrange("p (b j) -> p b j", j=P)

        m_late = sbuf.tile([P, HALF // P, N], F32, name="m_late", align_bytes=64)
        m_turned = {HALF // P + b: m_late[:, b, :] for b in range(HALF // P)}

        def blocks(ap):
            return ap.rearrange("p (b j) -> p b j", j=P)

        def gate(t, h, b):
            acc = bank(b)
            opening = 0 if h == 0 and t < 2 else 1
            for a in (opening, 1 - opening):
                n0 = a * N + t * P
                nc.tensor.matmul_mx(
                    out=acc[:],
                    lhsT=wg_codes[:, 2 * n0 : 2 * (n0 + P)].bitcast(FP4X4),
                    lhsT_scale=wg_planes[:, n0 : n0 + P],
                    rhs=v_codes[h][:, 2 * a * HALF : 2 * (a + 1) * HALF].bitcast(FP4X4),
                    rhs_scale=v_planes[a][:, half_cols(h)],
                    start=(a == opening),
                    stop=(a != opening),
                )
            nc.scalar.activation(s[t, h], acc[:], ACT.Sigmoid, bias=minus_bias[:, t : t + 1], scale=-1.0)

        def candidate(jb, b):
            acc = bank(b)
            h, j0 = divmod(jb * P, HALF)
            for a in (1, 0):
                nc.tensor.matmul_mx(
                    out=acc[:],
                    lhsT=v_codes[h][:, 2 * (a * HALF + j0) : 2 * (a * HALF + j0 + P)].bitcast(FP4X4),
                    lhsT_scale=v_planes[a][:, jb * P : (jb + 1) * P],
                    rhs=wh_codes[a][:].bitcast(FP8X4),
                    rhs_scale=wh_planes[a][:],
                    start=(a == 1),
                    stop=(a == 0),
                )
            nc.scalar.activation(m_turned[jb], acc[:], ACT.Tanh, scale=-1.0)

        m = {}

        def turn_m(t, h):
            m[t, h] = bank(1 + t)
            for b in range(HALF // P):
                nc.tensor.transpose(m[t, h][:, b * P : (b + 1) * P], m_turned[h * PACK + b][:, t * P : (t + 1) * P], ident[:])

        y_rows = out_0.rearrange("(p t) j -> p t j", t=PACK)
        y_words = out_1[0].rearrange("p j i -> p (j i)").bitcast(I32)
        y_plane = sbuf.tile([P, J], U8, name="y_plane", align_bytes=64)
        y = [sbuf.tile([P, PACK, HALF], F32, name="y%d" % h, align_bytes=64) for h in range(HALVES)]
        y_codes = sbuf.tile([P, J], I32, name="y_codes", align_bytes=64)
        y_bf16 = [sbuf.tile([P, PACK * CHUNK], BF16, name="y_bf16_%d" % c, tag="y_bf16_%d" % (c % 3), align_bytes=64) for c in range(CHUNKS)]

        def gather_r(t, h):
            nc.vector.tensor_tensor(rs[t, h], r_slices[t][:].indirect(entries(half_cols(h))), s[t, h], ALU.mult)

        def multiply(t, h):
            nc.vector.scalar_tensor_tensor(gated[t, h], blocks(s[t, h]), 1.0, blocks(m[t, h][:]), ALU.subtract, ALU.mult)

        def store_rows(slices, cols):
            h = cols.start // HALF
            nc.sync.dma_start(y_rows[:, slices, cols], y[h][:, slices, cols.start - h * HALF : cols.stop - h * HALF])

        def add_gpsimd(t, h):
            nc.gpsimd.tensor_tensor(blocks(y[h][:, t, :]), blocks(rs[t, h]), gated[t, h], ALU.add)

        def add_turned(t, h, b, turned):
            acc = bank(b)
            for n, term in enumerate((gated[t, h], blocks(rs[t, h]))):
                for k in range(HALF // P):
                    first, final = (n, k) == (0, 0), (n, k) == (1, HALF // P - 1)
                    nc.tensor.matmul(acc[:, k * P : (k + 1) * P], term[:, k, :], ident[:], is_transpose=True, start=first, stop=final)
            nc.scalar.copy(turned, acc[:])

        def turn_back(t, h, b, turned):
            acc = bank(b)
            for k in range(HALF // P):
                nc.tensor.transpose(acc[:, k * P : (k + 1) * P], turned[:, k * P : (k + 1) * P], ident[:])
            nc.scalar.copy(y[h][:, t, :], acc[:])

        def y_chunk(c):
            return y[c // PER_HALF][:, :, chunk_cols(c % PER_HALF)]

        def round_y(c, copy, groups=slice(0, CHUNK // 4)):
            copy(
                y_bf16[c][:].rearrange("p (g i t) -> p g t i", t=PACK, i=4)[:, groups],
                y_chunk(c).rearrange("p t (g i) -> p g t i", i=4)[:, groups],
            )

        def quantise_y(c):
            nc.vector.quantize_mx(out=y_codes[:, chunk_cols(c)].bitcast(FP8X4), scales=y_plane[:, chunk_cols(c)], in_=y_bf16[c][:])

        def one(t):
            return slice(t, t + 1)

        def candidate_rows(t, b):
            acc = bank(b)
            for a in (1, 0):
                nc.tensor.matmul_mx(
                    out=acc[:],
                    lhsT=wh_codes[a][:, t * P : (t + 1) * P].bitcast(FP8X4),
                    lhsT_scale=wh_planes[a][:, t * P : (t + 1) * P],
                    rhs=v_codes[0][:, 2 * a * HALF : 2 * (a + 1) * HALF].bitcast(FP4X4),
                    rhs_scale=v_planes[a][:, half_cols(0)],
                    start=(a == 1),
                    stop=(a == 0),
                )
            nc.scalar.activation(m_first[:, t, :], acc[:], ACT.Tanh, scale=-1.0)

        for t, h, b in ((0, 0, 0), (0, 1, 1), (1, 0, 2), (1, 1, 3)):
            gate(t, h, b)
        candidate_rows(0, 6)
        candidate_rows(1, 7)
        gate(2, 0, 4)
        gate(3, 0, 5)
        candidate(4, 0)
        candidate(5, 1)
        candidate_rows(2, 2)
        candidate_rows(3, 3)
        candidate(6, 4)
        candidate(7, 6)
        gate(2, 1, 7)
        gate(3, 1, 0)
        nc.vector.tensor_tensor(rs_first[:, 0, :], r_slices[0][:].indirect(offsets[:]), s_first[:, 0, :], ALU.mult)
        for t in range(2):
            nc.vector.scalar_tensor_tensor(m_first[:, t, :], s[t, 0], 1.0, m_first[:, t, :], ALU.subtract, ALU.mult)
        nc.vector.scalar_tensor_tensor(m_first[:, 2:, :], s_late[0][:], 1.0, m_first[:, 2:, :], ALU.subtract, ALU.mult)
        for t in range(PACK):
            gated[t, 0] = blocks(m_first[:, t, :])
        nc.vector.tensor_tensor(rs_first[:, 1, :], r_slices[1][:].indirect(offsets[:]), s_first[:, 1, :], ALU.mult)
        gather_r(2, 0)
        gather_r(3, 0)
        turned = [sbuf.tile([P, HALF], F32, name="turned%d" % i, align_bytes=64) for i in range(4)]
        add_turned(0, 0, 6, turned[0][:])
        s_turned = bank(2)
        for b in range(HALF // P):
            nc.tensor.transpose(s_turned[:, b * P : (b + 1) * P], s[1, 1][:, b * P : (b + 1) * P], ident[:])
        for t in (0, 2, 3):
            turn_m(t, 1)
        add_turned(1, 0, 5, turned[1][:])
        turn_back(0, 0, 7, turned[0][:])
        add_turned(2, 0, 6, turned[2][:])
        turn_back(1, 0, 0, turned[1][:])
        acc = bank(7)
        for b in range(HALF // P):
            nc.tensor.transpose(acc[:, b * P : (b + 1) * P], rs[1, 1][:, b * P : (b + 1) * P], ident[:])
        nc.scalar.copy(turned[3][:], acc[:])
        store_rows(slice(0, 2), half_cols(0))
        turn_back(2, 0, 5, turned[2][:])
        add_gpsimd(3, 0)
        store_rows(slice(2, 4), half_cols(0))
        new_gated(1, "s_late0")
        nc.vector.scalar_tensor_tensor(gated[1, 1], blocks(s_turned[:]), 1.0, m_late[:, :, P : 2 * P], ALU.subtract, ALU.mult)
        for t in (0, 2, 3):
            multiply(t, 1)
        add_gpsimd(0, 1)
        nc.gpsimd.dma_start(y_rows[:, :1, half_cols(1)], y[1][:, :1, :])
        acc = bank(0)
        for n, term in enumerate((blocks(turned[3][:]), gated[1, 1])):
            for k in range(HALF // P):
                first, final = (n, k) == (0, 0), (n, k) == (1, HALF // P - 1)
                nc.tensor.matmul(acc[:, k * P : (k + 1) * P], term[:, k, :], ident[:], is_transpose=True, start=first, stop=final)
        nc.scalar.copy(y[1][:, 1, :], acc[:])
        for c in range(PER_HALF):
            round_y(c, nc.scalar.copy)
        rs[2, 1] = s[0, 1]
        rs_last = m_late[:, 0, P : 3 * P], m_late[:, 1, P : 3 * P]
        gather_r(2, 1)
        for i in range(PER_HALF):
            part = chunk_cols(i)
            cols = chunk_cols(PER_HALF + i)
            nc.vector.tensor_tensor(rs_last[i], r_slices[LAST][:].indirect(entries(cols)), s[LAST, 1][:, part], ALU.mult)
            nc.vector.tensor_tensor(y[1][:, 2, part], rs[2, 1][:, part], gated_tile[1][:, 2, part], ALU.add)
            nc.vector.tensor_tensor(y[1][:, LAST, part], rs_last[i], gated_tile[1][:, LAST, part], ALU.add)
            store_rows(slice(1, PACK), cols)
        for c in range(PER_HALF):
            quantise_y(c)
        nc.sync.dma_start(y_words[:, half_cols(0)], y_codes[:, half_cols(0)])
        round_y(2, nc.scalar.copy, slice(0, VECTOR_G))
        round_y(2, nc.vector.tensor_copy, slice(VECTOR_G, CHUNK // 4))
        round_y(3, nc.vector.tensor_copy, slice(0, VECTOR_G))
        round_y(3, nc.scalar.copy, slice(VECTOR_G, CHUNK // 4))
        for c in (2, 3):
            quantise_y(c)
            nc.sync.dma_start(y_words[:, chunk_cols(c)], y_codes[:, chunk_cols(c)])

        for q in range(QUADS):
            queue = nc.sync if q % 2 == 0 else nc.scalar
            queue.dma_start(
                out_2[0, PLANE_ROWS * q : PLANE_ROWS * (q + 1), :].bitcast(I32),
                y_plane[32 * q : 32 * q + PLANE_ROWS, :].bitcast(I32),
            )
